import numpy as np
import ml_dtypes


def mxq(x, axis, fmt="e4m3"):
    dtype, down = {"e4m3": (ml_dtypes.float8_e4m3fn, 7), "e5m2": (ml_dtypes.float8_e5m2, 14)}[fmt]
    v = np.moveaxis(np.asarray(x, np.float32).astype(ml_dtypes.bfloat16).astype(np.float64), axis, -1)
    blocks = v.reshape(v.shape[:-1] + (-1, 32))
    amax = np.abs(blocks).max(-1, keepdims=True)
    byte = np.maximum(np.where(amax > 0, np.frexp(amax)[1] - 1 + 127, 0) - down, 1)
    scale = np.exp2(byte - 127.0)
    codes = (blocks / scale).astype(np.float32).astype(dtype).astype(np.float64)
    return np.moveaxis((codes * scale).reshape(v.shape), -1, axis)


WIDE = False


def mx_kscale(k):
    if not WIDE:
        return np.ones(k)
    levels = np.array([10, -10, 5, -5, 0])
    if k % 512:
        return np.exp2(np.random.permutation(np.resize(levels, k // 32))).repeat(32)
    a = np.empty((k // 512, 16))
    for p in range(k // 512):
        a[p, :8] = np.random.permutation(np.resize(levels, 8))
        for g in range(8):
            far = levels[np.abs(levels - a[p, g]) >= 10]
            a[p, g + 8] = far[np.random.randint(len(far))]
    return np.exp2(a.ravel()).repeat(32)


def f64(x):
    return np.asarray(x).astype(np.float64)


def striped(idx):
    return np.tile(idx.reshape(-1, 16).T, (8, 1)).astype(np.uint16)


def unstriped(offs):
    return offs[:16].T.reshape(-1).astype(np.int64)


E2M1 = np.array([0.0, 0.5, 1.0, 1.5, 2.0, 3.0, 4.0, 6.0, -0.0, -0.5, -1.0, -1.5, -2.0, -3.0, -4.0, -6.0])


def pack_weight(w, fmt):
    k, n = w.shape
    w = f64(np.asarray(w, np.float32).astype(ml_dtypes.bfloat16)).reshape(k // 32, 32, n)
    amax = np.abs(w).max(1)
    if fmt == "e4m3":
        byte = np.frexp(amax)[1] - 1 + 127 - 7
    else:
        mant, ex = np.frexp(amax / 6.0)
        byte = np.where(mant > 0.5, ex, ex - 1) + 127
    byte = np.clip(np.where(amax > 0, byte, 1), 1, 254)
    scaled = (w * np.exp2(127.0 - byte)[:, None, :]).reshape(k, n).astype(np.float32)
    by_word = np.ascontiguousarray(scaled.reshape(k // 512, 128, 4, n).transpose(0, 1, 3, 2))
    if fmt == "e4m3":
        words = by_word.astype(ml_dtypes.float8_e4m3fn).view(np.uint8)
    else:
        c = by_word.astype(ml_dtypes.float4_e2m1fn).view(np.uint8) & 0xF
        words = (c[..., 0::2] | (c[..., 1::2] << 4)).reshape(k // 512, 128, 2 * n)
    return np.ascontiguousarray(words), np.ascontiguousarray(byte.astype(np.uint8).reshape(k // 512, 16, n))


def unpack_weight(words, scales, fmt):
    g, _, n = scales.shape
    words = np.ascontiguousarray(words).reshape(g, 128, n, -1)
    if fmt == "e4m3":
        vals = words.view(ml_dtypes.float8_e4m3fn).astype(np.float64)
    else:
        nib = np.empty((g, 128, n, 4), np.uint8)
        nib[..., 0::2] = words & 0xF
        nib[..., 1::2] = words >> 4
        vals = E2M1[nib]
    vals = vals * np.repeat(np.exp2(scales.astype(np.float64) - 127.0), 8, axis=1)[..., None]
    return vals.transpose(0, 1, 3, 2).reshape(g * 512, n)


def gelu(v):
    return 0.5 * v * (1.0 + np.tanh(np.sqrt(2.0 / np.pi) * (v + 0.044715 * v**3)))


K, T, S, M, N = 1024, 2048, 1024, 512, 512

def setup_inputs():
    n = np.random.standard_normal
    s = mx_kscale(K)[:, None]
    u = mx_kscale(S)
    idx = np.random.permutation(T)[:S]
    tab_words, tab_scales = pack_weight(n((K, T)) / np.sqrt(K) * s, "e4m3")
    tab2_words, tab2_scales = pack_weight(n((K, T)) / np.sqrt(K) * s, "e4m3")
    w4_words, w4_scales = pack_weight(n((K, N)) / np.sqrt(K) * s, "e2m1")
    wdT = n((N, T)) / np.sqrt(S)
    wdT[:, idx] /= u
    return {
        "x": (n((K, M)) / s).astype(np.float32),
        "tab_words": tab_words, "tab_scales": tab_scales,
        "tab2_words": tab2_words, "tab2_scales": tab2_scales,
        "offs": striped(idx),
        "g": (np.exp(0.3 * n(S)) * u).astype(np.float32),
        "wdT": wdT.astype(np.float32),
        "w4_words": w4_words, "w4_scales": w4_scales,
    }

def reference(x, tab_words, tab_scales, tab2_words, tab2_scales, offs, g, wdT, w4_words, w4_scales):
    v = unpack_weight(tab_words, tab_scales, "e4m3")[:, unstriped(offs)]
    v2 = unpack_weight(tab2_words, tab2_scales, "e4m3")[:, unstriped(offs)]
    w4 = unpack_weight(w4_words, w4_scales, "e2m1")
    xq = mxq(f64(x), 0, "e4m3")
    a = v.T @ xq
    b = v2.T @ xq
    h = np.abs(np.tanh(a) - np.tanh(b)) * f64(g)[:, None]
    wd = f64(wdT)[:, unstriped(offs)]
    return mxq(wd, 1, "e4m3") @ mxq(h, 0, "e4m3") + w4.T @ xq

@@ -1,0 +1,249 @@
+from contextlib import ExitStack
+
+import concourse.mybir as mybir
+from concourse.masks import make_identity
+
+K, T, S, M, N = 1024, 2048, 1024, 512, 512
+FLOPS = 2 * (2 * K * S * M + S * N * M + K * N * M)
+
+F32 = mybir.dt.float32
+BF16 = mybir.dt.bfloat16
+I32 = mybir.dt.int32
+U32 = mybir.dt.uint32
+U16 = mybir.dt.uint16
+U8 = mybir.dt.uint8
+FP8X4 = mybir.dt.float8_e4m3fn_x4
+FP4X4 = mybir.dt.float4_e2m1fn_x4
+ACT = mybir.ActivationFunctionType
+ALU = mybir.AluOpType
+
+P = 128
+PACK = 4
+PASS = P * PACK
+K_PASSES = K // PASS
+J_PASSES = S // PASS
+M_TILES = M // P
+N_TILES = N // P
+LIST_COLS = PASS // 16
+
+
+def tile_list_regime_spread_hedge_kernel(
+    tc, x, tab_words, tab_scales, tab2_words, tab2_scales, offs, g, wdT, w4_words, w4_scales, out
+):
+    nc = tc.nc
+    with ExitStack() as ctx:
+        keep = ctx.enter_context(tc.tile_pool(name="keep", bufs=1))
+        ring = ctx.enter_context(tc.tile_pool(name="ring", bufs=3))
+        psum = ctx.enter_context(tc.psum_pool(name="psum", bufs=1))
+
+        offsets = keep.tile([P, S // 16], U16, name="offsets")
+        nc.sync.dma_start(offsets[:], offs)
+
+        scale_rows = [keep.tile([P, T // 4], I32, name="scale_rows%d" % i, align_bytes=64) for i in range(2)]
+        w4_plane = keep.tile([P, K_PASSES, N // 4], I32, name="w4_plane", align_bytes=64)
+        for tile in scale_rows:
+            nc.vector.memset(tile[:], 0)
+        nc.vector.memset(w4_plane[:], 0)
+
+        ident = keep.tile([P, P], F32, name="ident")
+        make_identity(nc, ident[:])
+        warm = keep.tile([P, 1], F32, name="warm")
+        nc.scalar.activation(warm[:], ident[:, 0:1], ACT.Tanh)
+
+        words = [[keep.tile([P, T], U32, name="words%d_%d" % (i, a), align_bytes=64) for a in range(K_PASSES)] for i in range(2)]
+        x_raw = [keep.tile([P, PACK, M], F32, name="x_raw%d" % a) for a in range(K_PASSES)]
+        wd_raw = [keep.tile([P, T], F32, name="wd_raw%d" % n, align_bytes=64) for n in range(N_TILES)]
+        gains = keep.tile([P, J_PASSES, PACK], F32, name="gains")
+        w4_codes = keep.tile([P, K_PASSES, 2 * N], U8, name="w4_codes", align_bytes=64)
+
+        def load_scale_rows(i, src):
+            for q in range(4):
+                nc.sync.dma_start(scale_rows[i][32 * q : 32 * q + 8, :], src[:, 4 * q : 4 * q + 4, :].bitcast(I32))
+
+        def load_words(i, src, a):
+            nc.sync.dma_start(words[i][a][:].bitcast(I32), src[a].rearrange("p t i -> p (t i)").bitcast(I32))
+
+        def load_x(a):
+            nc.sync.dma_start(x_raw[a][:], x[a * PASS : (a + 1) * PASS, :].rearrange("(p i) m -> p i m", i=PACK))
+
+        def load_wd(n):
+            nc.sync.dma_start(wd_raw[n][:], wdT[n * P : (n + 1) * P, :])
+
+        load_scale_rows(0, tab_scales)
+        load_words(0, tab_words, 0)
+        load_scale_rows(1, tab2_scales)
+        load_x(0)
+        load_x(1)
+        load_words(0, tab_words, 1)
+        load_words(1, tab2_words, 0)
+        load_words(1, tab2_words, 1)
+        nc.sync.dma_start(gains[:], g.rearrange("(b p i) -> p b i", p=P, i=PACK))
+        load_wd(0)
+        nc.sync.dma_start(w4_codes[:].bitcast(I32), w4_words.rearrange("a p c -> p a c").bitcast(I32))
+        for q in range(4):
+            nc.sync.dma_start(
+                w4_plane[32 * q : 32 * q + 4, :, :],
+                w4_scales[:, 4 * q : 4 * q + 4, :].rearrange("a r c -> r a c").bitcast(I32),
+            )
+        for n in range(1, N_TILES):
+            load_wd(n)
+
+        picked_scales = [keep.tile([P, S], U8, name="picked_scales%d" % i, align_bytes=64) for i in range(2)]
+        picked_words = [
+            [[keep.tile([P, PASS], U32, name="picked_words%d_%d_%d" % (i, a, b), align_bytes=64) for b in range(J_PASSES)] for a in range(K_PASSES)]
+            for i in range(2)
+        ]
+
+        def gather_scales(i):
+            nc.vector.tensor_copy(picked_scales[i][:], scale_rows[i][:].bitcast(U8).indirect(offsets[:]))
+
+        def gather_words(i, a):
+            for b in range(J_PASSES):
+                nc.vector.tensor_copy(
+                    picked_words[i][a][b][:],
+                    words[i][a][:].indirect(offsets[:, b * LIST_COLS : (b + 1) * LIST_COLS]),
+                )
+
+        x_codes = [keep.tile([P, M], U32, name="x_codes%d" % a, align_bytes=64) for a in range(K_PASSES)]
+        x_plane = [keep.tile([P, M], U8, name="x_plane%d" % a, align_bytes=64) for a in range(K_PASSES)]
+        HALF = M // 2
+
+        def quantise_x(a):
+            for half in range(2):
+                cols = slice(half * HALF, (half + 1) * HALF)
+                x_bf = ring.tile([P, HALF, PACK], BF16, name="x_bf", align_bytes=64)
+                nc.scalar.copy(
+                    x_bf[:].rearrange("p (c e) i -> p c i e", e=4),
+                    x_raw[a][:, :, cols].rearrange("p i (c e) -> p c i e", e=4),
+                )
+                nc.vector.quantize_mx(
+                    out=x_codes[a][:, cols].bitcast(FP8X4),
+                    scales=x_plane[a][:, cols],
+                    in_=x_bf[:].rearrange("p m i -> p (m i)"),
+                )
+
+        gather_scales(0)
+        gather_words(0, 0)
+        gather_scales(1)
+        quantise_x(0)
+        quantise_x(1)
+        gather_words(0, 1)
+        gather_words(1, 0)
+        gather_words(1, 1)
+
+        def response(i, b, mt, sign, dst):
+            acc = psum.tile([P, PASS], F32, name="resp", bufs=3)
+            for a in range(K_PASSES):
+                nc.tensor.matmul_mx(
+                    out=acc[:],
+                    lhsT=x_codes[a][:, mt * P : (mt + 1) * P].bitcast(FP8X4),
+                    lhsT_scale=x_plane[a][:, mt * P : (mt + 1) * P],
+                    rhs=picked_words[i][a][b][:].bitcast(FP8X4),
+                    rhs_scale=picked_scales[i][4 * a : P, b * PASS : (b + 1) * PASS],
+                    start=(a == 0),
+                    stop=(a == K_PASSES - 1),
+                )
+            nc.scalar.activation(dst[:], acc[:].rearrange("m (p i) -> m i p", i=PACK), ACT.Tanh, scale=sign)
+
+        chunks = [(b, mt) for b in range(J_PASSES) for mt in range(M_TILES)]
+        calm = {}
+        for b, mt in chunks:
+            calm[b, mt] = keep.tile([P, PACK, P], F32, name="calm%d_%d" % (b, mt))
+        h_bf = [keep.tile([P, M, PACK], BF16, name="h_bf%d" % b, align_bytes=64) for b in range(J_PASSES)]
+        h_codes = [keep.tile([P, M], U32, name="h_codes%d" % b, align_bytes=64) for b in range(J_PASSES)]
+        h_plane = [keep.tile([P, M], U8, name="h_plane%d" % b, align_bytes=64) for b in range(J_PASSES)]
+
+        for b, mt in chunks:
+            response(0, b, mt, 1.0, calm[b, mt])
+
+        stressed = {}
+
+        def stress(c):
+            stressed[c] = ring.tile([P, PACK, P], F32, name="stressed")
+            response(1, c[0], c[1], -1.0, stressed[c])
+
+        def spread(c):
+            b, mt = c
+            diff = psum.tile([P, PACK, P], F32, name="diff", bufs=2)
+            for i in range(PACK):
+                nc.tensor.matmul(diff[:, i, :], stressed[c][:, i, :], ident[:], start=True, stop=False, is_transpose=True)
+                nc.tensor.matmul(diff[:, i, :], calm[c][:, i, :], ident[:], start=False, stop=True, is_transpose=True)
+            size = ring.tile([P, P, PACK], F32, name="size")
+            nc.scalar.activation(size[:], diff[:].rearrange("p i m -> p m i"), ACT.Abs)
+            nc.vector.tensor_tensor(
+                h_bf[b][:, mt * P : (mt + 1) * P, :],
+                size[:],
+                gains[:, b : b + 1, :].to_broadcast([P, P, PACK]),
+                ALU.mult,
+            )
+
+        def quantise_h(b, half):
+            cols = slice(half * HALF, (half + 1) * HALF)
+            nc.vector.quantize_mx(
+                out=h_codes[b][:, cols].bitcast(FP8X4),
+                scales=h_plane[b][:, cols],
+                in_=h_bf[b][:, cols, :].rearrange("p m i -> p (m i)"),
+            )
+
+        wd_codes = [keep.tile([P, J_PASSES * P], U32, name="wd_codes%d" % n, align_bytes=64) for n in range(N_TILES)]
+        wd_plane = [keep.tile([P, J_PASSES * P], U8, name="wd_plane%d" % n, align_bytes=64) for n in range(N_TILES)]
+
+        def down_weights(n):
+            wd_bf = ring.tile([P, 2, S // PACK, 2], BF16, name="wd_bf", align_bytes=64, bufs=N_TILES)
+            nc.vector.tensor_copy(wd_bf[:].rearrange("n u c e -> n c u e"), wd_raw[n][:].indirect(offsets[:]))
+            pairs = wd_bf[:].rearrange("n u c e -> n u (c e)").bitcast(F32)
+            turned = psum.tile([P, J_PASSES, 2, P], F32, name="turned", bufs=1)
+            for b in range(J_PASSES):
+                for u in range(2):
+                    nc.tensor.transpose(turned[:, b, u, :], pairs[:, u, b * P : (b + 1) * P], ident[:])
+            wd_in = ring.tile([P, J_PASSES, P, 2], F32, name="wd_in", align_bytes=64)
+            nc.scalar.copy(wd_in[:], turned[:].rearrange("p b u n -> p b n u"))
+            nc.vector.quantize_mx(
+                out=wd_codes[n][:].bitcast(FP8X4),
+                scales=wd_plane[n][:],
+                in_=wd_in[:].rearrange("p b n u -> p (b n u)").bitcast(BF16),
+            )
+
+        stress(chunks[0])
+        for s, c in enumerate(chunks):
+            if s + 1 < len(chunks):
+                stress(chunks[s + 1])
+            spread(c)
+            if s >= 2 and s % 2 == 0:
+                quantise_h((s - 2) // M_TILES, ((s - 2) % M_TILES) // 2)
+            if s % 2 == 1 and s // 2 < N_TILES - 1:
+                down_weights(s // 2)
+        quantise_h(J_PASSES - 1, 1)
+        down_weights(N_TILES - 1)
+
+        for n in range(N_TILES):
+            if n < 2:
+                total = psum.tile([P, M], F32, name="total", bufs=2)
+            else:
+                total = psum.tile([P, M], F32, name="resp", bufs=3)
+            for a in range(K_PASSES):
+                nc.tensor.matmul_mx(
+                    out=total[:],
+                    lhsT=w4_codes[:, a, 2 * n * P : 2 * (n + 1) * P].bitcast(FP4X4),
+                    lhsT_scale=w4_plane[:, a, :].bitcast(U8)[:, n * P : (n + 1) * P],
+                    rhs=x_codes[a][:].bitcast(FP8X4),
+                    rhs_scale=x_plane[a][:],
+                    start=(a == 0),
+                    stop=False,
+                )
+            for b in range(J_PASSES):
+                nc.tensor.matmul_mx(
+                    out=total[:],
+                    lhsT=wd_codes[n][:, b * P : (b + 1) * P].bitcast(FP8X4),
+                    lhsT_scale=wd_plane[n][:, b * P : (b + 1) * P],
+                    rhs=h_codes[b][:].bitcast(FP8X4),
+                    rhs_scale=h_plane[b][:],
+                    start=False,
+                    stop=(b == J_PASSES - 1),
+                )
+            result = ring.tile([P, M], F32, name="result", bufs=N_TILES)
+            if n % 2 == 0:
+                nc.scalar.copy(result[:], total[:])
+            else:
+                nc.vector.tensor_copy(result[:], total[:])
+            nc.sync.dma_start(out[n * P : (n + 1) * P, :], result[:])

@@ -24,7 +24,6 @@ K_PASSES = K // PASS
 J_PASSES = S // PASS
 M_TILES = M // P
 N_TILES = N // P
-LIST_COLS = PASS // 16
 
 
 def tile_list_regime_spread_hedge_kernel(
@@ -35,14 +34,15 @@ def tile_list_regime_spread_hedge_kernel(
         keep = ctx.enter_context(tc.tile_pool(name="keep", bufs=1))
         ring = ctx.enter_context(tc.tile_pool(name="ring", bufs=3))
         psum = ctx.enter_context(tc.psum_pool(name="psum", bufs=1))
+        reuse = ctx.enter_context(tc.tile_pool(name="reuse", bufs=1))
 
         offsets = keep.tile([P, S // 16], U16, name="offsets")
         nc.sync.dma_start(offsets[:], offs)
 
         scale_rows = [keep.tile([P, T // 4], I32, name="scale_rows%d" % i, align_bytes=64) for i in range(2)]
         w4_plane = keep.tile([P, K_PASSES, N // 4], I32, name="w4_plane", align_bytes=64)
-        for tile in scale_rows:
-            nc.vector.memset(tile[:], 0)
+        nc.gpsimd.memset(scale_rows[0][:], 0)
+        nc.vector.memset(scale_rows[1][:], 0)
         nc.vector.memset(w4_plane[:], 0)
 
         ident = keep.tile([P, P], F32, name="ident")
@@ -52,13 +52,14 @@ def tile_list_regime_spread_hedge_kernel(
 
         words = [[keep.tile([P, T], U32, name="words%d_%d" % (i, a), align_bytes=64) for a in range(K_PASSES)] for i in range(2)]
         x_raw = [keep.tile([P, PACK, M], F32, name="x_raw%d" % a) for a in range(K_PASSES)]
-        wd_raw = [keep.tile([P, T], F32, name="wd_raw%d" % n, align_bytes=64) for n in range(N_TILES)]
-        gains = keep.tile([P, J_PASSES, PACK], F32, name="gains")
+        wd_raw = [keep.tile([P, T], F32, name="wd_raw%d" % n, align_bytes=64) for n in range(N_TILES - 1)]
+        wd_raw.append(reuse.tile([P, T], F32, name="wd_raw_last", align_bytes=64, offset=0))
+        gains = keep.tile([P, J_PASSES, 2 * PACK], F32, name="gains")
         w4_codes = keep.tile([P, K_PASSES, 2 * N], U8, name="w4_codes", align_bytes=64)
 
-        def load_scale_rows(i, src):
+        def load_scale_rows(i, src, queue):
             for q in range(4):
-                nc.sync.dma_start(scale_rows[i][32 * q : 32 * q + 8, :], src[:, 4 * q : 4 * q + 4, :].bitcast(I32))
+                queue.dma_start(scale_rows[i][32 * q : 32 * q + 8, :], src[:, 4 * q : 4 * q + 4, :].bitcast(I32))
 
         def load_words(i, src, a):
             nc.sync.dma_start(words[i][a][:].bitcast(I32), src[a].rearrange("p t i -> p (t i)").bitcast(I32))
@@ -69,28 +70,27 @@ def tile_list_regime_spread_hedge_kernel(
         def load_wd(n):
             nc.sync.dma_start(wd_raw[n][:], wdT[n * P : (n + 1) * P, :])
 
-        load_scale_rows(0, tab_scales)
+        load_scale_rows(0, tab_scales, nc.sync)
         load_words(0, tab_words, 0)
-        load_scale_rows(1, tab2_scales)
+        load_scale_rows(1, tab2_scales, nc.sync)
         load_x(0)
         load_x(1)
         load_words(0, tab_words, 1)
         load_words(1, tab2_words, 0)
         load_words(1, tab2_words, 1)
-        nc.sync.dma_start(gains[:], g.rearrange("(b p i) -> p b i", p=P, i=PACK))
-        load_wd(0)
+        nc.sync.dma_start(gains[:, :, 0:PACK], g.rearrange("(b p i) -> p b i", p=P, i=PACK))
+        for n in range(N_TILES):
+            load_wd(n)
         nc.sync.dma_start(w4_codes[:].bitcast(I32), w4_words.rearrange("a p c -> p a c").bitcast(I32))
         for q in range(4):
             nc.sync.dma_start(
                 w4_plane[32 * q : 32 * q + 4, :, :],
                 w4_scales[:, 4 * q : 4 * q + 4, :].rearrange("a r c -> r a c").bitcast(I32),
             )
-        for n in range(1, N_TILES):
-            load_wd(n)
 
         picked_scales = [keep.tile([P, S], U8, name="picked_scales%d" % i, align_bytes=64) for i in range(2)]
         picked_words = [
-            [[keep.tile([P, PASS], U32, name="picked_words%d_%d_%d" % (i, a, b), align_bytes=64) for b in range(J_PASSES)] for a in range(K_PASSES)]
+            [keep.tile([P, S], U32, name="picked_words%d_%d" % (i, a), align_bytes=64) for a in range(K_PASSES)]
             for i in range(2)
         ]
 
@@ -98,10 +98,12 @@ def tile_list_regime_spread_hedge_kernel(
             nc.vector.tensor_copy(picked_scales[i][:], scale_rows[i][:].bitcast(U8).indirect(offsets[:]))
 
         def gather_words(i, a):
-            for b in range(J_PASSES):
+            pieces = 1 if a == 0 else J_PASSES
+            for piece in range(pieces):
+                lo, hi = piece * S // pieces, (piece + 1) * S // pieces
                 nc.vector.tensor_copy(
-                    picked_words[i][a][b][:],
-                    words[i][a][:].indirect(offsets[:, b * LIST_COLS : (b + 1) * LIST_COLS]),
+                    picked_words[i][a][:, lo:hi],
+                    words[i][a][:].indirect(offsets[:, lo // 16 : hi // 16]),
                 )
 
         x_codes = [keep.tile([P, M], U32, name="x_codes%d" % a, align_bytes=64) for a in range(K_PASSES)]
@@ -138,7 +140,7 @@ def tile_list_regime_spread_hedge_kernel(
                     out=acc[:],
                     lhsT=x_codes[a][:, mt * P : (mt + 1) * P].bitcast(FP8X4),
                     lhsT_scale=x_plane[a][:, mt * P : (mt + 1) * P],
-                    rhs=picked_words[i][a][b][:].bitcast(FP8X4),
+                    rhs=picked_words[i][a][:, b * PASS : (b + 1) * PASS].bitcast(FP8X4),
                     rhs_scale=picked_scales[i][4 * a : P, b * PASS : (b + 1) * PASS],
                     start=(a == 0),
                     stop=(a == K_PASSES - 1),
@@ -149,7 +151,7 @@ def tile_list_regime_spread_hedge_kernel(
         calm = {}
         for b, mt in chunks:
             calm[b, mt] = keep.tile([P, PACK, P], F32, name="calm%d_%d" % (b, mt))
-        h_bf = [keep.tile([P, M, PACK], BF16, name="h_bf%d" % b, align_bytes=64) for b in range(J_PASSES)]
+        h_bf = reuse.tile([P, J_PASSES, M, PACK], BF16, name="h_bf", align_bytes=64, offset=4096)
         h_codes = [keep.tile([P, M], U32, name="h_codes%d" % b, align_bytes=64) for b in range(J_PASSES)]
         h_plane = [keep.tile([P, M], U8, name="h_plane%d" % b, align_bytes=64) for b in range(J_PASSES)]
 
@@ -157,9 +159,10 @@ def tile_list_regime_spread_hedge_kernel(
             response(0, b, mt, 1.0, calm[b, mt])
 
         stressed = {}
+        size = keep.tile([P, J_PASSES, M, PACK], F32, name="size")
 
         def stress(c):
-            stressed[c] = ring.tile([P, PACK, P], F32, name="stressed")
+            stressed[c] = ring.tile([P, PACK, P], F32, name="stressed", bufs=len(chunks))
             response(1, c[0], c[1], -1.0, stressed[c])
 
         def spread(c):
@@ -168,12 +171,14 @@ def tile_list_regime_spread_hedge_kernel(
             for i in range(PACK):
                 nc.tensor.matmul(diff[:, i, :], stressed[c][:, i, :], ident[:], start=True, stop=False, is_transpose=True)
                 nc.tensor.matmul(diff[:, i, :], calm[c][:, i, :], ident[:], start=False, stop=True, is_transpose=True)
-            size = ring.tile([P, P, PACK], F32, name="size")
-            nc.scalar.activation(size[:], diff[:].rearrange("p i m -> p m i"), ACT.Abs)
+            nc.scalar.activation(size[:, b, mt * P : (mt + 1) * P, :], diff[:].rearrange("p i m -> p m i"), ACT.Abs)
+
+        def weigh(b, half):
+            cols = slice(half * HALF, (half + 1) * HALF)
             nc.vector.tensor_tensor(
-                h_bf[b][:, mt * P : (mt + 1) * P, :],
-                size[:],
-                gains[:, b : b + 1, :].to_broadcast([P, P, PACK]),
+                h_bf[:, b, cols, :],
+                size[:, b, cols, :],
+                gains[:, b : b + 1, 0:PACK].to_broadcast([P, HALF, PACK]),
                 ALU.mult,
             )
 
@@ -182,13 +187,14 @@ def tile_list_regime_spread_hedge_kernel(
             nc.vector.quantize_mx(
                 out=h_codes[b][:, cols].bitcast(FP8X4),
                 scales=h_plane[b][:, cols],
-                in_=h_bf[b][:, cols, :].rearrange("p m i -> p (m i)"),
+                in_=h_bf[:, b, cols, :].rearrange("p m i -> p (m i)"),
             )
 
-        wd_codes = [keep.tile([P, J_PASSES * P], U32, name="wd_codes%d" % n, align_bytes=64) for n in range(N_TILES)]
-        wd_plane = [keep.tile([P, J_PASSES * P], U8, name="wd_plane%d" % n, align_bytes=64) for n in range(N_TILES)]
+        wd_codes = reuse.tile([P, N_TILES, J_PASSES * P], U32, name="wd_codes", align_bytes=64, offset=0)
+        wd_plane = keep.tile([P, N_TILES, J_PASSES * P], U8, name="wd_plane", align_bytes=64)
+        wd_in = keep.tile([P, N_TILES, J_PASSES, P, 2], F32, name="wd_in", align_bytes=64)
 
-        def down_weights(n):
+        def turn_wd(n):
             wd_bf = ring.tile([P, 2, S // PACK, 2], BF16, name="wd_bf", align_bytes=64, bufs=N_TILES)
             nc.vector.tensor_copy(wd_bf[:].rearrange("n u c e -> n c u e"), wd_raw[n][:].indirect(offsets[:]))
             pairs = wd_bf[:].rearrange("n u c e -> n u (c e)").bitcast(F32)
@@ -196,25 +202,33 @@ def tile_list_regime_spread_hedge_kernel(
             for b in range(J_PASSES):
                 for u in range(2):
                     nc.tensor.transpose(turned[:, b, u, :], pairs[:, u, b * P : (b + 1) * P], ident[:])
-            wd_in = ring.tile([P, J_PASSES, P, 2], F32, name="wd_in", align_bytes=64)
-            nc.scalar.copy(wd_in[:], turned[:].rearrange("p b u n -> p b n u"))
+            nc.scalar.copy(wd_in[:, n, :, :, :], turned[:].rearrange("p b u n -> p b n u"))
+
+        def quantise_wd(pair):
+            tiles = slice(2 * pair, 2 * pair + 2)
             nc.vector.quantize_mx(
-                out=wd_codes[n][:].bitcast(FP8X4),
-                scales=wd_plane[n][:],
-                in_=wd_in[:].rearrange("p b n u -> p (b n u)").bitcast(BF16),
+                out=wd_codes[:, tiles, :].rearrange("p n c -> p (n c)").bitcast(FP8X4),
+                scales=wd_plane[:, tiles, :].rearrange("p n c -> p (n c)"),
+                in_=wd_in[:, tiles, :, :, :].rearrange("p t b n u -> p (t b n u)").bitcast(BF16),
             )
 
-        stress(chunks[0])
+        for c in chunks:
+            stress(c)
         for s, c in enumerate(chunks):
-            if s + 1 < len(chunks):
-                stress(chunks[s + 1])
+            if s % 2 == 0:
+                turn_wd(s // 2)
             spread(c)
-            if s >= 2 and s % 2 == 0:
-                quantise_h((s - 2) // M_TILES, ((s - 2) % M_TILES) // 2)
-            if s % 2 == 1 and s // 2 < N_TILES - 1:
-                down_weights(s // 2)
-        quantise_h(J_PASSES - 1, 1)
-        down_weights(N_TILES - 1)
+
+        weigh(0, 0)
+        quantise_wd(0)
+        weigh(0, 1)
+        quantise_h(0, 0)
+        quantise_wd(1)
+        quantise_h(0, 1)
+        weigh(1, 0)
+        weigh(1, 1)
+        quantise_h(1, 0)
+        quantise_h(1, 1)
 
         for n in range(N_TILES):
             if n < 2:
@@ -234,8 +248,8 @@ def tile_list_regime_spread_hedge_kernel(
             for b in range(J_PASSES):
                 nc.tensor.matmul_mx(
                     out=total[:],
-                    lhsT=wd_codes[n][:, b * P : (b + 1) * P].bitcast(FP8X4),
-                    lhsT_scale=wd_plane[n][:, b * P : (b + 1) * P],
+                    lhsT=wd_codes[:, n, b * P : (b + 1) * P].bitcast(FP8X4),
+                    lhsT_scale=wd_plane[:, n, b * P : (b + 1) * P],
                     rhs=h_codes[b][:].bitcast(FP8X4),
                     rhs_scale=h_plane[b][:],
                     start=False,

@@ -24,6 +24,8 @@ K_PASSES = K // PASS
 J_PASSES = S // PASS
 M_TILES = M // P
 N_TILES = N // P
+BANK = 2048
+WORK_BANKS = 4
 
 
 def tile_list_regime_spread_hedge_kernel(
@@ -35,6 +37,15 @@ def tile_list_regime_spread_hedge_kernel(
         ring = ctx.enter_context(tc.tile_pool(name="ring", bufs=3))
         psum = ctx.enter_context(tc.psum_pool(name="psum", bufs=1))
         reuse = ctx.enter_context(tc.tile_pool(name="reuse", bufs=1))
+
+        used = []
+
+        def next_turn():
+            used.append(len(used))
+            return used[-1]
+
+        def work_bank(shape, name):
+            return psum.tile(shape, F32, name=name, offset=BANK * (next_turn() % WORK_BANKS))
 
         offsets = keep.tile([P, S // 16], U16, name="offsets")
         nc.sync.dma_start(offsets[:], offs)
@@ -75,18 +86,18 @@ def tile_list_regime_spread_hedge_kernel(
         load_scale_rows(1, tab2_scales, nc.sync)
         load_x(0)
         load_x(1)
-        load_words(0, tab_words, 1)
-        load_words(1, tab2_words, 0)
-        load_words(1, tab2_words, 1)
         nc.sync.dma_start(gains[:, :, 0:PACK], g.rearrange("(b p i) -> p b i", p=P, i=PACK))
-        for n in range(N_TILES):
-            load_wd(n)
         nc.sync.dma_start(w4_codes[:].bitcast(I32), w4_words.rearrange("a p c -> p a c").bitcast(I32))
         for q in range(4):
             nc.sync.dma_start(
                 w4_plane[32 * q : 32 * q + 4, :, :],
                 w4_scales[:, 4 * q : 4 * q + 4, :].rearrange("a r c -> r a c").bitcast(I32),
             )
+        load_words(0, tab_words, 1)
+        load_words(1, tab2_words, 0)
+        load_words(1, tab2_words, 1)
+        for n in range(N_TILES):
+            load_wd(n)
 
         picked_scales = [keep.tile([P, S], U8, name="picked_scales%d" % i, align_bytes=64) for i in range(2)]
         picked_words = [
@@ -113,7 +124,7 @@ def tile_list_regime_spread_hedge_kernel(
         def quantise_x(a):
             for half in range(2):
                 cols = slice(half * HALF, (half + 1) * HALF)
-                x_bf = ring.tile([P, HALF, PACK], BF16, name="x_bf", align_bytes=64)
+                x_bf = ring.tile([P, HALF, PACK], BF16, name="x_bf", align_bytes=64, bufs=4)
                 nc.scalar.copy(
                     x_bf[:].rearrange("p (c e) i -> p c i e", e=4),
                     x_raw[a][:, :, cols].rearrange("p i (c e) -> p c i e", e=4),
@@ -133,8 +144,22 @@ def tile_list_regime_spread_hedge_kernel(
         gather_words(1, 0)
         gather_words(1, 1)
 
+        totals = [psum.tile([P, M], F32, name="total%d" % n, offset=BANK * (WORK_BANKS + n)) for n in range(N_TILES)]
+        for a in range(K_PASSES):
+            for n in range(N_TILES):
+                total = totals[n]
+                nc.tensor.matmul_mx(
+                    out=total[:],
+                    lhsT=w4_codes[:, a, 2 * n * P : 2 * (n + 1) * P].bitcast(FP4X4),
+                    lhsT_scale=w4_plane[:, a, :].bitcast(U8)[:, n * P : (n + 1) * P],
+                    rhs=x_codes[a][:].bitcast(FP8X4),
+                    rhs_scale=x_plane[a][:],
+                    start=(a == 0),
+                    stop=False,
+                )
+
         def response(i, b, mt, sign, dst):
-            acc = psum.tile([P, PASS], F32, name="resp", bufs=3)
+            acc = work_bank([P, PASS], "resp%d_%d_%d" % (i, b, mt))
             for a in range(K_PASSES):
                 nc.tensor.matmul_mx(
                     out=acc[:],
@@ -151,8 +176,14 @@ def tile_list_regime_spread_hedge_kernel(
         calm = {}
         for b, mt in chunks:
             calm[b, mt] = keep.tile([P, PACK, P], F32, name="calm%d_%d" % (b, mt))
-        h_bf = reuse.tile([P, J_PASSES, M, PACK], BF16, name="h_bf", align_bytes=64, offset=4096)
-        h_codes = [keep.tile([P, M], U32, name="h_codes%d" % b, align_bytes=64) for b in range(J_PASSES)]
+        h_bf = [keep.tile([P, HALF, PACK], BF16, name="h_bf%d" % k, align_bytes=64) for k in range(2)]
+        h_late = reuse.tile([P, 2, HALF, PACK], BF16, name="h_late", align_bytes=64, offset=0)
+        h_bf.extend(h_late[:, k, :, :] for k in range(2))
+        codes = reuse.tile([P, J_PASSES * M + N_TILES * J_PASSES * P], U32, name="codes", align_bytes=64, offset=4096)
+        h_codes = [codes[:, b * M : (b + 1) * M] for b in range(J_PASSES)]
+        gain_rows = keep.tile([P, J_PASSES, P, PACK], F32, name="gain_rows")
+        for b in range(J_PASSES):
+            nc.scalar.copy(gain_rows[:, b, :, :], gains[:, b : b + 1, 0:PACK].to_broadcast([P, P, PACK]))
         h_plane = [keep.tile([P, M], U8, name="h_plane%d" % b, align_bytes=64) for b in range(J_PASSES)]
 
         for b, mt in chunks:
@@ -167,18 +198,18 @@ def tile_list_regime_spread_hedge_kernel(
 
         def spread(c):
             b, mt = c
-            diff = psum.tile([P, PACK, P], F32, name="diff", bufs=2)
+            diff = work_bank([P, PACK, P], "diff%d_%d" % c)
             for i in range(PACK):
                 nc.tensor.matmul(diff[:, i, :], stressed[c][:, i, :], ident[:], start=True, stop=False, is_transpose=True)
                 nc.tensor.matmul(diff[:, i, :], calm[c][:, i, :], ident[:], start=False, stop=True, is_transpose=True)
             nc.scalar.activation(size[:, b, mt * P : (mt + 1) * P, :], diff[:].rearrange("p i m -> p m i"), ACT.Abs)
 
-        def weigh(b, half):
-            cols = slice(half * HALF, (half + 1) * HALF)
-            nc.vector.tensor_tensor(
-                h_bf[:, b, cols, :],
-                size[:, b, cols, :],
-                gains[:, b : b + 1, 0:PACK].to_broadcast([P, HALF, PACK]),
+        def weigh(c, engine):
+            b, mt = c
+            engine.tensor_tensor(
+                h_bf[2 * b + mt // 2][:, (mt % 2) * P : (mt % 2 + 1) * P, :],
+                size[:, b, mt * P : (mt + 1) * P, :],
+                gain_rows[:, b, :, :],
                 ALU.mult,
             )
 
@@ -187,21 +218,23 @@ def tile_list_regime_spread_hedge_kernel(
             nc.vector.quantize_mx(
                 out=h_codes[b][:, cols].bitcast(FP8X4),
                 scales=h_plane[b][:, cols],
-                in_=h_bf[:, b, cols, :].rearrange("p m i -> p (m i)"),
+                in_=h_bf[2 * b + half][:, :, :].rearrange("p m i -> p (m i)"),
             )
 
-        wd_codes = reuse.tile([P, N_TILES, J_PASSES * P], U32, name="wd_codes", align_bytes=64, offset=0)
+        wd_codes = codes[:, J_PASSES * M :].rearrange("p (n c) -> p n c", n=N_TILES)
         wd_plane = keep.tile([P, N_TILES, J_PASSES * P], U8, name="wd_plane", align_bytes=64)
         wd_in = keep.tile([P, N_TILES, J_PASSES, P, 2], F32, name="wd_in", align_bytes=64)
 
+        wd_bf = [keep.tile([P, J_PASSES, PASS + 32], BF16, name="wd_bf%d" % n, align_bytes=64) for n in range(N_TILES)]
+        for n in range(N_TILES):
+            nc.vector.tensor_copy(wd_bf[n][:, :, 0:PASS], wd_raw[n][:].indirect(offsets[:]))
+
         def turn_wd(n):
-            wd_bf = ring.tile([P, 2, S // PACK, 2], BF16, name="wd_bf", align_bytes=64, bufs=N_TILES)
-            nc.vector.tensor_copy(wd_bf[:].rearrange("n u c e -> n c u e"), wd_raw[n][:].indirect(offsets[:]))
-            pairs = wd_bf[:].rearrange("n u c e -> n u (c e)").bitcast(F32)
-            turned = psum.tile([P, J_PASSES, 2, P], F32, name="turned", bufs=1)
+            pairs = wd_bf[n][:].bitcast(F32)
+            turned = work_bank([P, J_PASSES, 2, P], "turned%d" % n)
             for b in range(J_PASSES):
                 for u in range(2):
-                    nc.tensor.transpose(turned[:, b, u, :], pairs[:, u, b * P : (b + 1) * P], ident[:])
+                    nc.tensor.transpose(turned[:, b, u, :], pairs[:, b, u : 2 * P : 2], ident[:])
             nc.scalar.copy(wd_in[:, n, :, :, :], turned[:].rearrange("p b u n -> p b n u"))
 
         def quantise_wd(pair):
@@ -212,45 +245,45 @@ def tile_list_regime_spread_hedge_kernel(
                 in_=wd_in[:, tiles, :, :, :].rearrange("p t b n u -> p (t b n u)").bitcast(BF16),
             )
 
-        for c in chunks:
-            stress(c)
-        for s, c in enumerate(chunks):
-            if s % 2 == 0:
-                turn_wd(s // 2)
-            spread(c)
+        for s in (0, 1, 2, 3):
+            stress(chunks[s])
+        for s in (0, 1):
+            spread(chunks[s])
+        for s in (4, 5):
+            stress(chunks[s])
+        for s in (2, 3):
+            spread(chunks[s])
+        turn_wd(0)
+        for s in (6, 7):
+            stress(chunks[s])
+        for s in (4, 5):
+            spread(chunks[s])
+        for n in (1, 2, 3):
+            turn_wd(n)
+        for s in (6, 7):
+            spread(chunks[s])
 
-        weigh(0, 0)
-        quantise_wd(0)
-        weigh(0, 1)
+        for s in range(4):
+            weigh(chunks[s], nc.gpsimd)
         quantise_h(0, 0)
-        quantise_wd(1)
         quantise_h(0, 1)
-        weigh(1, 0)
-        weigh(1, 1)
+        weigh(chunks[4], nc.vector)
+        weigh(chunks[5], nc.vector)
+        quantise_wd(0)
         quantise_h(1, 0)
+        quantise_wd(1)
+        weigh(chunks[6], nc.vector)
+        weigh(chunks[7], nc.vector)
         quantise_h(1, 1)
 
         for n in range(N_TILES):
-            if n < 2:
-                total = psum.tile([P, M], F32, name="total", bufs=2)
-            else:
-                total = psum.tile([P, M], F32, name="resp", bufs=3)
-            for a in range(K_PASSES):
-                nc.tensor.matmul_mx(
-                    out=total[:],
-                    lhsT=w4_codes[:, a, 2 * n * P : 2 * (n + 1) * P].bitcast(FP4X4),
-                    lhsT_scale=w4_plane[:, a, :].bitcast(U8)[:, n * P : (n + 1) * P],
-                    rhs=x_codes[a][:].bitcast(FP8X4),
-                    rhs_scale=x_plane[a][:],
-                    start=(a == 0),
-                    stop=False,
-                )
+            total = totals[n]
             for b in range(J_PASSES):
                 nc.tensor.matmul_mx(
                     out=total[:],
                     lhsT=wd_codes[:, n, b * P : (b + 1) * P].bitcast(FP8X4),
                     lhsT_scale=wd_plane[:, n, b * P : (b + 1) * P],
-                    rhs=h_codes[b][:].bitcast(FP8X4),
+                    rhs=h_codes[b].bitcast(FP8X4),
                     rhs_scale=h_plane[b][:],
                     start=False,
                     stop=(b == J_PASSES - 1),

@@ -24,8 +24,13 @@ K_PASSES = K // PASS
 J_PASSES = S // PASS
 M_TILES = M // P
 N_TILES = N // P
+QUADRANTS = 4
+LIST_ROWS = 16
+X_COLS = M // 2
 BANK = 2048
 WORK_BANKS = 4
+POOL_CHUNKS = 5
+EARLY_TILES = 2
 
 
 def tile_list_regime_spread_hedge_kernel(
@@ -34,23 +39,21 @@ def tile_list_regime_spread_hedge_kernel(
     nc = tc.nc
     with ExitStack() as ctx:
         keep = ctx.enter_context(tc.tile_pool(name="keep", bufs=1))
-        ring = ctx.enter_context(tc.tile_pool(name="ring", bufs=3))
+        ring = ctx.enter_context(tc.tile_pool(name="ring", bufs=1))
         psum = ctx.enter_context(tc.psum_pool(name="psum", bufs=1))
         reuse = ctx.enter_context(tc.tile_pool(name="reuse", bufs=1))
 
-        used = []
-
-        def next_turn():
-            used.append(len(used))
-            return used[-1]
+        handed_out = []
 
         def work_bank(shape, name):
-            return psum.tile(shape, F32, name=name, offset=BANK * (next_turn() % WORK_BANKS))
+            bank = len(handed_out) % WORK_BANKS
+            handed_out.append(name)
+            return psum.tile(shape, F32, name=name, offset=BANK * bank)
 
-        offsets = keep.tile([P, S // 16], U16, name="offsets")
+        offsets = keep.tile([P, S // LIST_ROWS], U16, name="offsets")
         nc.sync.dma_start(offsets[:], offs)
 
-        scale_rows = [keep.tile([P, T // 4], I32, name="scale_rows%d" % i, align_bytes=64) for i in range(2)]
+        scale_rows = [keep.tile([P, T // 4], I32, name="scale_rows%d" % t, align_bytes=64) for t in range(2)]
         w4_plane = keep.tile([P, K_PASSES, N // 4], I32, name="w4_plane", align_bytes=64)
         nc.gpsimd.memset(scale_rows[0][:], 0)
         nc.vector.memset(scale_rows[1][:], 0)
@@ -58,76 +61,72 @@ def tile_list_regime_spread_hedge_kernel(
 
         ident = keep.tile([P, P], F32, name="ident")
         make_identity(nc, ident[:])
-        warm = keep.tile([P, 1], F32, name="warm")
-        nc.scalar.activation(warm[:], ident[:, 0:1], ACT.Tanh)
 
-        words = [[keep.tile([P, T], U32, name="words%d_%d" % (i, a), align_bytes=64) for a in range(K_PASSES)] for i in range(2)]
+        words = [
+            [keep.tile([P, T], U32, name="words%d_%d" % (t, a), align_bytes=64) for a in range(K_PASSES)]
+            for t in range(2)
+        ]
         x_raw = [keep.tile([P, PACK, M], F32, name="x_raw%d" % a) for a in range(K_PASSES)]
         wd_raw = [keep.tile([P, T], F32, name="wd_raw%d" % n, align_bytes=64) for n in range(N_TILES - 1)]
         wd_raw.append(reuse.tile([P, T], F32, name="wd_raw_last", align_bytes=64, offset=0))
         gains = keep.tile([P, J_PASSES, 2 * PACK], F32, name="gains")
         w4_codes = keep.tile([P, K_PASSES, 2 * N], U8, name="w4_codes", align_bytes=64)
 
-        def load_scale_rows(i, src, queue):
-            for q in range(4):
-                queue.dma_start(scale_rows[i][32 * q : 32 * q + 8, :], src[:, 4 * q : 4 * q + 4, :].bitcast(I32))
+        def load_scale_rows(t, src):
+            for q in range(QUADRANTS):
+                rows = scale_rows[t][32 * q : 32 * q + 4 * K_PASSES, :]
+                nc.sync.dma_start(rows, src[:, 4 * q : 4 * q + 4, :].bitcast(I32))
 
-        def load_words(i, src, a):
-            nc.sync.dma_start(words[i][a][:].bitcast(I32), src[a].rearrange("p t i -> p (t i)").bitcast(I32))
+        def load_words(t, src, a):
+            nc.sync.dma_start(words[t][a][:].bitcast(I32), src[a].rearrange("p c i -> p (c i)").bitcast(I32))
 
-        def load_x(a):
-            nc.sync.dma_start(x_raw[a][:], x[a * PASS : (a + 1) * PASS, :].rearrange("(p i) m -> p i m", i=PACK))
-
-        def load_wd(n):
-            nc.sync.dma_start(wd_raw[n][:], wdT[n * P : (n + 1) * P, :])
-
-        load_scale_rows(0, tab_scales, nc.sync)
+        load_scale_rows(0, tab_scales)
+        load_scale_rows(1, tab2_scales)
         load_words(0, tab_words, 0)
-        load_scale_rows(1, tab2_scales, nc.sync)
-        load_x(0)
-        load_x(1)
-        nc.sync.dma_start(gains[:, :, 0:PACK], g.rearrange("(b p i) -> p b i", p=P, i=PACK))
-        nc.sync.dma_start(w4_codes[:].bitcast(I32), w4_words.rearrange("a p c -> p a c").bitcast(I32))
-        for q in range(4):
+        for a in range(K_PASSES):
+            nc.sync.dma_start(x_raw[a][:], x[a * PASS : (a + 1) * PASS, :].rearrange("(p i) m -> p i m", i=PACK))
+        for q in range(QUADRANTS):
             nc.sync.dma_start(
                 w4_plane[32 * q : 32 * q + 4, :, :],
                 w4_scales[:, 4 * q : 4 * q + 4, :].rearrange("a r c -> r a c").bitcast(I32),
             )
+        nc.sync.dma_start(gains[:, :, 0:PACK], g.rearrange("(s p i) -> p s i", p=P, i=PACK))
+        nc.sync.dma_start(w4_codes[:].bitcast(I32), w4_words.rearrange("a p c -> p a c").bitcast(I32))
         load_words(0, tab_words, 1)
         load_words(1, tab2_words, 0)
         load_words(1, tab2_words, 1)
         for n in range(N_TILES):
-            load_wd(n)
+            nc.sync.dma_start(wd_raw[n][:], wdT[n * P : (n + 1) * P, :])
 
-        picked_scales = [keep.tile([P, S], U8, name="picked_scales%d" % i, align_bytes=64) for i in range(2)]
+        picked_scales = [keep.tile([P, S], U8, name="picked_scales%d" % t, align_bytes=64) for t in range(2)]
         picked_words = [
-            [keep.tile([P, S], U32, name="picked_words%d_%d" % (i, a), align_bytes=64) for a in range(K_PASSES)]
-            for i in range(2)
+            [keep.tile([P, S], U32, name="picked_words%d_%d" % (t, a), align_bytes=64) for a in range(K_PASSES)]
+            for t in range(2)
         ]
 
-        def gather_scales(i):
-            nc.vector.tensor_copy(picked_scales[i][:], scale_rows[i][:].bitcast(U8).indirect(offsets[:]))
+        def gather_scales(t):
+            nc.vector.tensor_copy(picked_scales[t][:], scale_rows[t][:].bitcast(U8).indirect(offsets[:]))
 
-        def gather_words(i, a):
-            pieces = 1 if a == 0 else J_PASSES
+        def gather_words(t, a):
+            pieces = J_PASSES if a == K_PASSES - 1 else 1
             for piece in range(pieces):
                 lo, hi = piece * S // pieces, (piece + 1) * S // pieces
                 nc.vector.tensor_copy(
-                    picked_words[i][a][:, lo:hi],
-                    words[i][a][:].indirect(offsets[:, lo // 16 : hi // 16]),
+                    picked_words[t][a][:, lo:hi],
+                    words[t][a][:].indirect(offsets[:, lo // LIST_ROWS : hi // LIST_ROWS]),
                 )
 
         x_codes = [keep.tile([P, M], U32, name="x_codes%d" % a, align_bytes=64) for a in range(K_PASSES)]
         x_plane = [keep.tile([P, M], U8, name="x_plane%d" % a, align_bytes=64) for a in range(K_PASSES)]
-        HALF = M // 2
 
         def quantise_x(a):
-            for half in range(2):
-                cols = slice(half * HALF, (half + 1) * HALF)
-                x_bf = ring.tile([P, HALF, PACK], BF16, name="x_bf", align_bytes=64, bufs=4)
-                nc.scalar.copy(
+            for m0 in range(0, M, X_COLS):
+                cols = slice(m0, m0 + X_COLS)
+                x_bf = ring.tile([P, X_COLS, PACK], BF16, name="x_bf", align_bytes=64, bufs=K_PASSES * M // X_COLS)
+                nc.scalar.activation(
                     x_bf[:].rearrange("p (c e) i -> p c i e", e=4),
                     x_raw[a][:, :, cols].rearrange("p i (c e) -> p c i e", e=4),
+                    ACT.Copy,
                 )
                 nc.vector.quantize_mx(
                     out=x_codes[a][:, cols].bitcast(FP8X4),
@@ -147,9 +146,8 @@ def tile_list_regime_spread_hedge_kernel(
         totals = [psum.tile([P, M], F32, name="total%d" % n, offset=BANK * (WORK_BANKS + n)) for n in range(N_TILES)]
         for a in range(K_PASSES):
             for n in range(N_TILES):
-                total = totals[n]
                 nc.tensor.matmul_mx(
-                    out=total[:],
+                    out=totals[n][:],
                     lhsT=w4_codes[:, a, 2 * n * P : 2 * (n + 1) * P].bitcast(FP4X4),
                     lhsT_scale=w4_plane[:, a, :].bitcast(U8)[:, n * P : (n + 1) * P],
                     rhs=x_codes[a][:].bitcast(FP8X4),
@@ -158,139 +156,152 @@ def tile_list_regime_spread_hedge_kernel(
                     stop=False,
                 )
 
-        def response(i, b, mt, sign, dst):
-            acc = work_bank([P, PASS], "resp%d_%d_%d" % (i, b, mt))
+        def response(t, chunk, sign, dst):
+            s, mt = chunk
+            acc = work_bank([P, PASS], "resp%d_%d_%d" % (t, s, mt))
             for a in range(K_PASSES):
                 nc.tensor.matmul_mx(
                     out=acc[:],
                     lhsT=x_codes[a][:, mt * P : (mt + 1) * P].bitcast(FP8X4),
                     lhsT_scale=x_plane[a][:, mt * P : (mt + 1) * P],
-                    rhs=picked_words[i][a][:, b * PASS : (b + 1) * PASS].bitcast(FP8X4),
-                    rhs_scale=picked_scales[i][4 * a : P, b * PASS : (b + 1) * PASS],
+                    rhs=picked_words[t][a][:, s * PASS : (s + 1) * PASS].bitcast(FP8X4),
+                    rhs_scale=picked_scales[t][4 * a : P, s * PASS : (s + 1) * PASS],
                     start=(a == 0),
                     stop=(a == K_PASSES - 1),
                 )
-            nc.scalar.activation(dst[:], acc[:].rearrange("m (p i) -> m i p", i=PACK), ACT.Tanh, scale=sign)
+            nc.scalar.activation(
+                dst[:].rearrange("m i (c e) -> m c i e", e=2),
+                acc[:].rearrange("m (c e i) -> m c i e", e=2, i=PACK),
+                ACT.Tanh,
+                scale=sign,
+            )
 
-        chunks = [(b, mt) for b in range(J_PASSES) for mt in range(M_TILES)]
-        calm = {}
-        for b, mt in chunks:
-            calm[b, mt] = keep.tile([P, PACK, P], F32, name="calm%d_%d" % (b, mt))
-        h_bf = [keep.tile([P, HALF, PACK], BF16, name="h_bf%d" % k, align_bytes=64) for k in range(2)]
-        h_late = reuse.tile([P, 2, HALF, PACK], BF16, name="h_late", align_bytes=64, offset=0)
-        h_bf.extend(h_late[:, k, :, :] for k in range(2))
-        codes = reuse.tile([P, J_PASSES * M + N_TILES * J_PASSES * P], U32, name="codes", align_bytes=64, offset=4096)
-        h_codes = [codes[:, b * M : (b + 1) * M] for b in range(J_PASSES)]
+        chunks = [(s, mt) for s in range(J_PASSES) for mt in range(M_TILES)]
+        calm = [keep.tile([P, PACK, P], F32, name="calm%d_%d" % chunk) for chunk in chunks]
+
+        h_early = keep.tile([P, POOL_CHUNKS * P, PACK], BF16, name="h_early", align_bytes=64)
+        h_late = reuse.tile([P, (len(chunks) - POOL_CHUNKS) * P, PACK], BF16, name="h_late", align_bytes=64, offset=0)
+
+        def h_bf(first, many):
+            if first < POOL_CHUNKS:
+                return h_early[:, first * P : (first + many) * P, :]
+            return h_late[:, (first - POOL_CHUNKS) * P : (first - POOL_CHUNKS + many) * P, :]
+
+        codes = reuse.tile([P, J_PASSES * M + N_TILES * J_PASSES * P], U32, name="codes", align_bytes=64, offset=2 * T)
+        h_codes = [codes[:, s * M : (s + 1) * M] for s in range(J_PASSES)]
         gain_rows = keep.tile([P, J_PASSES, P, PACK], F32, name="gain_rows")
-        for b in range(J_PASSES):
-            nc.scalar.copy(gain_rows[:, b, :, :], gains[:, b : b + 1, 0:PACK].to_broadcast([P, P, PACK]))
-        h_plane = [keep.tile([P, M], U8, name="h_plane%d" % b, align_bytes=64) for b in range(J_PASSES)]
+        for s in range(J_PASSES):
+            nc.scalar.copy(gain_rows[:, s, :, :], gains[:, s : s + 1, 0:PACK].to_broadcast([P, P, PACK]))
+        h_plane = [keep.tile([P, M], U8, name="h_plane%d" % s, align_bytes=64) for s in range(J_PASSES)]
 
-        for b, mt in chunks:
-            response(0, b, mt, 1.0, calm[b, mt])
+        for c, chunk in enumerate(chunks):
+            response(0, chunk, 1.0, calm[c])
 
         stressed = {}
         size = keep.tile([P, J_PASSES, M, PACK], F32, name="size")
 
         def stress(c):
             stressed[c] = ring.tile([P, PACK, P], F32, name="stressed", bufs=len(chunks))
-            response(1, c[0], c[1], -1.0, stressed[c])
+            response(1, chunks[c], -1.0, stressed[c])
 
         def spread(c):
-            b, mt = c
-            diff = work_bank([P, PACK, P], "diff%d_%d" % c)
+            s, mt = chunks[c]
+            diff = work_bank([P, PACK, P], "diff%d_%d" % chunks[c])
             for i in range(PACK):
                 nc.tensor.matmul(diff[:, i, :], stressed[c][:, i, :], ident[:], start=True, stop=False, is_transpose=True)
                 nc.tensor.matmul(diff[:, i, :], calm[c][:, i, :], ident[:], start=False, stop=True, is_transpose=True)
-            nc.scalar.activation(size[:, b, mt * P : (mt + 1) * P, :], diff[:].rearrange("p i m -> p m i"), ACT.Abs)
+            nc.scalar.activation(size[:, s, mt * P : (mt + 1) * P, :], diff[:].rearrange("p i m -> p m i"), ACT.Abs)
 
-        def weigh(c, engine):
-            b, mt = c
-            engine.tensor_tensor(
-                h_bf[2 * b + mt // 2][:, (mt % 2) * P : (mt % 2 + 1) * P, :],
-                size[:, b, mt * P : (mt + 1) * P, :],
-                gain_rows[:, b, :, :],
-                ALU.mult,
-            )
+        def weigh(c):
+            s, mt = chunks[c]
+            engine = nc.gpsimd if c < POOL_CHUNKS else nc.vector
+            engine.tensor_tensor(h_bf(c, 1), size[:, s, mt * P : (mt + 1) * P, :], gain_rows[:, s, :, :], ALU.mult)
 
-        def quantise_h(b, half):
-            cols = slice(half * HALF, (half + 1) * HALF)
+        def quantise_h(first, many):
+            s, mt = chunks[first]
+            cols = slice(mt * P, (mt + many) * P)
             nc.vector.quantize_mx(
-                out=h_codes[b][:, cols].bitcast(FP8X4),
-                scales=h_plane[b][:, cols],
-                in_=h_bf[2 * b + half][:, :, :].rearrange("p m i -> p (m i)"),
+                out=h_codes[s][:, cols].bitcast(FP8X4),
+                scales=h_plane[s][:, cols],
+                in_=h_bf(first, many).rearrange("p m i -> p (m i)"),
             )
 
         wd_codes = codes[:, J_PASSES * M :].rearrange("p (n c) -> p n c", n=N_TILES)
         wd_plane = keep.tile([P, N_TILES, J_PASSES * P], U8, name="wd_plane", align_bytes=64)
         wd_in = keep.tile([P, N_TILES, J_PASSES, P, 2], F32, name="wd_in", align_bytes=64)
 
-        wd_bf = [keep.tile([P, J_PASSES, PASS + 32], BF16, name="wd_bf%d" % n, align_bytes=64) for n in range(N_TILES)]
+        wd_bf = [keep.tile([P, 2, S // PACK, 2], BF16, name="wd_bf%d" % n, align_bytes=64) for n in range(N_TILES)]
         for n in range(N_TILES):
-            nc.vector.tensor_copy(wd_bf[n][:, :, 0:PASS], wd_raw[n][:].indirect(offsets[:]))
+            nc.vector.tensor_copy(wd_bf[n][:].rearrange("n u c e -> n c u e"), wd_raw[n][:].indirect(offsets[:]))
 
         def turn_wd(n):
-            pairs = wd_bf[n][:].bitcast(F32)
+            pairs = wd_bf[n][:].rearrange("n u c e -> n u (c e)").bitcast(F32)
             turned = work_bank([P, J_PASSES, 2, P], "turned%d" % n)
-            for b in range(J_PASSES):
+            for s in range(J_PASSES):
                 for u in range(2):
-                    nc.tensor.transpose(turned[:, b, u, :], pairs[:, b, u : 2 * P : 2], ident[:])
-            nc.scalar.copy(wd_in[:, n, :, :, :], turned[:].rearrange("p b u n -> p b n u"))
+                    nc.tensor.transpose(turned[:, s, u, :], pairs[:, u, s * P : (s + 1) * P], ident[:])
+            nc.scalar.copy(wd_in[:, n, :, :, :], turned[:].rearrange("p s u n -> p s n u"))
 
-        def quantise_wd(pair):
-            tiles = slice(2 * pair, 2 * pair + 2)
+        def quantise_wd(first, many):
+            tiles = slice(first, first + many)
             nc.vector.quantize_mx(
                 out=wd_codes[:, tiles, :].rearrange("p n c -> p (n c)").bitcast(FP8X4),
                 scales=wd_plane[:, tiles, :].rearrange("p n c -> p (n c)"),
-                in_=wd_in[:, tiles, :, :, :].rearrange("p t b n u -> p (t b n u)").bitcast(BF16),
+                in_=wd_in[:, tiles, :, :, :].rearrange("p t s n u -> p (t s n u)").bitcast(BF16),
             )
 
-        for s in (0, 1, 2, 3):
-            stress(chunks[s])
-        for s in (0, 1):
-            spread(chunks[s])
-        for s in (4, 5):
-            stress(chunks[s])
-        for s in (2, 3):
-            spread(chunks[s])
-        turn_wd(0)
-        for s in (6, 7):
-            stress(chunks[s])
-        for s in (4, 5):
-            spread(chunks[s])
-        for n in (1, 2, 3):
+        stress(0)
+        for c in range(0, len(chunks), 2):
+            for ahead in (c + 1, c + 2):
+                if ahead < len(chunks):
+                    stress(ahead)
+            if c + 2 == len(chunks):
+                for n in range(EARLY_TILES):
+                    turn_wd(n)
+            spread(c)
+            spread(c + 1)
+        for n in range(EARLY_TILES, N_TILES):
             turn_wd(n)
-        for s in (6, 7):
-            spread(chunks[s])
 
-        for s in range(4):
-            weigh(chunks[s], nc.gpsimd)
-        quantise_h(0, 0)
-        quantise_h(0, 1)
-        weigh(chunks[4], nc.vector)
-        weigh(chunks[5], nc.vector)
-        quantise_wd(0)
-        quantise_h(1, 0)
-        quantise_wd(1)
-        weigh(chunks[6], nc.vector)
-        weigh(chunks[7], nc.vector)
-        quantise_h(1, 1)
+        for c in range(POOL_CHUNKS):
+            weigh(c)
+        quantise_h(0, M_TILES)
+        quantise_wd(0, EARLY_TILES)
+        for c in range(POOL_CHUNKS, len(chunks)):
+            weigh(c)
+            quantise_h(c - 1, 1)
+        quantise_wd(N_TILES - 2, 1)
+        quantise_h(len(chunks) - 1, 1)
+        quantise_wd(N_TILES - 1, 1)
 
-        for n in range(N_TILES):
-            total = totals[n]
-            for b in range(J_PASSES):
-                nc.tensor.matmul_mx(
-                    out=total[:],
-                    lhsT=wd_codes[:, n, b * P : (b + 1) * P].bitcast(FP8X4),
-                    lhsT_scale=wd_plane[:, n, b * P : (b + 1) * P],
-                    rhs=h_codes[b].bitcast(FP8X4),
-                    rhs_scale=h_plane[b][:],
-                    start=False,
-                    stop=(b == J_PASSES - 1),
-                )
+        def down(n, s, cols, last):
+            nc.tensor.matmul_mx(
+                out=totals[n][:, cols],
+                lhsT=wd_codes[:, n, s * P : (s + 1) * P].bitcast(FP8X4),
+                lhsT_scale=wd_plane[:, n, s * P : (s + 1) * P],
+                rhs=h_codes[s][:, cols].bitcast(FP8X4),
+                rhs_scale=h_plane[s][:, cols],
+                start=False,
+                stop=last,
+            )
+
+        def store(n):
             result = ring.tile([P, M], F32, name="result", bufs=N_TILES)
             if n % 2 == 0:
-                nc.scalar.copy(result[:], total[:])
+                nc.scalar.copy(result[:], totals[n][:])
             else:
-                nc.vector.tensor_copy(result[:], total[:])
+                nc.vector.tensor_copy(result[:], totals[n][:])
             nc.sync.dma_start(out[n * P : (n + 1) * P, :], result[:])
+
+        for n in range(EARLY_TILES):
+            down(n, 0, slice(0, M), False)
+            down(n, 1, slice(0, M - 2 * P), False)
+        for n in range(EARLY_TILES):
+            down(n, 1, slice(M - 2 * P, M - P), False)
+        for n in range(EARLY_TILES):
+            down(n, 1, slice(M - P, M), True)
+            store(n)
+        for n in range(EARLY_TILES, N_TILES):
+            down(n, 0, slice(0, M), False)
+            down(n, 1, slice(0, M), True)
+            store(n)

@@ -85,6 +85,9 @@ def tile_list_regime_spread_hedge_kernel(
         load_words(0, tab_words, 0)
         for a in range(K_PASSES):
             nc.sync.dma_start(x_raw[a][:], x[a * PASS : (a + 1) * PASS, :].rearrange("(p i) m -> p i m", i=PACK))
+        load_words(0, tab_words, 1)
+        load_words(1, tab2_words, 0)
+        load_words(1, tab2_words, 1)
         for q in range(QUADRANTS):
             nc.sync.dma_start(
                 w4_plane[32 * q : 32 * q + 4, :, :],
@@ -92,9 +95,6 @@ def tile_list_regime_spread_hedge_kernel(
             )
         nc.sync.dma_start(gains[:, :, 0:PACK], g.rearrange("(s p i) -> p s i", p=P, i=PACK))
         nc.sync.dma_start(w4_codes[:].bitcast(I32), w4_words.rearrange("a p c -> p a c").bitcast(I32))
-        load_words(0, tab_words, 1)
-        load_words(1, tab2_words, 0)
-        load_words(1, tab2_words, 1)
         for n in range(N_TILES):
             nc.sync.dma_start(wd_raw[n][:], wdT[n * P : (n + 1) * P, :])
 
@@ -143,19 +143,6 @@ def tile_list_regime_spread_hedge_kernel(
         gather_words(1, 0)
         gather_words(1, 1)
 
-        totals = [psum.tile([P, M], F32, name="total%d" % n, offset=BANK * (WORK_BANKS + n)) for n in range(N_TILES)]
-        for a in range(K_PASSES):
-            for n in range(N_TILES):
-                nc.tensor.matmul_mx(
-                    out=totals[n][:],
-                    lhsT=w4_codes[:, a, 2 * n * P : 2 * (n + 1) * P].bitcast(FP4X4),
-                    lhsT_scale=w4_plane[:, a, :].bitcast(U8)[:, n * P : (n + 1) * P],
-                    rhs=x_codes[a][:].bitcast(FP8X4),
-                    rhs_scale=x_plane[a][:],
-                    start=(a == 0),
-                    stop=False,
-                )
-
         def response(t, chunk, sign, dst):
             s, mt = chunk
             acc = work_bank([P, PASS], "resp%d_%d_%d" % (t, s, mt))
@@ -189,9 +176,6 @@ def tile_list_regime_spread_hedge_kernel(
 
         codes = reuse.tile([P, J_PASSES * M + N_TILES * J_PASSES * P], U32, name="codes", align_bytes=64, offset=2 * T)
         h_codes = [codes[:, s * M : (s + 1) * M] for s in range(J_PASSES)]
-        gain_rows = keep.tile([P, J_PASSES, P, PACK], F32, name="gain_rows")
-        for s in range(J_PASSES):
-            nc.scalar.copy(gain_rows[:, s, :, :], gains[:, s : s + 1, 0:PACK].to_broadcast([P, P, PACK]))
         h_plane = [keep.tile([P, M], U8, name="h_plane%d" % s, align_bytes=64) for s in range(J_PASSES)]
 
         for c, chunk in enumerate(chunks):
@@ -204,18 +188,35 @@ def tile_list_regime_spread_hedge_kernel(
             stressed[c] = ring.tile([P, PACK, P], F32, name="stressed", bufs=len(chunks))
             response(1, chunks[c], -1.0, stressed[c])
 
+        diffs = {}
+
+        def turn_onto_diff(c, values, opens):
+            if opens:
+                diffs[c] = psum.tile([P, PACK, P], F32, name="diff%d" % c, offset=BANK * (WORK_BANKS + c % N_TILES))
+            for i in range(PACK):
+                nc.tensor.matmul(
+                    diffs[c][:, i, :],
+                    values[:, i, :],
+                    ident[:],
+                    start=(opens and i == 0),
+                    stop=(not opens and i == PACK - 1),
+                    is_transpose=True,
+                )
+
+        for c in range(N_TILES):
+            turn_onto_diff(c, calm[c], True)
+
         def spread(c):
             s, mt = chunks[c]
-            diff = work_bank([P, PACK, P], "diff%d_%d" % chunks[c])
-            for i in range(PACK):
-                nc.tensor.matmul(diff[:, i, :], stressed[c][:, i, :], ident[:], start=True, stop=False, is_transpose=True)
-                nc.tensor.matmul(diff[:, i, :], calm[c][:, i, :], ident[:], start=False, stop=True, is_transpose=True)
-            nc.scalar.activation(size[:, s, mt * P : (mt + 1) * P, :], diff[:].rearrange("p i m -> p m i"), ACT.Abs)
+            if c >= N_TILES:
+                turn_onto_diff(c, calm[c], True)
+            turn_onto_diff(c, stressed[c], False)
+            nc.scalar.activation(size[:, s, mt * P : (mt + 1) * P, :], diffs[c][:].rearrange("p i m -> p m i"), ACT.Abs)
 
         def weigh(c):
             s, mt = chunks[c]
             engine = nc.gpsimd if c < POOL_CHUNKS else nc.vector
-            engine.tensor_tensor(h_bf(c, 1), size[:, s, mt * P : (mt + 1) * P, :], gain_rows[:, s, :, :], ALU.mult)
+            engine.tensor_tensor(h_bf(c, 1), size[:, s, mt * P : (mt + 1) * P, :], gains[:, s : s + 1, 0:PACK].to_broadcast([P, P, PACK]), ALU.mult)
 
         def quantise_h(first, many):
             s, mt = chunks[first]
@@ -250,17 +251,36 @@ def tile_list_regime_spread_hedge_kernel(
                 in_=wd_in[:, tiles, :, :, :].rearrange("p t s n u -> p (t s n u)").bitcast(BF16),
             )
 
+        totals = {}
+
+        def open_total(n):
+            totals[n] = psum.tile([P, M], F32, name="total%d" % n, offset=BANK * (WORK_BANKS + n))
+            for a in range(K_PASSES):
+                nc.tensor.matmul_mx(
+                    out=totals[n][:],
+                    lhsT=w4_codes[:, a, 2 * n * P : 2 * (n + 1) * P].bitcast(FP4X4),
+                    lhsT_scale=w4_plane[:, a, :].bitcast(U8)[:, n * P : (n + 1) * P],
+                    rhs=x_codes[a][:].bitcast(FP8X4),
+                    rhs_scale=x_plane[a][:],
+                    start=(a == 0),
+                    stop=False,
+                )
+
         stress(0)
-        for c in range(0, len(chunks), 2):
-            for ahead in (c + 1, c + 2):
-                if ahead < len(chunks):
-                    stress(ahead)
-            if c + 2 == len(chunks):
-                for n in range(EARLY_TILES):
-                    turn_wd(n)
+        last = len(chunks) - 1
+        for c in range(last - 1):
+            stress(c + 1)
+            if c == last - 2:
+                turn_wd(0)
             spread(c)
-            spread(c + 1)
+        stress(last)
+        turn_wd(1)
+        open_total(0)
+        spread(last - 1)
+        open_total(1)
+        spread(last)
         for n in range(EARLY_TILES, N_TILES):
+            open_total(n)
             turn_wd(n)
 
         for c in range(POOL_CHUNKS):

@@ -29,7 +29,7 @@ LIST_ROWS = 16
 X_COLS = M // 2
 BANK = 2048
 WORK_BANKS = 4
-POOL_CHUNKS = 5
+POOL_CHUNKS = 6
 EARLY_TILES = 2
 
 
@@ -41,6 +41,7 @@ def tile_list_regime_spread_hedge_kernel(
         keep = ctx.enter_context(tc.tile_pool(name="keep", bufs=1))
         ring = ctx.enter_context(tc.tile_pool(name="ring", bufs=1))
         psum = ctx.enter_context(tc.psum_pool(name="psum", bufs=1))
+        early = ctx.enter_context(tc.tile_pool(name="early", bufs=1))
         reuse = ctx.enter_context(tc.tile_pool(name="reuse", bufs=1))
 
         handed_out = []
@@ -88,24 +89,32 @@ def tile_list_regime_spread_hedge_kernel(
         load_words(0, tab_words, 1)
         load_words(1, tab2_words, 0)
         load_words(1, tab2_words, 1)
-        for q in range(QUADRANTS):
-            nc.sync.dma_start(
-                w4_plane[32 * q : 32 * q + 4, :, :],
-                w4_scales[:, 4 * q : 4 * q + 4, :].rearrange("a r c -> r a c").bitcast(I32),
-            )
         nc.sync.dma_start(gains[:, :, 0:PACK], g.rearrange("(s p i) -> p s i", p=P, i=PACK))
-        nc.sync.dma_start(w4_codes[:].bitcast(I32), w4_words.rearrange("a p c -> p a c").bitcast(I32))
         for n in range(N_TILES):
+            if n == N_TILES // 2:
+                for q in range(QUADRANTS):
+                    nc.sync.dma_start(
+                        w4_plane[32 * q : 32 * q + 4, :, :],
+                        w4_scales[:, 4 * q : 4 * q + 4, :].rearrange("a r c -> r a c").bitcast(I32),
+                    )
+                nc.sync.dma_start(w4_codes[:].bitcast(I32), w4_words.rearrange("a p c -> p a c").bitcast(I32))
             nc.sync.dma_start(wd_raw[n][:], wdT[n * P : (n + 1) * P, :])
 
-        picked_scales = [keep.tile([P, S], U8, name="picked_scales%d" % t, align_bytes=64) for t in range(2)]
+        calm_scales = keep.tile([P, S], U8, name="calm_scales", align_bytes=64)
+        picked_scales = [
+            [calm_scales[:, s * PASS : (s + 1) * PASS] for s in range(J_PASSES)],
+            [
+                keep.tile([P, PASS], U8, name="picked_scales1_0", align_bytes=64),
+                early.tile([P, PASS], U8, name="picked_scales1_1", align_bytes=64, offset=0),
+            ],
+        ]
         picked_words = [
             [keep.tile([P, S], U32, name="picked_words%d_%d" % (t, a), align_bytes=64) for a in range(K_PASSES)]
             for t in range(2)
         ]
 
-        def gather_scales(t):
-            nc.vector.tensor_copy(picked_scales[t][:], scale_rows[t][:].bitcast(U8).indirect(offsets[:]))
+        def gather_scales(t, lo, hi, dst):
+            nc.vector.tensor_copy(dst, scale_rows[t][:].bitcast(U8).indirect(offsets[:, lo // LIST_ROWS : hi // LIST_ROWS]))
 
         def gather_words(t, a):
             pieces = J_PASSES if a == K_PASSES - 1 else 1
@@ -119,10 +128,12 @@ def tile_list_regime_spread_hedge_kernel(
         x_codes = [keep.tile([P, M], U32, name="x_codes%d" % a, align_bytes=64) for a in range(K_PASSES)]
         x_plane = [keep.tile([P, M], U8, name="x_plane%d" % a, align_bytes=64) for a in range(K_PASSES)]
 
-        def quantise_x(a):
-            for m0 in range(0, M, X_COLS):
+        def quantise_x(a, first, many):
+            for m0 in range(first * X_COLS, (first + many) * X_COLS, X_COLS):
                 cols = slice(m0, m0 + X_COLS)
-                x_bf = ring.tile([P, X_COLS, PACK], BF16, name="x_bf", align_bytes=64, bufs=K_PASSES * M // X_COLS)
+                x_bf = early.tile(
+                    [P, X_COLS, PACK], BF16, name="x_bf%d_%d" % (a, m0), align_bytes=64, offset=2 * PACK * (a * M + m0)
+                )
                 nc.scalar.activation(
                     x_bf[:].rearrange("p (c e) i -> p c i e", e=4),
                     x_raw[a][:, :, cols].rearrange("p i (c e) -> p c i e", e=4),
@@ -134,25 +145,27 @@ def tile_list_regime_spread_hedge_kernel(
                     in_=x_bf[:].rearrange("p m i -> p (m i)"),
                 )
 
-        gather_scales(0)
         gather_words(0, 0)
-        gather_scales(1)
-        quantise_x(0)
-        quantise_x(1)
+        gather_scales(0, 0, S, calm_scales[:])
+        gather_scales(1, 0, PASS, picked_scales[1][0][:])
+        quantise_x(0, 0, 1)
+        gather_scales(1, PASS, S, picked_scales[1][1][:])
+        quantise_x(0, 1, 1)
+        quantise_x(1, 0, 1)
         gather_words(0, 1)
+        quantise_x(1, 1, 1)
         gather_words(1, 0)
         gather_words(1, 1)
 
-        def response(t, chunk, sign, dst):
+        def response(t, chunk, sign, dst, acc):
             s, mt = chunk
-            acc = work_bank([P, PASS], "resp%d_%d_%d" % (t, s, mt))
             for a in range(K_PASSES):
                 nc.tensor.matmul_mx(
                     out=acc[:],
                     lhsT=x_codes[a][:, mt * P : (mt + 1) * P].bitcast(FP8X4),
                     lhsT_scale=x_plane[a][:, mt * P : (mt + 1) * P],
                     rhs=picked_words[t][a][:, s * PASS : (s + 1) * PASS].bitcast(FP8X4),
-                    rhs_scale=picked_scales[t][4 * a : P, s * PASS : (s + 1) * PASS],
+                    rhs_scale=picked_scales[t][s][4 * a : P, :],
                     start=(a == 0),
                     stop=(a == K_PASSES - 1),
                 )
@@ -163,7 +176,7 @@ def tile_list_regime_spread_hedge_kernel(
                 scale=sign,
             )
 
-        chunks = [(s, mt) for s in range(J_PASSES) for mt in range(M_TILES)]
+        chunks = [(s, 2 * half + u) for half in range(2) for s in range(J_PASSES) for u in range(2)]
         calm = [keep.tile([P, PACK, P], F32, name="calm%d_%d" % chunk) for chunk in chunks]
 
         h_early = keep.tile([P, POOL_CHUNKS * P, PACK], BF16, name="h_early", align_bytes=64)
@@ -179,20 +192,21 @@ def tile_list_regime_spread_hedge_kernel(
         h_plane = [keep.tile([P, M], U8, name="h_plane%d" % s, align_bytes=64) for s in range(J_PASSES)]
 
         for c, chunk in enumerate(chunks):
-            response(0, chunk, 1.0, calm[c])
+            bank = (c + WORK_BANKS) % len(chunks)
+            response(0, chunk, 1.0, calm[c], psum.tile([P, PASS], F32, name="calm_sum%d" % c, offset=BANK * bank))
 
         stressed = {}
         size = keep.tile([P, J_PASSES, M, PACK], F32, name="size")
 
         def stress(c):
             stressed[c] = ring.tile([P, PACK, P], F32, name="stressed", bufs=len(chunks))
-            response(1, chunks[c], -1.0, stressed[c])
+            response(1, chunks[c], -1.0, stressed[c], work_bank([P, PASS], "stressed_sum%d" % c))
 
         diffs = {}
 
         def turn_onto_diff(c, values, opens):
             if opens:
-                diffs[c] = psum.tile([P, PACK, P], F32, name="diff%d" % c, offset=BANK * (WORK_BANKS + c % N_TILES))
+                diffs[c] = psum.tile([P, PACK, P], F32, name="diff%d" % c, offset=BANK * (WORK_BANKS + (c if c < 4 else 2 + c % 2)))
             for i in range(PACK):
                 nc.tensor.matmul(
                     diffs[c][:, i, :],
@@ -235,13 +249,13 @@ def tile_list_regime_spread_hedge_kernel(
         for n in range(N_TILES):
             nc.vector.tensor_copy(wd_bf[n][:].rearrange("n u c e -> n c u e"), wd_raw[n][:].indirect(offsets[:]))
 
-        def turn_wd(n):
+        def turn_wd(n, copy):
             pairs = wd_bf[n][:].rearrange("n u c e -> n u (c e)").bitcast(F32)
             turned = work_bank([P, J_PASSES, 2, P], "turned%d" % n)
             for s in range(J_PASSES):
                 for u in range(2):
                     nc.tensor.transpose(turned[:, s, u, :], pairs[:, u, s * P : (s + 1) * P], ident[:])
-            nc.scalar.copy(wd_in[:, n, :, :, :], turned[:].rearrange("p s u n -> p s n u"))
+            copy(wd_in[:, n, :, :, :], turned[:].rearrange("p s u n -> p s n u"))
 
         def quantise_wd(first, many):
             tiles = slice(first, first + many)
@@ -253,75 +267,81 @@ def tile_list_regime_spread_hedge_kernel(
 
         totals = {}
 
-        def open_total(n):
-            totals[n] = psum.tile([P, M], F32, name="total%d" % n, offset=BANK * (WORK_BANKS + n))
-            for a in range(K_PASSES):
+        def open_total(pair, half, tile):
+            totals[pair, half] = tile
+            for u in range(2):
+                n = 2 * pair + u
+                for v in range(2):
+                    cols = slice((2 * half + v) * P, (2 * half + v + 1) * P)
+                    for a in range(K_PASSES):
+                        nc.tensor.matmul_mx(
+                            out=tile[:, u, v * P : (v + 1) * P],
+                            lhsT=w4_codes[:, a, 2 * n * P : 2 * (n + 1) * P].bitcast(FP4X4),
+                            lhsT_scale=w4_plane[:, a, :].bitcast(U8)[:, n * P : (n + 1) * P],
+                            rhs=x_codes[a][:, cols].bitcast(FP8X4),
+                            rhs_scale=x_plane[a][:, cols],
+                            start=(u == 0 and v == 0 and a == 0),
+                            stop=False,
+                        )
+
+        def down(pair, s, mt, many, last):
+            half, v = divmod(mt, 2)
+            cols = slice(mt * P, (mt + many) * P)
+            for u in range(2):
+                n = 2 * pair + u
                 nc.tensor.matmul_mx(
-                    out=totals[n][:],
-                    lhsT=w4_codes[:, a, 2 * n * P : 2 * (n + 1) * P].bitcast(FP4X4),
-                    lhsT_scale=w4_plane[:, a, :].bitcast(U8)[:, n * P : (n + 1) * P],
-                    rhs=x_codes[a][:].bitcast(FP8X4),
-                    rhs_scale=x_plane[a][:],
-                    start=(a == 0),
-                    stop=False,
+                    out=totals[pair, half][:, u, v * P : (v + many) * P],
+                    lhsT=wd_codes[:, n, s * P : (s + 1) * P].bitcast(FP8X4),
+                    lhsT_scale=wd_plane[:, n, s * P : (s + 1) * P],
+                    rhs=h_codes[s][:, cols].bitcast(FP8X4),
+                    rhs_scale=h_plane[s][:, cols],
+                    start=False,
+                    stop=(last and u == 1),
                 )
 
-        stress(0)
+        def store(pair, half, copy):
+            result = ring.tile([P, 2, M // 2], F32, name="result", bufs=4)
+            copy(result[:], totals[pair, half][:])
+            rows = out[2 * pair * P : 2 * (pair + 1) * P, half * M // 2 : (half + 1) * M // 2]
+            nc.sync.dma_start(rows.rearrange("(u p) m -> p u m", p=P), result[:])
+
         last = len(chunks) - 1
-        for c in range(last - 1):
+        stress(0)
+        for c in range(last):
             stress(c + 1)
-            if c == last - 2:
-                turn_wd(0)
+            if c % 2 == 0 and c > 0:
+                turn_wd(c // 2 - 1, nc.scalar.copy)
             spread(c)
-        stress(last)
-        turn_wd(1)
-        open_total(0)
-        spread(last - 1)
-        open_total(1)
+            if c in (3, 4):
+                open_total(c - 3, 0, psum.tile([P, 2, M // 2], F32, name="total%d" % c, offset=BANK * (WORK_BANKS + c - 3)))
+        turn_wd(N_TILES - 1, nc.scalar.copy)
+        open_total(0, 1, work_bank([P, 2, M // 2], "total_c"))
         spread(last)
-        for n in range(EARLY_TILES, N_TILES):
-            open_total(n)
-            turn_wd(n)
+        open_total(1, 1, work_bank([P, 2, M // 2], "total_d"))
 
         for c in range(POOL_CHUNKS):
             weigh(c)
-        quantise_h(0, M_TILES)
-        quantise_wd(0, EARLY_TILES)
-        for c in range(POOL_CHUNKS, len(chunks)):
-            weigh(c)
-            quantise_h(c - 1, 1)
-        quantise_wd(N_TILES - 2, 1)
-        quantise_h(len(chunks) - 1, 1)
-        quantise_wd(N_TILES - 1, 1)
-
-        def down(n, s, cols, last):
-            nc.tensor.matmul_mx(
-                out=totals[n][:, cols],
-                lhsT=wd_codes[:, n, s * P : (s + 1) * P].bitcast(FP8X4),
-                lhsT_scale=wd_plane[:, n, s * P : (s + 1) * P],
-                rhs=h_codes[s][:, cols].bitcast(FP8X4),
-                rhs_scale=h_plane[s][:, cols],
-                start=False,
-                stop=last,
-            )
-
-        def store(n):
-            result = ring.tile([P, M], F32, name="result", bufs=N_TILES)
-            if n % 2 == 0:
-                nc.scalar.copy(result[:], totals[n][:])
-            else:
-                nc.vector.tensor_copy(result[:], totals[n][:])
-            nc.sync.dma_start(out[n * P : (n + 1) * P, :], result[:])
-
-        for n in range(EARLY_TILES):
-            down(n, 0, slice(0, M), False)
-            down(n, 1, slice(0, M - 2 * P), False)
-        for n in range(EARLY_TILES):
-            down(n, 1, slice(M - 2 * P, M - P), False)
-        for n in range(EARLY_TILES):
-            down(n, 1, slice(M - P, M), True)
-            store(n)
-        for n in range(EARLY_TILES, N_TILES):
-            down(n, 0, slice(0, M), False)
-            down(n, 1, slice(0, M), True)
-            store(n)
+        quantise_h(0, 2)
+        quantise_h(2, 2)
+        quantise_wd(0, 2)
+        down(0, 0, 0, 2, False)
+        down(0, 1, 0, 2, True)
+        quantise_h(4, 2)
+        store(0, 0, nc.vector.tensor_copy)
+        quantise_wd(2, 1)
+        weigh(6)
+        quantise_wd(3, 1)
+        quantise_h(6, 1)
+        down(1, 0, 0, 2, False)
+        down(1, 1, 0, 2, True)
+        for pair in range(2):
+            down(pair, 0, 2, 2, False)
+        weigh(7)
+        store(1, 0, nc.scalar.copy)
+        for pair in range(2):
+            down(pair, 1, 2, 1, False)
+        quantise_h(7, 1)
+        for pair in range(2):
+            down(pair, 1, 3, 1, True)
+        store(0, 1, nc.scalar.copy)
+        store(1, 1, nc.vector.tensor_copy)

@@ -91,14 +91,13 @@ def tile_list_regime_spread_hedge_kernel(
         load_words(1, tab2_words, 1)
         nc.sync.dma_start(gains[:, :, 0:PACK], g.rearrange("(s p i) -> p s i", p=P, i=PACK))
         for n in range(N_TILES):
-            if n == N_TILES // 2:
-                for q in range(QUADRANTS):
-                    nc.sync.dma_start(
-                        w4_plane[32 * q : 32 * q + 4, :, :],
-                        w4_scales[:, 4 * q : 4 * q + 4, :].rearrange("a r c -> r a c").bitcast(I32),
-                    )
-                nc.sync.dma_start(w4_codes[:].bitcast(I32), w4_words.rearrange("a p c -> p a c").bitcast(I32))
             nc.sync.dma_start(wd_raw[n][:], wdT[n * P : (n + 1) * P, :])
+        for q in range(QUADRANTS):
+            nc.sync.dma_start(
+                w4_plane[32 * q : 32 * q + 4, :, :],
+                w4_scales[:, 4 * q : 4 * q + 4, :].rearrange("a r c -> r a c").bitcast(I32),
+            )
+        nc.sync.dma_start(w4_codes[:].bitcast(I32), w4_words.rearrange("a p c -> p a c").bitcast(I32))
 
         calm_scales = keep.tile([P, S], U8, name="calm_scales", align_bytes=64)
         picked_scales = [
@@ -315,8 +314,8 @@ def tile_list_regime_spread_hedge_kernel(
             if c in (3, 4):
                 open_total(c - 3, 0, psum.tile([P, 2, M // 2], F32, name="total%d" % c, offset=BANK * (WORK_BANKS + c - 3)))
         turn_wd(N_TILES - 1, nc.scalar.copy)
-        open_total(0, 1, work_bank([P, 2, M // 2], "total_c"))
         spread(last)
+        open_total(0, 1, work_bank([P, 2, M // 2], "total_c"))
         open_total(1, 1, work_bank([P, 2, M // 2], "total_d"))
 
         for c in range(POOL_CHUNKS):
@@ -327,7 +326,7 @@ def tile_list_regime_spread_hedge_kernel(
         down(0, 0, 0, 2, False)
         down(0, 1, 0, 2, True)
         quantise_h(4, 2)
-        store(0, 0, nc.vector.tensor_copy)
+        store(0, 0, nc.scalar.copy)
         quantise_wd(2, 1)
         weigh(6)
         quantise_wd(3, 1)

@@ -44,12 +44,13 @@ def tile_list_regime_spread_hedge_kernel(
         early = ctx.enter_context(tc.tile_pool(name="early", bufs=1))
         reuse = ctx.enter_context(tc.tile_pool(name="reuse", bufs=1))
 
-        handed_out = []
-
-        def work_bank(shape, name):
-            bank = len(handed_out) % WORK_BANKS
-            handed_out.append(name)
+        def bank_tile(shape, name, bank):
             return psum.tile(shape, F32, name=name, offset=BANK * bank)
+
+        STRESS_BANK = (0, 1, 2, 3, 2, 3, 4, 5)
+        DIFF_BANK = (0, 1, 4, 5, 6, 7, 0, 1)
+        TURN_BANK = (2, 3, 4, 5)
+        TOTAL_BANK = (6, 7, 2, 3)
 
         offsets = keep.tile([P, S // LIST_ROWS], U16, name="offsets")
         nc.sync.dma_start(offsets[:], offs)
@@ -67,7 +68,11 @@ def tile_list_regime_spread_hedge_kernel(
             [keep.tile([P, T], U32, name="words%d_%d" % (t, a), align_bytes=64) for a in range(K_PASSES)]
             for t in range(2)
         ]
-        x_raw = [keep.tile([P, PACK, M], F32, name="x_raw%d" % a) for a in range(K_PASSES)]
+        x_first = keep.tile([P, PACK, M], F32, name="x_first")
+        x_raw = [
+            [x_first[:, :, half * X_COLS : (half + 1) * X_COLS] for half in range(2)],
+            [keep.tile([P, PACK, X_COLS], F32, name="x_second%d" % half)[:] for half in range(2)],
+        ]
         wd_raw = [keep.tile([P, T], F32, name="wd_raw%d" % n, align_bytes=64) for n in range(N_TILES - 1)]
         wd_raw.append(reuse.tile([P, T], F32, name="wd_raw_last", align_bytes=64, offset=0))
         gains = keep.tile([P, J_PASSES, 2 * PACK], F32, name="gains")
@@ -84,9 +89,10 @@ def tile_list_regime_spread_hedge_kernel(
         load_scale_rows(0, tab_scales)
         load_scale_rows(1, tab2_scales)
         load_words(0, tab_words, 0)
-        for a in range(K_PASSES):
-            nc.sync.dma_start(x_raw[a][:], x[a * PASS : (a + 1) * PASS, :].rearrange("(p i) m -> p i m", i=PACK))
+        nc.sync.dma_start(x_first[:], x[0:PASS, :].rearrange("(p i) m -> p i m", i=PACK))
+        nc.sync.dma_start(x_raw[1][0], x[PASS:K, 0:X_COLS].rearrange("(p i) m -> p i m", i=PACK))
         load_words(0, tab_words, 1)
+        nc.sync.dma_start(x_raw[1][1], x[PASS:K, X_COLS:M].rearrange("(p i) m -> p i m", i=PACK))
         load_words(1, tab2_words, 0)
         load_words(1, tab2_words, 1)
         nc.sync.dma_start(gains[:, :, 0:PACK], g.rearrange("(s p i) -> p s i", p=P, i=PACK))
@@ -104,11 +110,10 @@ def tile_list_regime_spread_hedge_kernel(
             [calm_scales[:, s * PASS : (s + 1) * PASS] for s in range(J_PASSES)],
             [
                 keep.tile([P, PASS], U8, name="picked_scales1_0", align_bytes=64),
-                early.tile([P, PASS], U8, name="picked_scales1_1", align_bytes=64, offset=0),
             ],
         ]
         picked_words = [
-            [keep.tile([P, S], U32, name="picked_words%d_%d" % (t, a), align_bytes=64) for a in range(K_PASSES)]
+            [keep.tile([P, S], U32, name="picked_words%d_%d" % (t, a), align_bytes=64) if (t, a) != (0, 1) else None for a in range(K_PASSES)]
             for t in range(2)
         ]
 
@@ -135,7 +140,7 @@ def tile_list_regime_spread_hedge_kernel(
                 )
                 nc.scalar.activation(
                     x_bf[:].rearrange("p (c e) i -> p c i e", e=4),
-                    x_raw[a][:, :, cols].rearrange("p i (c e) -> p c i e", e=4),
+                    x_raw[a][m0 // X_COLS].rearrange("p i (c e) -> p c i e", e=4),
                     ACT.Copy,
                 )
                 nc.vector.quantize_mx(
@@ -148,9 +153,11 @@ def tile_list_regime_spread_hedge_kernel(
         gather_scales(0, 0, S, calm_scales[:])
         gather_scales(1, 0, PASS, picked_scales[1][0][:])
         quantise_x(0, 0, 1)
+        picked_scales[1].append(early.tile([P, PASS], U8, name="picked_scales1_1", align_bytes=64, offset=0))
         gather_scales(1, PASS, S, picked_scales[1][1][:])
         quantise_x(0, 1, 1)
         quantise_x(1, 0, 1)
+        picked_words[0][1] = early.tile([P, S], U32, name="picked_second", align_bytes=64, offset=2 * PACK * X_COLS)
         gather_words(0, 1)
         quantise_x(1, 1, 1)
         gather_words(1, 0)
@@ -199,31 +206,38 @@ def tile_list_regime_spread_hedge_kernel(
 
         def stress(c):
             stressed[c] = ring.tile([P, PACK, P], F32, name="stressed", bufs=len(chunks))
-            response(1, chunks[c], -1.0, stressed[c], work_bank([P, PASS], "stressed_sum%d" % c))
+            response(1, chunks[c], -1.0, stressed[c], bank_tile([P, PASS], "stressed_sum%d" % c, STRESS_BANK[c]))
 
         diffs = {}
 
-        def turn_onto_diff(c, values, opens):
+        def turn_onto_diff(c, values, opens, closes):
             if opens:
-                diffs[c] = psum.tile([P, PACK, P], F32, name="diff%d" % c, offset=BANK * (WORK_BANKS + (c if c < 4 else 2 + c % 2)))
+                diffs[c] = bank_tile([P, PACK, P], "diff%d" % c, DIFF_BANK[c])
             for i in range(PACK):
                 nc.tensor.matmul(
                     diffs[c][:, i, :],
                     values[:, i, :],
                     ident[:],
                     start=(opens and i == 0),
-                    stop=(not opens and i == PACK - 1),
+                    stop=(closes and i == PACK - 1),
                     is_transpose=True,
                 )
 
-        for c in range(N_TILES):
-            turn_onto_diff(c, calm[c], True)
+        for c in range(2, 6):
+            turn_onto_diff(c, calm[c], True, False)
+
+        added = {}
+
+        def add(c):
+            added[c] = keep.tile([P, PACK, P], F32, name="added%d" % c)
+            nc.gpsimd.tensor_tensor(added[c][:], calm[c][:], stressed[c][:], ALU.add)
 
         def spread(c):
             s, mt = chunks[c]
-            if c >= N_TILES:
-                turn_onto_diff(c, calm[c], True)
-            turn_onto_diff(c, stressed[c], False)
+            if c in added:
+                turn_onto_diff(c, added[c], True, True)
+            else:
+                turn_onto_diff(c, stressed[c], False, True)
             nc.scalar.activation(size[:, s, mt * P : (mt + 1) * P, :], diffs[c][:].rearrange("p i m -> p m i"), ACT.Abs)
 
         def weigh(c):
@@ -250,7 +264,7 @@ def tile_list_regime_spread_hedge_kernel(
 
         def turn_wd(n, copy):
             pairs = wd_bf[n][:].rearrange("n u c e -> n u (c e)").bitcast(F32)
-            turned = work_bank([P, J_PASSES, 2, P], "turned%d" % n)
+            turned = bank_tile([P, J_PASSES, 2, P], "turned%d" % n, TURN_BANK[n])
             for s in range(J_PASSES):
                 for u in range(2):
                     nc.tensor.transpose(turned[:, s, u, :], pairs[:, u, s * P : (s + 1) * P], ident[:])
@@ -304,22 +318,42 @@ def tile_list_regime_spread_hedge_kernel(
             rows = out[2 * pair * P : 2 * (pair + 1) * P, half * M // 2 : (half + 1) * M // 2]
             nc.sync.dma_start(rows.rearrange("(u p) m -> p u m", p=P), result[:])
 
-        last = len(chunks) - 1
-        stress(0)
-        for c in range(last):
-            stress(c + 1)
-            if c % 2 == 0 and c > 0:
-                turn_wd(c // 2 - 1, nc.scalar.copy)
-            spread(c)
-            if c in (3, 4):
-                open_total(c - 3, 0, psum.tile([P, 2, M // 2], F32, name="total%d" % c, offset=BANK * (WORK_BANKS + c - 3)))
-        turn_wd(N_TILES - 1, nc.scalar.copy)
-        spread(last)
-        open_total(0, 1, work_bank([P, 2, M // 2], "total_c"))
-        open_total(1, 1, work_bank([P, 2, M // 2], "total_d"))
+        def open_half(half):
+            for pair in range(2):
+                k = 2 * half + pair
+                open_total(pair, half, bank_tile([P, 2, M // 2], "total%d" % k, TOTAL_BANK[k]))
 
-        for c in range(POOL_CHUNKS):
+        stress(0)
+        stress(1)
+        add(0)
+        stress(2)
+        add(1)
+        stress(3)
+        for c in (2, 0):
+            spread(c)
             weigh(c)
+        stress(4)
+        for c in (3, 1):
+            spread(c)
+            weigh(c)
+        stress(5)
+        turn_onto_diff(6, calm[6], True, False)
+        stress(6)
+        spread(4)
+        weigh(4)
+        turn_wd(0, nc.scalar.copy)
+        turn_onto_diff(7, calm[7], True, False)
+        stress(7)
+        spread(5)
+        weigh(5)
+        turn_wd(1, nc.scalar.copy)
+        open_half(0)
+        spread(6)
+        turn_wd(2, nc.scalar.copy)
+        turn_wd(3, nc.scalar.copy)
+        spread(7)
+        open_half(1)
+
         quantise_h(0, 2)
         quantise_h(2, 2)
         quantise_wd(0, 2)

@@ -44,13 +44,12 @@ def tile_list_regime_spread_hedge_kernel(
         early = ctx.enter_context(tc.tile_pool(name="early", bufs=1))
         reuse = ctx.enter_context(tc.tile_pool(name="reuse", bufs=1))
 
-        def bank_tile(shape, name, bank):
-            return psum.tile(shape, F32, name=name, offset=BANK * bank)
+        handed_out = []
 
-        STRESS_BANK = (0, 1, 2, 3, 2, 3, 4, 5)
-        DIFF_BANK = (0, 1, 4, 5, 6, 7, 0, 1)
-        TURN_BANK = (2, 3, 4, 5)
-        TOTAL_BANK = (6, 7, 2, 3)
+        def work_bank(shape, name):
+            bank = len(handed_out) % WORK_BANKS
+            handed_out.append(name)
+            return psum.tile(shape, F32, name=name, offset=BANK * bank)
 
         offsets = keep.tile([P, S // LIST_ROWS], U16, name="offsets")
         nc.sync.dma_start(offsets[:], offs)
@@ -156,10 +155,17 @@ def tile_list_regime_spread_hedge_kernel(
         picked_scales[1].append(early.tile([P, PASS], U8, name="picked_scales1_1", align_bytes=64, offset=0))
         gather_scales(1, PASS, S, picked_scales[1][1][:])
         quantise_x(0, 1, 1)
-        quantise_x(1, 0, 1)
-        picked_words[0][1] = early.tile([P, S], U32, name="picked_second", align_bytes=64, offset=2 * PACK * X_COLS)
-        gather_words(0, 1)
-        quantise_x(1, 1, 1)
+        second = []
+        for s in range(J_PASSES):
+            second.append(early.tile([P, PASS], U32, name="second%d" % s, align_bytes=64, offset=2 * PACK * X_COLS * (s + 1)))
+            nc.vector.tensor_copy(second[s][:], words[0][1][:].indirect(offsets[:, s * PASS // LIST_ROWS : (s + 1) * PASS // LIST_ROWS]))
+            quantise_x(1, s, 1)
+
+        def picked(t, a, s):
+            if (t, a) == (0, 1):
+                return second[s][:]
+            return picked_words[t][a][:, s * PASS : (s + 1) * PASS]
+
         gather_words(1, 0)
         gather_words(1, 1)
 
@@ -170,7 +176,7 @@ def tile_list_regime_spread_hedge_kernel(
                     out=acc[:],
                     lhsT=x_codes[a][:, mt * P : (mt + 1) * P].bitcast(FP8X4),
                     lhsT_scale=x_plane[a][:, mt * P : (mt + 1) * P],
-                    rhs=picked_words[t][a][:, s * PASS : (s + 1) * PASS].bitcast(FP8X4),
+                    rhs=picked(t, a, s).bitcast(FP8X4),
                     rhs_scale=picked_scales[t][s][4 * a : P, :],
                     start=(a == 0),
                     stop=(a == K_PASSES - 1),
@@ -194,8 +200,8 @@ def tile_list_regime_spread_hedge_kernel(
             return h_late[:, (first - POOL_CHUNKS) * P : (first - POOL_CHUNKS + many) * P, :]
 
         codes = reuse.tile([P, J_PASSES * M + N_TILES * J_PASSES * P], U32, name="codes", align_bytes=64, offset=2 * T)
-        h_codes = [codes[:, s * M : (s + 1) * M] for s in range(J_PASSES)]
-        h_plane = [keep.tile([P, M], U8, name="h_plane%d" % s, align_bytes=64) for s in range(J_PASSES)]
+        h_codes = codes[:, 0 : J_PASSES * M]
+        h_plane = keep.tile([P, J_PASSES * M], U8, name="h_plane", align_bytes=64)
 
         for c, chunk in enumerate(chunks):
             bank = (c + WORK_BANKS) % len(chunks)
@@ -206,38 +212,31 @@ def tile_list_regime_spread_hedge_kernel(
 
         def stress(c):
             stressed[c] = ring.tile([P, PACK, P], F32, name="stressed", bufs=len(chunks))
-            response(1, chunks[c], -1.0, stressed[c], bank_tile([P, PASS], "stressed_sum%d" % c, STRESS_BANK[c]))
+            response(1, chunks[c], -1.0, stressed[c], work_bank([P, PASS], "stressed_sum%d" % c))
 
         diffs = {}
 
-        def turn_onto_diff(c, values, opens, closes):
+        def turn_onto_diff(c, values, opens):
             if opens:
-                diffs[c] = bank_tile([P, PACK, P], "diff%d" % c, DIFF_BANK[c])
+                diffs[c] = psum.tile([P, PACK, P], F32, name="diff%d" % c, offset=BANK * (WORK_BANKS + (c if c < 4 else 2 + c % 2)))
             for i in range(PACK):
                 nc.tensor.matmul(
                     diffs[c][:, i, :],
                     values[:, i, :],
                     ident[:],
                     start=(opens and i == 0),
-                    stop=(closes and i == PACK - 1),
+                    stop=(not opens and i == PACK - 1),
                     is_transpose=True,
                 )
 
-        for c in range(2, 6):
-            turn_onto_diff(c, calm[c], True, False)
-
-        added = {}
-
-        def add(c):
-            added[c] = keep.tile([P, PACK, P], F32, name="added%d" % c)
-            nc.gpsimd.tensor_tensor(added[c][:], calm[c][:], stressed[c][:], ALU.add)
+        for c in range(N_TILES):
+            turn_onto_diff(c, calm[c], True)
 
         def spread(c):
             s, mt = chunks[c]
-            if c in added:
-                turn_onto_diff(c, added[c], True, True)
-            else:
-                turn_onto_diff(c, stressed[c], False, True)
+            if c >= N_TILES:
+                turn_onto_diff(c, calm[c], True)
+            turn_onto_diff(c, stressed[c], False)
             nc.scalar.activation(size[:, s, mt * P : (mt + 1) * P, :], diffs[c][:].rearrange("p i m -> p m i"), ACT.Abs)
 
         def weigh(c):
@@ -246,17 +245,23 @@ def tile_list_regime_spread_hedge_kernel(
             engine.tensor_tensor(h_bf(c, 1), size[:, s, mt * P : (mt + 1) * P, :], gains[:, s : s + 1, 0:PACK].to_broadcast([P, P, PACK]), ALU.mult)
 
         def quantise_h(first, many):
-            s, mt = chunks[first]
-            cols = slice(mt * P, (mt + many) * P)
+            cols = slice(first * P, (first + many) * P)
             nc.vector.quantize_mx(
-                out=h_codes[s][:, cols].bitcast(FP8X4),
-                scales=h_plane[s][:, cols],
+                out=h_codes[:, cols].bitcast(FP8X4),
+                scales=h_plane[:, cols],
                 in_=h_bf(first, many).rearrange("p m i -> p (m i)"),
             )
 
         wd_codes = codes[:, J_PASSES * M :].rearrange("p (n c) -> p n c", n=N_TILES)
         wd_plane = keep.tile([P, N_TILES, J_PASSES * P], U8, name="wd_plane", align_bytes=64)
-        wd_in = keep.tile([P, N_TILES, J_PASSES, P, 2], F32, name="wd_in", align_bytes=64)
+        wd_pair = keep.tile([P, 2, J_PASSES, P, 2], F32, name="wd_pair", align_bytes=64)
+        wd_third = reuse.tile([P, 1, J_PASSES, P, 2], F32, name="wd_third", align_bytes=64, offset=T)
+        wd_fourth = keep.tile([P, 1, J_PASSES, P, 2], F32, name="wd_fourth", align_bytes=64)
+
+        def wd_in(first, many):
+            if first < 2:
+                return wd_pair[:, first : first + many, :, :, :]
+            return (wd_third, wd_fourth)[first - 2][:]
 
         wd_bf = [keep.tile([P, 2, S // PACK, 2], BF16, name="wd_bf%d" % n, align_bytes=64) for n in range(N_TILES)]
         for n in range(N_TILES):
@@ -264,18 +269,18 @@ def tile_list_regime_spread_hedge_kernel(
 
         def turn_wd(n, copy):
             pairs = wd_bf[n][:].rearrange("n u c e -> n u (c e)").bitcast(F32)
-            turned = bank_tile([P, J_PASSES, 2, P], "turned%d" % n, TURN_BANK[n])
+            turned = work_bank([P, J_PASSES, 2, P], "turned%d" % n)
             for s in range(J_PASSES):
                 for u in range(2):
                     nc.tensor.transpose(turned[:, s, u, :], pairs[:, u, s * P : (s + 1) * P], ident[:])
-            copy(wd_in[:, n, :, :, :], turned[:].rearrange("p s u n -> p s n u"))
+            copy(wd_in(n, 1)[:, 0, :, :, :], turned[:].rearrange("p s u n -> p s n u"))
 
         def quantise_wd(first, many):
             tiles = slice(first, first + many)
             nc.vector.quantize_mx(
                 out=wd_codes[:, tiles, :].rearrange("p n c -> p (n c)").bitcast(FP8X4),
                 scales=wd_plane[:, tiles, :].rearrange("p n c -> p (n c)"),
-                in_=wd_in[:, tiles, :, :, :].rearrange("p t s n u -> p (t s n u)").bitcast(BF16),
+                in_=wd_in(first, many).rearrange("p t s n u -> p (t s n u)").bitcast(BF16),
             )
 
         totals = {}
@@ -299,15 +304,16 @@ def tile_list_regime_spread_hedge_kernel(
 
         def down(pair, s, mt, many, last):
             half, v = divmod(mt, 2)
-            cols = slice(mt * P, (mt + many) * P)
+            first = chunks.index((s, mt))
+            cols = slice(first * P, (first + many) * P)
             for u in range(2):
                 n = 2 * pair + u
                 nc.tensor.matmul_mx(
                     out=totals[pair, half][:, u, v * P : (v + many) * P],
                     lhsT=wd_codes[:, n, s * P : (s + 1) * P].bitcast(FP8X4),
                     lhsT_scale=wd_plane[:, n, s * P : (s + 1) * P],
-                    rhs=h_codes[s][:, cols].bitcast(FP8X4),
-                    rhs_scale=h_plane[s][:, cols],
+                    rhs=h_codes[:, cols].bitcast(FP8X4),
+                    rhs_scale=h_plane[:, cols],
                     start=False,
                     stop=(last and u == 1),
                 )
@@ -318,44 +324,23 @@ def tile_list_regime_spread_hedge_kernel(
             rows = out[2 * pair * P : 2 * (pair + 1) * P, half * M // 2 : (half + 1) * M // 2]
             nc.sync.dma_start(rows.rearrange("(u p) m -> p u m", p=P), result[:])
 
-        def open_half(half):
-            for pair in range(2):
-                k = 2 * half + pair
-                open_total(pair, half, bank_tile([P, 2, M // 2], "total%d" % k, TOTAL_BANK[k]))
-
+        last = len(chunks) - 1
         stress(0)
-        stress(1)
-        add(0)
-        stress(2)
-        add(1)
-        stress(3)
-        for c in (2, 0):
+        for c in range(last):
+            stress(c + 1)
+            if c % 2 == 0 and c > 0:
+                turn_wd(c // 2 - 1, nc.vector.tensor_copy if c == 6 else nc.scalar.copy)
             spread(c)
-            weigh(c)
-        stress(4)
-        for c in (3, 1):
-            spread(c)
-            weigh(c)
-        stress(5)
-        turn_onto_diff(6, calm[6], True, False)
-        stress(6)
-        spread(4)
-        weigh(4)
-        turn_wd(0, nc.scalar.copy)
-        turn_onto_diff(7, calm[7], True, False)
-        stress(7)
-        spread(5)
-        weigh(5)
-        turn_wd(1, nc.scalar.copy)
-        open_half(0)
-        spread(6)
-        turn_wd(2, nc.scalar.copy)
-        turn_wd(3, nc.scalar.copy)
-        spread(7)
-        open_half(1)
+            if c in (3, 4):
+                open_total(c - 3, 0, psum.tile([P, 2, M // 2], F32, name="total%d" % c, offset=BANK * (WORK_BANKS + c - 3)))
+        turn_wd(N_TILES - 1, nc.scalar.copy)
+        spread(last)
+        open_total(0, 1, work_bank([P, 2, M // 2], "total_c"))
+        open_total(1, 1, work_bank([P, 2, M // 2], "total_d"))
 
-        quantise_h(0, 2)
-        quantise_h(2, 2)
+        for c in range(POOL_CHUNKS):
+            weigh(c)
+        quantise_h(0, 4)
         quantise_wd(0, 2)
         down(0, 0, 0, 2, False)
         down(0, 1, 0, 2, True)

@@ -29,6 +29,8 @@ LIST_ROWS = 16
 X_COLS = M // 2
 BANK = 2048
 WORK_BANKS = 4
+SUM_BANKS = (4, 5, 6, 7)
+DIFF_BANKS = (0, 1, 2, 3)
 POOL_CHUNKS = 6
 EARLY_TILES = 2
 
@@ -112,7 +114,7 @@ def tile_list_regime_spread_hedge_kernel(
             ],
         ]
         picked_words = [
-            [keep.tile([P, S], U32, name="picked_words%d_%d" % (t, a), align_bytes=64) if (t, a) != (0, 1) else None for a in range(K_PASSES)]
+            [keep.tile([P, S], U32, name="picked_words%d_%d" % (t, a), align_bytes=64) if a == 0 else None for a in range(K_PASSES)]
             for t in range(2)
         ]
 
@@ -162,24 +164,26 @@ def tile_list_regime_spread_hedge_kernel(
             quantise_x(1, s, 1)
 
         def picked(t, a, s):
-            if (t, a) == (0, 1):
-                return second[s][:]
+            if a == 1:
+                return (second, closing)[t][s][:]
             return picked_words[t][a][:, s * PASS : (s + 1) * PASS]
 
         gather_words(1, 0)
-        gather_words(1, 1)
+        closing = [keep.tile([P, PASS], U32, name="closing%d" % s, align_bytes=64) for s in range(J_PASSES)]
+        for s in range(J_PASSES):
+            nc.vector.tensor_copy(closing[s][:], words[1][1][:].indirect(offsets[:, s * PASS // LIST_ROWS : (s + 1) * PASS // LIST_ROWS]))
 
-        def response(t, chunk, sign, dst, acc):
+        def response(t, chunk, sign, dst, acc, passes=(0, 1)):
             s, mt = chunk
-            for a in range(K_PASSES):
+            for a in passes:
                 nc.tensor.matmul_mx(
                     out=acc[:],
                     lhsT=x_codes[a][:, mt * P : (mt + 1) * P].bitcast(FP8X4),
                     lhsT_scale=x_plane[a][:, mt * P : (mt + 1) * P],
                     rhs=picked(t, a, s).bitcast(FP8X4),
                     rhs_scale=picked_scales[t][s][4 * a : P, :],
-                    start=(a == 0),
-                    stop=(a == K_PASSES - 1),
+                    start=(a == passes[0]),
+                    stop=(a == passes[-1]),
                 )
             nc.scalar.activation(
                 dst[:].rearrange("m i (c e) -> m c i e", e=2),
@@ -189,36 +193,31 @@ def tile_list_regime_spread_hedge_kernel(
             )
 
         chunks = [(s, 2 * half + u) for half in range(2) for s in range(J_PASSES) for u in range(2)]
-        calm = [keep.tile([P, PACK, P], F32, name="calm%d_%d" % chunk) for chunk in chunks]
+        calm = {chunk: keep.tile([P, PACK, P], F32, name="calm%d_%d" % chunk) for chunk in chunks}
 
-        h_early = keep.tile([P, POOL_CHUNKS * P, PACK], BF16, name="h_early", align_bytes=64)
-        h_late = reuse.tile([P, (len(chunks) - POOL_CHUNKS) * P, PACK], BF16, name="h_late", align_bytes=64, offset=0)
+        def bank_tile(shape, name, bank):
+            return psum.tile(shape, F32, name=name, offset=BANK * bank)
 
-        def h_bf(first, many):
-            if first < POOL_CHUNKS:
-                return h_early[:, first * P : (first + many) * P, :]
-            return h_late[:, (first - POOL_CHUNKS) * P : (first - POOL_CHUNKS + many) * P, :]
-
-        codes = reuse.tile([P, J_PASSES * M + N_TILES * J_PASSES * P], U32, name="codes", align_bytes=64, offset=2 * T)
+        h_bf = keep.tile([P, len(chunks) * P, PACK], BF16, name="h_bf", align_bytes=64)
+        codes = reuse.tile([P, J_PASSES * M + N_TILES * J_PASSES * P], U32, name="codes", align_bytes=64, offset=0)
         h_codes = codes[:, 0 : J_PASSES * M]
         h_plane = keep.tile([P, J_PASSES * M], U8, name="h_plane", align_bytes=64)
 
         for c, chunk in enumerate(chunks):
-            bank = (c + WORK_BANKS) % len(chunks)
-            response(0, chunk, 1.0, calm[c], psum.tile([P, PASS], F32, name="calm_sum%d" % c, offset=BANK * bank))
+            response(0, chunk, 1.0, calm[chunk], bank_tile([P, PASS], "calm_sum%d" % c, c))
 
         stressed = {}
         size = keep.tile([P, J_PASSES, M, PACK], F32, name="size")
 
         def stress(c):
-            stressed[c] = ring.tile([P, PACK, P], F32, name="stressed", bufs=len(chunks))
-            response(1, chunks[c], -1.0, stressed[c], work_bank([P, PASS], "stressed_sum%d" % c))
+            stressed[c] = ring.tile([P, PACK, P], F32, name="stressed", bufs=2)
+            response(1, chunks[c], -1.0, stressed[c], bank_tile([P, PASS], "stressed_sum%d" % c, SUM_BANKS[c % WORK_BANKS]))
 
         diffs = {}
 
         def turn_onto_diff(c, values, opens):
             if opens:
-                diffs[c] = psum.tile([P, PACK, P], F32, name="diff%d" % c, offset=BANK * (WORK_BANKS + (c if c < 4 else 2 + c % 2)))
+                diffs[c] = bank_tile([P, PACK, P], "diff%d" % c, DIFF_BANKS[c % WORK_BANKS])
             for i in range(PACK):
                 nc.tensor.matmul(
                     diffs[c][:, i, :],
@@ -229,58 +228,56 @@ def tile_list_regime_spread_hedge_kernel(
                     is_transpose=True,
                 )
 
-        for c in range(N_TILES):
-            turn_onto_diff(c, calm[c], True)
+        for c in range(WORK_BANKS):
+            turn_onto_diff(c, calm[chunks[c]], True)
 
         def spread(c):
             s, mt = chunks[c]
-            if c >= N_TILES:
-                turn_onto_diff(c, calm[c], True)
+            if c >= WORK_BANKS:
+                turn_onto_diff(c, calm[chunks[c]], True)
             turn_onto_diff(c, stressed[c], False)
             nc.scalar.activation(size[:, s, mt * P : (mt + 1) * P, :], diffs[c][:].rearrange("p i m -> p m i"), ACT.Abs)
 
         def weigh(c):
             s, mt = chunks[c]
             engine = nc.gpsimd if c < POOL_CHUNKS else nc.vector
-            engine.tensor_tensor(h_bf(c, 1), size[:, s, mt * P : (mt + 1) * P, :], gains[:, s : s + 1, 0:PACK].to_broadcast([P, P, PACK]), ALU.mult)
+            cols = slice(mt * P, (mt + 1) * P)
+            engine.tensor_tensor(h_bf[:, c * P : (c + 1) * P, :], size[:, s, cols, :], gains[:, s : s + 1, 0:PACK].to_broadcast([P, P, PACK]), ALU.mult)
 
         def quantise_h(first, many):
             cols = slice(first * P, (first + many) * P)
             nc.vector.quantize_mx(
                 out=h_codes[:, cols].bitcast(FP8X4),
                 scales=h_plane[:, cols],
-                in_=h_bf(first, many).rearrange("p m i -> p (m i)"),
+                in_=h_bf[:, cols, :].rearrange("p m i -> p (m i)"),
             )
 
         wd_codes = codes[:, J_PASSES * M :].rearrange("p (n c) -> p n c", n=N_TILES)
         wd_plane = keep.tile([P, N_TILES, J_PASSES * P], U8, name="wd_plane", align_bytes=64)
-        wd_pair = keep.tile([P, 2, J_PASSES, P, 2], F32, name="wd_pair", align_bytes=64)
-        wd_third = reuse.tile([P, 1, J_PASSES, P, 2], F32, name="wd_third", align_bytes=64, offset=T)
-        wd_fourth = keep.tile([P, 1, J_PASSES, P, 2], F32, name="wd_fourth", align_bytes=64)
-
-        def wd_in(first, many):
-            if first < 2:
-                return wd_pair[:, first : first + many, :, :, :]
-            return (wd_third, wd_fourth)[first - 2][:]
+        wd_in = keep.tile([P, N_TILES, J_PASSES, P, 2], F32, name="wd_in", align_bytes=64)
 
         wd_bf = [keep.tile([P, 2, S // PACK, 2], BF16, name="wd_bf%d" % n, align_bytes=64) for n in range(N_TILES)]
         for n in range(N_TILES):
             nc.vector.tensor_copy(wd_bf[n][:].rearrange("n u c e -> n c u e"), wd_raw[n][:].indirect(offsets[:]))
 
-        def turn_wd(n, copy):
+        turned = {}
+
+        def turn_wd(n, bank):
             pairs = wd_bf[n][:].rearrange("n u c e -> n u (c e)").bitcast(F32)
-            turned = work_bank([P, J_PASSES, 2, P], "turned%d" % n)
+            turned[n] = bank_tile([P, J_PASSES, 2, P], "turned%d" % n, bank)
             for s in range(J_PASSES):
                 for u in range(2):
-                    nc.tensor.transpose(turned[:, s, u, :], pairs[:, u, s * P : (s + 1) * P], ident[:])
-            copy(wd_in(n, 1)[:, 0, :, :, :], turned[:].rearrange("p s u n -> p s n u"))
+                    nc.tensor.transpose(turned[n][:, s, u, :], pairs[:, u, s * P : (s + 1) * P], ident[:])
+
+        def collect_wd(n, copy):
+            copy(wd_in[:, n, :, :, :], turned[n][:].rearrange("p s u n -> p s n u"))
 
         def quantise_wd(first, many):
             tiles = slice(first, first + many)
             nc.vector.quantize_mx(
                 out=wd_codes[:, tiles, :].rearrange("p n c -> p (n c)").bitcast(FP8X4),
                 scales=wd_plane[:, tiles, :].rearrange("p n c -> p (n c)"),
-                in_=wd_in(first, many).rearrange("p t s n u -> p (t s n u)").bitcast(BF16),
+                in_=wd_in[:, tiles, :, :, :].rearrange("p t s n u -> p (t s n u)").bitcast(BF16),
             )
 
         totals = {}
@@ -328,15 +325,18 @@ def tile_list_regime_spread_hedge_kernel(
         stress(0)
         for c in range(last):
             stress(c + 1)
-            if c % 2 == 0 and c > 0:
-                turn_wd(c // 2 - 1, nc.vector.tensor_copy if c == 6 else nc.scalar.copy)
             spread(c)
-            if c in (3, 4):
-                open_total(c - 3, 0, psum.tile([P, 2, M // 2], F32, name="total%d" % c, offset=BANK * (WORK_BANKS + c - 3)))
-        turn_wd(N_TILES - 1, nc.scalar.copy)
         spread(last)
-        open_total(0, 1, work_bank([P, 2, M // 2], "total_c"))
-        open_total(1, 1, work_bank([P, 2, M // 2], "total_d"))
+        turn_wd(0, SUM_BANKS[0])
+        turn_wd(1, SUM_BANKS[1])
+        turn_wd(2, SUM_BANKS[3])
+        for (pair, half), bank in zip(((0, 0), (1, 0), (0, 1), (1, 1)), (DIFF_BANKS[0], SUM_BANKS[2], DIFF_BANKS[1], DIFF_BANKS[2])):
+            open_total(pair, half, bank_tile([P, 2, M // 2], "total%d_%d" % (pair, half), bank))
+        turn_wd(3, DIFF_BANKS[3])
+        collect_wd(0, nc.scalar.copy)
+        collect_wd(1, nc.scalar.copy)
+        collect_wd(2, nc.vector.tensor_copy)
+        collect_wd(3, nc.scalar.copy)
 
         for c in range(POOL_CHUNKS):
             weigh(c)
@@ -344,22 +344,18 @@ def tile_list_regime_spread_hedge_kernel(
         quantise_wd(0, 2)
         down(0, 0, 0, 2, False)
         down(0, 1, 0, 2, True)
-        quantise_h(4, 2)
         store(0, 0, nc.scalar.copy)
-        quantise_wd(2, 1)
         weigh(6)
-        quantise_wd(3, 1)
-        quantise_h(6, 1)
+        quantise_wd(2, 2)
         down(1, 0, 0, 2, False)
         down(1, 1, 0, 2, True)
+        store(1, 0, nc.scalar.copy)
+        weigh(7)
+        quantise_h(4, 2)
         for pair in range(2):
             down(pair, 0, 2, 2, False)
-        weigh(7)
-        store(1, 0, nc.scalar.copy)
+        quantise_h(6, 2)
         for pair in range(2):
-            down(pair, 1, 2, 1, False)
-        quantise_h(7, 1)
-        for pair in range(2):
-            down(pair, 1, 3, 1, True)
+            down(pair, 1, 2, 2, True)
         store(0, 1, nc.scalar.copy)
         store(1, 1, nc.vector.tensor_copy)

@@ -29,8 +29,10 @@ LIST_ROWS = 16
 X_COLS = M // 2
 BANK = 2048
 WORK_BANKS = 4
-SUM_BANKS = (4, 5, 6, 7)
-DIFF_BANKS = (0, 1, 2, 3)
+SUM_BANKS = (5, 6, 7)
+DIFF_OF = (0, 0, 2, 3, 1, 4, 2, 0)
+ADDED = (1,)
+EARLY = (0, 2, 3, 4, 5)
 POOL_CHUNKS = 6
 EARLY_TILES = 2
 
@@ -198,8 +200,15 @@ def tile_list_regime_spread_hedge_kernel(
         def bank_tile(shape, name, bank):
             return psum.tile(shape, F32, name=name, offset=BANK * bank)
 
-        h_bf = keep.tile([P, len(chunks) * P, PACK], BF16, name="h_bf", align_bytes=64)
-        codes = reuse.tile([P, J_PASSES * M + N_TILES * J_PASSES * P], U32, name="codes", align_bytes=64, offset=0)
+        h_early = keep.tile([P, POOL_CHUNKS * P, PACK], BF16, name="h_early", align_bytes=64)
+        h_late = reuse.tile([P, (len(chunks) - POOL_CHUNKS) * P, PACK], BF16, name="h_late", align_bytes=64, offset=2 * T)
+
+        def h_bf(first, many):
+            if first < POOL_CHUNKS:
+                return h_early[:, first * P : (first + many) * P, :]
+            return h_late[:, (first - POOL_CHUNKS) * P : (first - POOL_CHUNKS + many) * P, :]
+
+        codes = reuse.tile([P, J_PASSES * M + N_TILES * J_PASSES * P], U32, name="codes", align_bytes=64, offset=3 * T)
         h_codes = codes[:, 0 : J_PASSES * M]
         h_plane = keep.tile([P, J_PASSES * M], U8, name="h_plane", align_bytes=64)
 
@@ -210,51 +219,59 @@ def tile_list_regime_spread_hedge_kernel(
         size = keep.tile([P, J_PASSES, M, PACK], F32, name="size")
 
         def stress(c):
-            stressed[c] = ring.tile([P, PACK, P], F32, name="stressed", bufs=2)
-            response(1, chunks[c], -1.0, stressed[c], bank_tile([P, PASS], "stressed_sum%d" % c, SUM_BANKS[c % WORK_BANKS]))
+            stressed[c] = ring.tile([P, PACK, P], F32, name="stressed", bufs=3)
+            response(1, chunks[c], -1.0, stressed[c], bank_tile([P, PASS], "stressed_sum%d" % c, SUM_BANKS[c % len(SUM_BANKS)]))
 
         diffs = {}
 
-        def turn_onto_diff(c, values, opens):
+        def turn_onto_diff(c, values, opens, closes):
             if opens:
-                diffs[c] = bank_tile([P, PACK, P], "diff%d" % c, DIFF_BANKS[c % WORK_BANKS])
+                diffs[c] = bank_tile([P, PACK, P], "diff%d" % c, DIFF_OF[c])
             for i in range(PACK):
                 nc.tensor.matmul(
                     diffs[c][:, i, :],
                     values[:, i, :],
                     ident[:],
                     start=(opens and i == 0),
-                    stop=(not opens and i == PACK - 1),
+                    stop=(closes and i == PACK - 1),
                     is_transpose=True,
                 )
 
-        for c in range(WORK_BANKS):
-            turn_onto_diff(c, calm[chunks[c]], True)
+        for c in EARLY:
+            turn_onto_diff(c, calm[chunks[c]], True, False)
 
         def spread(c):
             s, mt = chunks[c]
-            if c >= WORK_BANKS:
-                turn_onto_diff(c, calm[chunks[c]], True)
-            turn_onto_diff(c, stressed[c], False)
+            if c in ADDED:
+                both = ring.tile([P, PACK, P], F32, name="both", bufs=len(ADDED))
+                nc.gpsimd.tensor_tensor(both[:], calm[chunks[c]][:], stressed[c][:], ALU.add)
+                turn_onto_diff(c, both, True, True)
+            else:
+                if c not in EARLY:
+                    turn_onto_diff(c, calm[chunks[c]], True, False)
+                turn_onto_diff(c, stressed[c], False, True)
             nc.scalar.activation(size[:, s, mt * P : (mt + 1) * P, :], diffs[c][:].rearrange("p i m -> p m i"), ACT.Abs)
 
         def weigh(c):
             s, mt = chunks[c]
             engine = nc.gpsimd if c < POOL_CHUNKS else nc.vector
             cols = slice(mt * P, (mt + 1) * P)
-            engine.tensor_tensor(h_bf[:, c * P : (c + 1) * P, :], size[:, s, cols, :], gains[:, s : s + 1, 0:PACK].to_broadcast([P, P, PACK]), ALU.mult)
+            engine.tensor_tensor(h_bf(c, 1), size[:, s, cols, :], gains[:, s : s + 1, 0:PACK].to_broadcast([P, P, PACK]), ALU.mult)
 
         def quantise_h(first, many):
             cols = slice(first * P, (first + many) * P)
             nc.vector.quantize_mx(
                 out=h_codes[:, cols].bitcast(FP8X4),
                 scales=h_plane[:, cols],
-                in_=h_bf[:, cols, :].rearrange("p m i -> p (m i)"),
+                in_=h_bf(first, many).rearrange("p m i -> p (m i)"),
             )
 
         wd_codes = codes[:, J_PASSES * M :].rearrange("p (n c) -> p n c", n=N_TILES)
         wd_plane = keep.tile([P, N_TILES, J_PASSES * P], U8, name="wd_plane", align_bytes=64)
-        wd_in = keep.tile([P, N_TILES, J_PASSES, P, 2], F32, name="wd_in", align_bytes=64)
+        wd_in = [
+            reuse.tile([P, 2, J_PASSES, P, 2], F32, name="wd_in0", align_bytes=64, offset=0),
+            keep.tile([P, 2, J_PASSES, P, 2], F32, name="wd_in1", align_bytes=64),
+        ]
 
         wd_bf = [keep.tile([P, 2, S // PACK, 2], BF16, name="wd_bf%d" % n, align_bytes=64) for n in range(N_TILES)]
         for n in range(N_TILES):
@@ -270,14 +287,14 @@ def tile_list_regime_spread_hedge_kernel(
                     nc.tensor.transpose(turned[n][:, s, u, :], pairs[:, u, s * P : (s + 1) * P], ident[:])
 
         def collect_wd(n, copy):
-            copy(wd_in[:, n, :, :, :], turned[n][:].rearrange("p s u n -> p s n u"))
+            copy(wd_in[n // 2][:, n % 2, :, :, :], turned[n][:].rearrange("p s u n -> p s n u"))
 
         def quantise_wd(first, many):
             tiles = slice(first, first + many)
             nc.vector.quantize_mx(
                 out=wd_codes[:, tiles, :].rearrange("p n c -> p (n c)").bitcast(FP8X4),
                 scales=wd_plane[:, tiles, :].rearrange("p n c -> p (n c)"),
-                in_=wd_in[:, tiles, :, :, :].rearrange("p t s n u -> p (t s n u)").bitcast(BF16),
+                in_=wd_in[first // 2][:, first % 2 : first % 2 + many, :, :, :].rearrange("p t s n u -> p (t s n u)").bitcast(BF16),
             )
 
         totals = {}
@@ -316,7 +333,7 @@ def tile_list_regime_spread_hedge_kernel(
                 )
 
         def store(pair, half, copy):
-            result = ring.tile([P, 2, M // 2], F32, name="result", bufs=4)
+            result = ring.tile([P, 2, M // 2], F32, name="result", bufs=2)
             copy(result[:], totals[pair, half][:])
             rows = out[2 * pair * P : 2 * (pair + 1) * P, half * M // 2 : (half + 1) * M // 2]
             nc.sync.dma_start(rows.rearrange("(u p) m -> p u m", p=P), result[:])
@@ -327,15 +344,15 @@ def tile_list_regime_spread_hedge_kernel(
             stress(c + 1)
             spread(c)
         spread(last)
-        turn_wd(0, SUM_BANKS[0])
-        turn_wd(1, SUM_BANKS[1])
-        turn_wd(2, SUM_BANKS[3])
-        for (pair, half), bank in zip(((0, 0), (1, 0), (0, 1), (1, 1)), (DIFF_BANKS[0], SUM_BANKS[2], DIFF_BANKS[1], DIFF_BANKS[2])):
+        turn_wd(0, DIFF_OF[3])
+        turn_wd(1, SUM_BANKS[2])
+        turn_wd(2, DIFF_OF[5])
+        for (pair, half), bank in zip(((0, 0), (1, 0), (0, 1), (1, 1)), (DIFF_OF[4], SUM_BANKS[0], SUM_BANKS[1], DIFF_OF[6])):
             open_total(pair, half, bank_tile([P, 2, M // 2], "total%d_%d" % (pair, half), bank))
-        turn_wd(3, DIFF_BANKS[3])
+        turn_wd(3, DIFF_OF[7])
         collect_wd(0, nc.scalar.copy)
-        collect_wd(1, nc.scalar.copy)
-        collect_wd(2, nc.vector.tensor_copy)
+        collect_wd(1, nc.vector.tensor_copy)
+        collect_wd(2, nc.scalar.copy)
         collect_wd(3, nc.scalar.copy)
 
         for c in range(POOL_CHUNKS):
@@ -357,5 +374,9 @@ def tile_list_regime_spread_hedge_kernel(
         quantise_h(6, 2)
         for pair in range(2):
             down(pair, 1, 2, 2, True)
-        store(0, 1, nc.scalar.copy)
-        store(1, 1, nc.vector.tensor_copy)
+        for u in range(2):
+            for pair, copy in ((0, nc.scalar.copy), (1, nc.vector.tensor_copy)):
+                n = 2 * pair + u
+                result = ring.tile([P, M // 2], F32, name="last_result", bufs=N_TILES)
+                copy(result[:], totals[pair, 1][:, u, :])
+                nc.sync.dma_start(out[n * P : (n + 1) * P, M // 2 : M], result[:])

@@ -28,13 +28,11 @@ QUADRANTS = 4
 LIST_ROWS = 16
 X_COLS = M // 2
 BANK = 2048
-WORK_BANKS = 4
-SUM_BANKS = (5, 6, 7)
-DIFF_OF = (0, 0, 2, 3, 1, 4, 2, 0)
-ADDED = (1,)
-EARLY = (0, 2, 3, 4, 5)
-POOL_CHUNKS = 6
-EARLY_TILES = 2
+BANKS = 8
+SUM_BANKS = 3
+POOL_CHUNKS = 5
+ADDED_CHUNK = 1
+STRESSED_BUFS = 5
 
 
 def tile_list_regime_spread_hedge_kernel(
@@ -48,11 +46,7 @@ def tile_list_regime_spread_hedge_kernel(
         early = ctx.enter_context(tc.tile_pool(name="early", bufs=1))
         reuse = ctx.enter_context(tc.tile_pool(name="reuse", bufs=1))
 
-        handed_out = []
-
-        def work_bank(shape, name):
-            bank = len(handed_out) % WORK_BANKS
-            handed_out.append(name)
+        def bank_tile(shape, name, bank):
             return psum.tile(shape, F32, name=name, offset=BANK * bank)
 
         offsets = keep.tile([P, S // LIST_ROWS], U16, name="offsets")
@@ -99,93 +93,80 @@ def tile_list_regime_spread_hedge_kernel(
         load_words(1, tab2_words, 0)
         load_words(1, tab2_words, 1)
         nc.sync.dma_start(gains[:, :, 0:PACK], g.rearrange("(s p i) -> p s i", p=P, i=PACK))
-        for n in range(N_TILES):
+        for n in range(N_TILES - 1):
             nc.sync.dma_start(wd_raw[n][:], wdT[n * P : (n + 1) * P, :])
         for q in range(QUADRANTS):
             nc.sync.dma_start(
                 w4_plane[32 * q : 32 * q + 4, :, :],
                 w4_scales[:, 4 * q : 4 * q + 4, :].rearrange("a r c -> r a c").bitcast(I32),
             )
+        nc.sync.dma_start(wd_raw[-1][:], wdT[N - P : N, :])
         nc.sync.dma_start(w4_codes[:].bitcast(I32), w4_words.rearrange("a p c -> p a c").bitcast(I32))
 
+        def list_half(s):
+            return offsets[:, s * PASS // LIST_ROWS : (s + 1) * PASS // LIST_ROWS]
+
         calm_scales = keep.tile([P, S], U8, name="calm_scales", align_bytes=64)
-        picked_scales = [
-            [calm_scales[:, s * PASS : (s + 1) * PASS] for s in range(J_PASSES)],
-            [
-                keep.tile([P, PASS], U8, name="picked_scales1_0", align_bytes=64),
-            ],
-        ]
-        picked_words = [
-            [keep.tile([P, S], U32, name="picked_words%d_%d" % (t, a), align_bytes=64) if a == 0 else None for a in range(K_PASSES)]
-            for t in range(2)
-        ]
-
-        def gather_scales(t, lo, hi, dst):
-            nc.vector.tensor_copy(dst, scale_rows[t][:].bitcast(U8).indirect(offsets[:, lo // LIST_ROWS : hi // LIST_ROWS]))
-
-        def gather_words(t, a):
-            pieces = J_PASSES if a == K_PASSES - 1 else 1
-            for piece in range(pieces):
-                lo, hi = piece * S // pieces, (piece + 1) * S // pieces
-                nc.vector.tensor_copy(
-                    picked_words[t][a][:, lo:hi],
-                    words[t][a][:].indirect(offsets[:, lo // LIST_ROWS : hi // LIST_ROWS]),
-                )
+        stressed_scales = [keep.tile([P, PASS], U8, name="stressed_scales0", align_bytes=64)]
+        first_words = [keep.tile([P, S], U32, name="first_words%d" % t, align_bytes=64) for t in range(2)]
+        second_words = [[], []]
 
         x_codes = [keep.tile([P, M], U32, name="x_codes%d" % a, align_bytes=64) for a in range(K_PASSES)]
         x_plane = [keep.tile([P, M], U8, name="x_plane%d" % a, align_bytes=64) for a in range(K_PASSES)]
 
-        def quantise_x(a, first, many):
-            for m0 in range(first * X_COLS, (first + many) * X_COLS, X_COLS):
-                cols = slice(m0, m0 + X_COLS)
-                x_bf = early.tile(
-                    [P, X_COLS, PACK], BF16, name="x_bf%d_%d" % (a, m0), align_bytes=64, offset=2 * PACK * (a * M + m0)
-                )
-                nc.scalar.activation(
-                    x_bf[:].rearrange("p (c e) i -> p c i e", e=4),
-                    x_raw[a][m0 // X_COLS].rearrange("p i (c e) -> p c i e", e=4),
-                    ACT.Copy,
-                )
-                nc.vector.quantize_mx(
-                    out=x_codes[a][:, cols].bitcast(FP8X4),
-                    scales=x_plane[a][:, cols],
-                    in_=x_bf[:].rearrange("p m i -> p (m i)"),
-                )
+        def x_bf_offset(a, half):
+            return 2 * PACK * X_COLS * (2 * a + half)
 
-        gather_words(0, 0)
-        gather_scales(0, 0, S, calm_scales[:])
-        gather_scales(1, 0, PASS, picked_scales[1][0][:])
-        quantise_x(0, 0, 1)
-        picked_scales[1].append(early.tile([P, PASS], U8, name="picked_scales1_1", align_bytes=64, offset=0))
-        gather_scales(1, PASS, S, picked_scales[1][1][:])
-        quantise_x(0, 1, 1)
-        second = []
+        def quantise_x(a, half):
+            cols = slice(half * X_COLS, (half + 1) * X_COLS)
+            x_bf = early.tile(
+                [P, X_COLS, PACK], BF16, name="x_bf%d_%d" % (a, half), align_bytes=64, offset=x_bf_offset(a, half)
+            )
+            nc.scalar.activation(
+                x_bf[:].rearrange("p (c e) i -> p c i e", e=4),
+                x_raw[a][half].rearrange("p i (c e) -> p c i e", e=4),
+                ACT.Copy,
+            )
+            nc.vector.quantize_mx(
+                out=x_codes[a][:, cols].bitcast(FP8X4),
+                scales=x_plane[a][:, cols],
+                in_=x_bf[:].rearrange("p m i -> p (m i)"),
+            )
+
+        nc.vector.tensor_copy(first_words[0][:], words[0][0][:].indirect(offsets[:]))
+        nc.vector.tensor_copy(calm_scales[:], scale_rows[0][:].bitcast(U8).indirect(offsets[:]))
+        nc.vector.tensor_copy(stressed_scales[0][:], scale_rows[1][:].bitcast(U8).indirect(list_half(0)))
+        quantise_x(0, 0)
+        stressed_scales.append(early.tile([P, PASS], U8, name="stressed_scales1", align_bytes=64, offset=x_bf_offset(0, 0)))
+        nc.vector.tensor_copy(stressed_scales[1][:], scale_rows[1][:].bitcast(U8).indirect(list_half(1)))
+        quantise_x(0, 1)
+        for s, follows in enumerate((x_bf_offset(0, 1), x_bf_offset(1, 0))):
+            second_words[0].append(early.tile([P, PASS], U32, name="calm_second%d" % s, align_bytes=64, offset=follows))
+            nc.vector.tensor_copy(second_words[0][s][:], words[0][1][:].indirect(list_half(s)))
+            quantise_x(1, s)
+        nc.vector.tensor_copy(first_words[1][:], words[1][0][:].indirect(offsets[:]))
         for s in range(J_PASSES):
-            second.append(early.tile([P, PASS], U32, name="second%d" % s, align_bytes=64, offset=2 * PACK * X_COLS * (s + 1)))
-            nc.vector.tensor_copy(second[s][:], words[0][1][:].indirect(offsets[:, s * PASS // LIST_ROWS : (s + 1) * PASS // LIST_ROWS]))
-            quantise_x(1, s, 1)
+            second_words[1].append(keep.tile([P, PASS], U32, name="stressed_second%d" % s, align_bytes=64))
+            nc.vector.tensor_copy(second_words[1][s][:], words[1][1][:].indirect(list_half(s)))
 
-        def picked(t, a, s):
-            if a == 1:
-                return (second, closing)[t][s][:]
-            return picked_words[t][a][:, s * PASS : (s + 1) * PASS]
+        def picked_words(t, a, s):
+            return first_words[t][:, s * PASS : (s + 1) * PASS] if a == 0 else second_words[t][s][:]
 
-        gather_words(1, 0)
-        closing = [keep.tile([P, PASS], U32, name="closing%d" % s, align_bytes=64) for s in range(J_PASSES)]
-        for s in range(J_PASSES):
-            nc.vector.tensor_copy(closing[s][:], words[1][1][:].indirect(offsets[:, s * PASS // LIST_ROWS : (s + 1) * PASS // LIST_ROWS]))
+        def picked_plane(t, a, s):
+            rows = calm_scales[:, s * PASS : (s + 1) * PASS] if t == 0 else stressed_scales[s][:]
+            return rows[4 * a : P, :]
 
-        def response(t, chunk, sign, dst, acc, passes=(0, 1)):
+        def response(t, chunk, sign, dst, acc):
             s, mt = chunk
-            for a in passes:
+            for a in range(K_PASSES):
                 nc.tensor.matmul_mx(
                     out=acc[:],
                     lhsT=x_codes[a][:, mt * P : (mt + 1) * P].bitcast(FP8X4),
                     lhsT_scale=x_plane[a][:, mt * P : (mt + 1) * P],
-                    rhs=picked(t, a, s).bitcast(FP8X4),
-                    rhs_scale=picked_scales[t][s][4 * a : P, :],
-                    start=(a == passes[0]),
-                    stop=(a == passes[-1]),
+                    rhs=picked_words(t, a, s).bitcast(FP8X4),
+                    rhs_scale=picked_plane(t, a, s),
+                    start=(a == 0),
+                    stop=(a == K_PASSES - 1),
                 )
             nc.scalar.activation(
                 dst[:].rearrange("m i (c e) -> m c i e", e=2),
@@ -195,13 +176,11 @@ def tile_list_regime_spread_hedge_kernel(
             )
 
         chunks = [(s, 2 * half + u) for half in range(2) for s in range(J_PASSES) for u in range(2)]
-        calm = {chunk: keep.tile([P, PACK, P], F32, name="calm%d_%d" % chunk) for chunk in chunks}
-
-        def bank_tile(shape, name, bank):
-            return psum.tile(shape, F32, name=name, offset=BANK * bank)
+        last = len(chunks) - 1
+        calm = [keep.tile([P, PACK, P], F32, name="calm%d_%d" % chunk) for chunk in chunks]
 
         h_early = keep.tile([P, POOL_CHUNKS * P, PACK], BF16, name="h_early", align_bytes=64)
-        h_late = reuse.tile([P, (len(chunks) - POOL_CHUNKS) * P, PACK], BF16, name="h_late", align_bytes=64, offset=2 * T)
+        h_late = reuse.tile([P, (len(chunks) - POOL_CHUNKS) * P, PACK], BF16, name="h_late", align_bytes=64, offset=0)
 
         def h_bf(first, many):
             if first < POOL_CHUNKS:
@@ -213,20 +192,27 @@ def tile_list_regime_spread_hedge_kernel(
         h_plane = keep.tile([P, J_PASSES * M], U8, name="h_plane", align_bytes=64)
 
         for c, chunk in enumerate(chunks):
-            response(0, chunk, 1.0, calm[chunk], bank_tile([P, PASS], "calm_sum%d" % c, c))
+            response(0, chunk, 1.0, calm[c], bank_tile([P, PASS], "calm_sum%d" % c, c))
+
+        sum_bank = [BANKS - SUM_BANKS + c % SUM_BANKS for c in range(len(chunks))]
+        opened_early = [c for c in range(len(chunks)) if c != ADDED_CHUNK][: BANKS - SUM_BANKS]
+        diff_bank = {c: bank for bank, c in enumerate(opened_early)}
+        diff_bank[ADDED_CHUNK] = diff_bank[0]
+        diff_bank[last - 1] = diff_bank[ADDED_CHUNK + 1]
+        diff_bank[last] = diff_bank[ADDED_CHUNK]
 
         stressed = {}
         size = keep.tile([P, J_PASSES, M, PACK], F32, name="size")
 
         def stress(c):
-            stressed[c] = ring.tile([P, PACK, P], F32, name="stressed", bufs=3)
-            response(1, chunks[c], -1.0, stressed[c], bank_tile([P, PASS], "stressed_sum%d" % c, SUM_BANKS[c % len(SUM_BANKS)]))
+            stressed[c] = ring.tile([P, PACK, P], F32, name="stressed", bufs=STRESSED_BUFS)
+            response(1, chunks[c], -1.0, stressed[c], bank_tile([P, PASS], "stressed_sum%d" % c, sum_bank[c]))
 
         diffs = {}
 
         def turn_onto_diff(c, values, opens, closes):
             if opens:
-                diffs[c] = bank_tile([P, PACK, P], "diff%d" % c, DIFF_OF[c])
+                diffs[c] = bank_tile([P, PACK, P], "diff%d" % c, diff_bank[c])
             for i in range(PACK):
                 nc.tensor.matmul(
                     diffs[c][:, i, :],
@@ -237,18 +223,18 @@ def tile_list_regime_spread_hedge_kernel(
                     is_transpose=True,
                 )
 
-        for c in EARLY:
-            turn_onto_diff(c, calm[chunks[c]], True, False)
+        for c in opened_early:
+            turn_onto_diff(c, calm[c], True, False)
 
         def spread(c):
             s, mt = chunks[c]
-            if c in ADDED:
-                both = ring.tile([P, PACK, P], F32, name="both", bufs=len(ADDED))
-                nc.gpsimd.tensor_tensor(both[:], calm[chunks[c]][:], stressed[c][:], ALU.add)
+            if c == ADDED_CHUNK:
+                both = ring.tile([P, PACK, P], F32, name="both")
+                nc.gpsimd.tensor_tensor(both[:], calm[c][:], stressed[c][:], ALU.add)
                 turn_onto_diff(c, both, True, True)
             else:
-                if c not in EARLY:
-                    turn_onto_diff(c, calm[chunks[c]], True, False)
+                if c not in opened_early:
+                    turn_onto_diff(c, calm[c], True, False)
                 turn_onto_diff(c, stressed[c], False, True)
             nc.scalar.activation(size[:, s, mt * P : (mt + 1) * P, :], diffs[c][:].rearrange("p i m -> p m i"), ACT.Abs)
 
@@ -256,7 +242,8 @@ def tile_list_regime_spread_hedge_kernel(
             s, mt = chunks[c]
             engine = nc.gpsimd if c < POOL_CHUNKS else nc.vector
             cols = slice(mt * P, (mt + 1) * P)
-            engine.tensor_tensor(h_bf(c, 1), size[:, s, cols, :], gains[:, s : s + 1, 0:PACK].to_broadcast([P, P, PACK]), ALU.mult)
+            gain = gains[:, s : s + 1, 0:PACK].to_broadcast([P, P, PACK])
+            engine.tensor_tensor(h_bf(c, 1), size[:, s, cols, :], gain, ALU.mult)
 
         def quantise_h(first, many):
             cols = slice(first * P, (first + many) * P)
@@ -268,10 +255,7 @@ def tile_list_regime_spread_hedge_kernel(
 
         wd_codes = codes[:, J_PASSES * M :].rearrange("p (n c) -> p n c", n=N_TILES)
         wd_plane = keep.tile([P, N_TILES, J_PASSES * P], U8, name="wd_plane", align_bytes=64)
-        wd_in = [
-            reuse.tile([P, 2, J_PASSES, P, 2], F32, name="wd_in0", align_bytes=64, offset=0),
-            keep.tile([P, 2, J_PASSES, P, 2], F32, name="wd_in1", align_bytes=64),
-        ]
+        wd_in = [keep.tile([P, 2, J_PASSES, P, 2], F32, name="wd_in%d" % pair, align_bytes=64) for pair in range(2)]
 
         wd_bf = [keep.tile([P, 2, S // PACK, 2], BF16, name="wd_bf%d" % n, align_bytes=64) for n in range(N_TILES)]
         for n in range(N_TILES):
@@ -286,20 +270,21 @@ def tile_list_regime_spread_hedge_kernel(
                 for u in range(2):
                     nc.tensor.transpose(turned[n][:, s, u, :], pairs[:, u, s * P : (s + 1) * P], ident[:])
 
-        def collect_wd(n, copy):
-            copy(wd_in[n // 2][:, n % 2, :, :, :], turned[n][:].rearrange("p s u n -> p s n u"))
+        def collect_wd(n):
+            nc.scalar.copy(wd_in[n // 2][:, n % 2, :, :, :], turned[n][:].rearrange("p s u n -> p s n u"))
 
-        def quantise_wd(first, many):
-            tiles = slice(first, first + many)
+        def quantise_wd(pair):
+            tiles = slice(2 * pair, 2 * pair + 2)
             nc.vector.quantize_mx(
                 out=wd_codes[:, tiles, :].rearrange("p n c -> p (n c)").bitcast(FP8X4),
                 scales=wd_plane[:, tiles, :].rearrange("p n c -> p (n c)"),
-                in_=wd_in[first // 2][:, first % 2 : first % 2 + many, :, :, :].rearrange("p t s n u -> p (t s n u)").bitcast(BF16),
+                in_=wd_in[pair][:].rearrange("p t s n u -> p (t s n u)").bitcast(BF16),
             )
 
         totals = {}
 
-        def open_total(pair, half, tile):
+        def open_total(pair, half, bank):
+            tile = bank_tile([P, 2, M // 2], "total%d_%d" % (pair, half), bank)
             totals[pair, half] = tile
             for u in range(2):
                 n = 2 * pair + u
@@ -316,9 +301,10 @@ def tile_list_regime_spread_hedge_kernel(
                             stop=False,
                         )
 
-        def down(pair, s, mt, many, last):
+        def down(pair, first, many):
+            s, mt = chunks[first]
             half, v = divmod(mt, 2)
-            first = chunks.index((s, mt))
+            closes = s == J_PASSES - 1 and v + many == 2
             cols = slice(first * P, (first + many) * P)
             for u in range(2):
                 n = 2 * pair + u
@@ -329,54 +315,63 @@ def tile_list_regime_spread_hedge_kernel(
                     rhs=h_codes[:, cols].bitcast(FP8X4),
                     rhs_scale=h_plane[:, cols],
                     start=False,
-                    stop=(last and u == 1),
+                    stop=(closes and u == 1),
                 )
 
-        def store(pair, half, copy):
+        def store_first_half(pair):
             result = ring.tile([P, 2, M // 2], F32, name="result", bufs=2)
-            copy(result[:], totals[pair, half][:])
-            rows = out[2 * pair * P : 2 * (pair + 1) * P, half * M // 2 : (half + 1) * M // 2]
+            nc.scalar.copy(result[:], totals[pair, 0][:])
+            rows = out[2 * pair * P : 2 * (pair + 1) * P, 0 : M // 2]
             nc.sync.dma_start(rows.rearrange("(u p) m -> p u m", p=P), result[:])
 
-        last = len(chunks) - 1
-        stress(0)
-        for c in range(last):
-            stress(c + 1)
-            spread(c)
+        spread_order = [ADDED_CHUNK + 1, ADDED_CHUNK] + list(range(ADDED_CHUNK + 2, last))
+        for c in range(SUM_BANKS):
+            stress(c)
+        spread(0)
+        for c in range(SUM_BANKS, len(chunks), 2):
+            for d in range(c, min(c + 2, len(chunks))):
+                stress(d)
+            for d in spread_order[c - SUM_BANKS : c - SUM_BANKS + 2]:
+                spread(d)
         spread(last)
-        turn_wd(0, DIFF_OF[3])
-        turn_wd(1, SUM_BANKS[2])
-        turn_wd(2, DIFF_OF[5])
-        for (pair, half), bank in zip(((0, 0), (1, 0), (0, 1), (1, 1)), (DIFF_OF[4], SUM_BANKS[0], SUM_BANKS[1], DIFF_OF[6])):
-            open_total(pair, half, bank_tile([P, 2, M // 2], "total%d_%d" % (pair, half), bank))
-        turn_wd(3, DIFF_OF[7])
-        collect_wd(0, nc.scalar.copy)
-        collect_wd(1, nc.vector.tensor_copy)
-        collect_wd(2, nc.scalar.copy)
-        collect_wd(3, nc.scalar.copy)
+
+        turn_wd(0, diff_bank[3])
+        turn_wd(1, sum_bank[5])
+        turn_wd(2, diff_bank[5])
+        open_total(0, 0, diff_bank[4])
+        open_total(1, 0, sum_bank[6])
+        turn_wd(3, diff_bank[7])
+        open_total(0, 1, sum_bank[7])
+        open_total(1, 1, diff_bank[6])
+        for n in range(N_TILES):
+            collect_wd(n)
 
         for c in range(POOL_CHUNKS):
             weigh(c)
+
+        def finish_first_half(pair):
+            quantise_wd(pair)
+            for s in range(J_PASSES):
+                down(pair, 2 * s, 2)
+            store_first_half(pair)
+
         quantise_h(0, 4)
-        quantise_wd(0, 2)
-        down(0, 0, 0, 2, False)
-        down(0, 1, 0, 2, True)
-        store(0, 0, nc.scalar.copy)
+        finish_first_half(0)
+        weigh(5)
+        finish_first_half(1)
+        quantise_h(4, 1)
+        quantise_h(5, 1)
+        for pair in range(2):
+            down(pair, 4, 2)
         weigh(6)
-        quantise_wd(2, 2)
-        down(1, 0, 0, 2, False)
-        down(1, 1, 0, 2, True)
-        store(1, 0, nc.scalar.copy)
         weigh(7)
-        quantise_h(4, 2)
-        for pair in range(2):
-            down(pair, 0, 2, 2, False)
-        quantise_h(6, 2)
-        for pair in range(2):
-            down(pair, 1, 2, 2, True)
+        for c in (last - 1, last):
+            quantise_h(c, 1)
+            for pair in range(2):
+                down(pair, c, 1)
         for u in range(2):
-            for pair, copy in ((0, nc.scalar.copy), (1, nc.vector.tensor_copy)):
+            for pair, copy in enumerate((nc.scalar.copy, nc.vector.tensor_copy)):
                 n = 2 * pair + u
-                result = ring.tile([P, M // 2], F32, name="last_result", bufs=N_TILES)
-                copy(result[:], totals[pair, 1][:, u, :])
-                nc.sync.dma_start(out[n * P : (n + 1) * P, M // 2 : M], result[:])
+                tile_out = ring.tile([P, M // 2], F32, name="tile_out", bufs=N_TILES)
+                copy(tile_out[:], totals[pair, 1][:, u, :])
+                nc.sync.dma_start(out[n * P : (n + 1) * P, M // 2 : M], tile_out[:])

@@ -27,8 +27,14 @@ N_TILES = N // P
 QUADRANTS = 4
 LIST_ROWS = 16
 X_COLS = M // 2
+SLOT = 4 * T
+LAST_SLOT = 6
+GAINS_BYTES = 64
+ROWS_AT = (0, 64)
+PLANE_AT = (0, 8)
 BANK = 2048
 BANKS = 8
+CALM_BANKS = 6
 SUM_BANKS = 3
 POOL_CHUNKS = 5
 ADDED_CHUNK = 1
@@ -43,8 +49,8 @@ def tile_list_regime_spread_hedge_kernel(
         keep = ctx.enter_context(tc.tile_pool(name="keep", bufs=1))
         ring = ctx.enter_context(tc.tile_pool(name="ring", bufs=1))
         psum = ctx.enter_context(tc.psum_pool(name="psum", bufs=1))
+        stream = ctx.enter_context(tc.tile_pool(name="stream", bufs=1))
         early = ctx.enter_context(tc.tile_pool(name="early", bufs=1))
-        reuse = ctx.enter_context(tc.tile_pool(name="reuse", bufs=1))
 
         def bank_tile(shape, name, bank):
             return psum.tile(shape, F32, name=name, offset=BANK * bank)
@@ -52,79 +58,85 @@ def tile_list_regime_spread_hedge_kernel(
         offsets = keep.tile([P, S // LIST_ROWS], U16, name="offsets")
         nc.sync.dma_start(offsets[:], offs)
 
-        scale_rows = [keep.tile([P, T // 4], I32, name="scale_rows%d" % t, align_bytes=64) for t in range(2)]
-        w4_plane = keep.tile([P, K_PASSES, N // 4], I32, name="w4_plane", align_bytes=64)
-        nc.gpsimd.memset(scale_rows[0][:], 0)
-        nc.vector.memset(scale_rows[1][:], 0)
-        nc.vector.memset(w4_plane[:], 0)
-
         ident = keep.tile([P, P], F32, name="ident")
         make_identity(nc, ident[:])
 
-        words = [
-            [keep.tile([P, T], U32, name="words%d_%d" % (t, a), align_bytes=64) for a in range(K_PASSES)]
+        def slot_tile(shape, dtype, name, slot, shift=0):
+            return stream.tile(shape, dtype, name=name, align_bytes=64, offset=SLOT * slot + GAINS_BYTES * (slot > 2) + shift)
+
+        scale_rows = [slot_tile([P, T // 4], I32, "scale_rows%d" % t, 2 * t + 1, -T // 2) for t in range(2)]
+        for t, src in enumerate((tab_scales, tab2_scales)):
+            first = ROWS_AT[t]
+            nc.sync.dma_start(scale_rows[t][first : first + 32, :], src.rearrange("a q c -> (a q) c").bitcast(I32))
+        nc.vector.memset(scale_rows[0][32:64, :], 0)
+        nc.vector.memset(scale_rows[0][64:P, :], 0)
+        nc.vector.memset(scale_rows[1][0:64, :], 0)
+        nc.vector.memset(scale_rows[1][96:P, :], 0)
+        planes = [
+            [keep.tile([P, S // 4], I32, name="plane%d_%d" % (t, a), align_bytes=64) for a in range(K_PASSES)]
             for t in range(2)
         ]
-        x_first = keep.tile([P, PACK, M], F32, name="x_first")
-        x_raw = [
-            [x_first[:, :, half * X_COLS : (half + 1) * X_COLS] for half in range(2)],
-            [keep.tile([P, PACK, X_COLS], F32, name="x_second%d" % half)[:] for half in range(2)],
-        ]
-        wd_raw = [keep.tile([P, T], F32, name="wd_raw%d" % n, align_bytes=64) for n in range(N_TILES - 1)]
-        wd_raw.append(reuse.tile([P, T], F32, name="wd_raw_last", align_bytes=64, offset=0))
-        gains = keep.tile([P, J_PASSES, 2 * PACK], F32, name="gains")
-        w4_codes = keep.tile([P, K_PASSES, 2 * N], U8, name="w4_codes", align_bytes=64)
+        for t in range(2):
+            for a in range(K_PASSES):
+                nc.gpsimd.memset(planes[t][a][:], 0)
 
-        def load_scale_rows(t, src):
-            for q in range(QUADRANTS):
-                rows = scale_rows[t][32 * q : 32 * q + 4 * K_PASSES, :]
-                nc.sync.dma_start(rows, src[:, 4 * q : 4 * q + 4, :].bitcast(I32))
+        def load_words(name, src, slot):
+            tile = slot_tile([P, T], U32, name, slot)
+            nc.sync.dma_start(tile[:].bitcast(I32), src.rearrange("p c i -> p (c i)").bitcast(I32))
+            return tile
 
-        def load_words(t, src, a):
-            nc.sync.dma_start(words[t][a][:].bitcast(I32), src[a].rearrange("p c i -> p (c i)").bitcast(I32))
+        def load_wd(n, slot):
+            tile = slot_tile([P, T], F32, "wd_raw%d" % n, slot)
+            nc.sync.dma_start(tile[:], wdT[n * P : (n + 1) * P, :])
+            return tile
 
-        load_scale_rows(0, tab_scales)
-        load_scale_rows(1, tab2_scales)
-        load_words(0, tab_words, 0)
-        nc.sync.dma_start(x_first[:], x[0:PASS, :].rearrange("(p i) m -> p i m", i=PACK))
-        nc.sync.dma_start(x_raw[1][0], x[PASS:K, 0:X_COLS].rearrange("(p i) m -> p i m", i=PACK))
-        load_words(0, tab_words, 1)
-        nc.sync.dma_start(x_raw[1][1], x[PASS:K, X_COLS:M].rearrange("(p i) m -> p i m", i=PACK))
-        load_words(1, tab2_words, 0)
-        load_words(1, tab2_words, 1)
+        words = {(0, 0): load_words("words0_0", tab_words[0], 4)}
+        x_raw = [slot_tile([P, PACK, M], F32, "x_raw%d" % a, 5 + a) for a in range(K_PASSES)]
+        for a in range(K_PASSES):
+            nc.sync.dma_start(x_raw[a][:], x[a * PASS : (a + 1) * PASS, :].rearrange("(p i) m -> p i m", i=PACK))
+
+        picked_rows = [keep.tile([P, S], U8, name="picked_rows%d" % t, align_bytes=64) for t in range(2)]
+        for t in range(2):
+            nc.vector.tensor_copy(picked_rows[t][:], scale_rows[t][:].bitcast(U8).indirect(offsets[:]))
+
+        def move_rows(t, first, many):
+            for u in range(first, first + many):
+                a, r = divmod(u, 4)
+                row = ROWS_AT[t] + 16 * a + r
+                nc.sync.dma_start(
+                    planes[t][a][PLANE_AT[t] + u : P : 32, :], picked_rows[t][row : row + 13 : 4, :].bitcast(I32)
+                )
+
+        move_rows(0, 0, 6)
+        words[0, 1] = load_words("words0_1", tab_words[1], 0)
+        move_rows(0, 6, 2)
+        words[1, 0] = load_words("words1_0", tab2_words[0], 1)
+        move_rows(1, 0, 4)
+        words[1, 1] = load_words("words1_1", tab2_words[1], 2)
+        move_rows(1, 4, 4)
+        gains = slot_tile([P, J_PASSES, 2 * PACK], F32, "gains", 3, -GAINS_BYTES)
         nc.sync.dma_start(gains[:, :, 0:PACK], g.rearrange("(s p i) -> p s i", p=P, i=PACK))
-        for n in range(N_TILES - 1):
-            nc.sync.dma_start(wd_raw[n][:], wdT[n * P : (n + 1) * P, :])
-        for q in range(QUADRANTS):
-            nc.sync.dma_start(
-                w4_plane[32 * q : 32 * q + 4, :, :],
-                w4_scales[:, 4 * q : 4 * q + 4, :].rearrange("a r c -> r a c").bitcast(I32),
-            )
-        nc.sync.dma_start(wd_raw[-1][:], wdT[N - P : N, :])
-        nc.sync.dma_start(w4_codes[:].bitcast(I32), w4_words.rearrange("a p c -> p a c").bitcast(I32))
+        wd_raw = [load_wd(0, 3)]
 
         def list_half(s):
             return offsets[:, s * PASS // LIST_ROWS : (s + 1) * PASS // LIST_ROWS]
 
-        calm_scales = keep.tile([P, S], U8, name="calm_scales", align_bytes=64)
-        stressed_scales = [keep.tile([P, PASS], U8, name="stressed_scales0", align_bytes=64)]
-        first_words = [keep.tile([P, S], U32, name="first_words%d" % t, align_bytes=64) for t in range(2)]
-        second_words = [[], []]
-
+        stressed_first = keep.tile([P, S], U32, name="stressed_first", align_bytes=64)
+        second_words = [
+            [keep.tile([P, PASS], U32, name="second_words%d_%d" % (t, s), align_bytes=64) for s in range(J_PASSES)]
+            for t in range(2)
+        ]
         x_codes = [keep.tile([P, M], U32, name="x_codes%d" % a, align_bytes=64) for a in range(K_PASSES)]
         x_plane = [keep.tile([P, M], U8, name="x_plane%d" % a, align_bytes=64) for a in range(K_PASSES)]
-
-        def x_bf_offset(a, half):
-            return 2 * PACK * X_COLS * (2 * a + half)
 
         def quantise_x(a, half):
             cols = slice(half * X_COLS, (half + 1) * X_COLS)
             x_bf = early.tile(
-                [P, X_COLS, PACK], BF16, name="x_bf%d_%d" % (a, half), align_bytes=64, offset=x_bf_offset(a, half)
+                [P, X_COLS, PACK], BF16, name="x_bf%d_%d" % (a, half), align_bytes=64, offset=2 * PACK * X_COLS * (2 * a + half)
             )
             nc.scalar.activation(
                 x_bf[:].rearrange("p (c e) i -> p c i e", e=4),
-                x_raw[a][half].rearrange("p i (c e) -> p c i e", e=4),
+                x_raw[a][:, :, cols].rearrange("p i (c e) -> p c i e", e=4),
                 ACT.Copy,
             )
             nc.vector.quantize_mx(
@@ -133,28 +145,39 @@ def tile_list_regime_spread_hedge_kernel(
                 in_=x_bf[:].rearrange("p m i -> p (m i)"),
             )
 
-        nc.vector.tensor_copy(first_words[0][:], words[0][0][:].indirect(offsets[:]))
-        nc.vector.tensor_copy(calm_scales[:], scale_rows[0][:].bitcast(U8).indirect(offsets[:]))
-        nc.vector.tensor_copy(stressed_scales[0][:], scale_rows[1][:].bitcast(U8).indirect(list_half(0)))
+        calm_first = [keep.tile([P, PASS], U32, name="calm_first0", align_bytes=64)]
+        nc.vector.tensor_copy(calm_first[0][:], words[0, 0][:].indirect(list_half(0)))
         quantise_x(0, 0)
-        stressed_scales.append(early.tile([P, PASS], U8, name="stressed_scales1", align_bytes=64, offset=x_bf_offset(0, 0)))
-        nc.vector.tensor_copy(stressed_scales[1][:], scale_rows[1][:].bitcast(U8).indirect(list_half(1)))
+        calm_first.append(early.tile([P, PASS], U32, name="calm_first1", align_bytes=64, offset=0))
+        nc.vector.tensor_copy(calm_first[1][:], words[0, 0][:].indirect(list_half(1)))
         quantise_x(0, 1)
-        for s, follows in enumerate((x_bf_offset(0, 1), x_bf_offset(1, 0))):
-            second_words[0].append(early.tile([P, PASS], U32, name="calm_second%d" % s, align_bytes=64, offset=follows))
-            nc.vector.tensor_copy(second_words[0][s][:], words[0][1][:].indirect(list_half(s)))
-            quantise_x(1, s)
-        nc.vector.tensor_copy(first_words[1][:], words[1][0][:].indirect(offsets[:]))
+        for half in range(2):
+            quantise_x(1, half)
         for s in range(J_PASSES):
-            second_words[1].append(keep.tile([P, PASS], U32, name="stressed_second%d" % s, align_bytes=64))
-            nc.vector.tensor_copy(second_words[1][s][:], words[1][1][:].indirect(list_half(s)))
+            nc.vector.tensor_copy(second_words[0][s][:], words[0, 1][:].indirect(list_half(s)))
+        nc.vector.tensor_copy(stressed_first[:], words[1, 0][:].indirect(offsets[:]))
+        for s in range(J_PASSES):
+            nc.vector.tensor_copy(second_words[1][s][:], words[1, 1][:].indirect(list_half(s)))
+
+        wd_raw.extend(load_wd(n, 3 + n) for n in range(1, N_TILES - 1))
+        w4_plane = slot_tile([P, K_PASSES, N // 4], I32, "w4_plane", 0, SLOT // 2)
+        nc.gpsimd.memset(w4_plane[:], 0)
+        for q in range(QUADRANTS):
+            nc.sync.dma_start(
+                w4_plane[32 * q : 32 * q + 4, :, :],
+                w4_scales[:, 4 * q : 4 * q + 4, :].rearrange("a r c -> r a c").bitcast(I32),
+            )
+        wd_raw.append(load_wd(N_TILES - 1, LAST_SLOT))
+        w4_codes = slot_tile([P, K_PASSES, 2 * N], U8, "w4_codes", 1)
+        nc.sync.dma_start(w4_codes[:].bitcast(I32), w4_words.rearrange("a p c -> p a c").bitcast(I32))
 
         def picked_words(t, a, s):
-            return first_words[t][:, s * PASS : (s + 1) * PASS] if a == 0 else second_words[t][s][:]
+            if a == 1:
+                return second_words[t][s][:]
+            return calm_first[s][:] if t == 0 else stressed_first[:, s * PASS : (s + 1) * PASS]
 
         def picked_plane(t, a, s):
-            rows = calm_scales[:, s * PASS : (s + 1) * PASS] if t == 0 else stressed_scales[s][:]
-            return rows[4 * a : P, :]
+            return planes[t][a][:].bitcast(U8)[PLANE_AT[t] + 4 * a : P, s * PASS : (s + 1) * PASS]
 
         def response(t, chunk, sign, dst, acc):
             s, mt = chunk
@@ -180,23 +203,27 @@ def tile_list_regime_spread_hedge_kernel(
         calm = [keep.tile([P, PACK, P], F32, name="calm%d_%d" % chunk) for chunk in chunks]
 
         h_early = keep.tile([P, POOL_CHUNKS * P, PACK], BF16, name="h_early", align_bytes=64)
-        h_late = reuse.tile([P, (len(chunks) - POOL_CHUNKS) * P, PACK], BF16, name="h_late", align_bytes=64, offset=0)
+        h_late = slot_tile([P, (len(chunks) - POOL_CHUNKS) * P, PACK], BF16, "h_late", LAST_SLOT)
 
         def h_bf(first, many):
             if first < POOL_CHUNKS:
                 return h_early[:, first * P : (first + many) * P, :]
             return h_late[:, (first - POOL_CHUNKS) * P : (first - POOL_CHUNKS + many) * P, :]
 
-        codes = reuse.tile([P, J_PASSES * M + N_TILES * J_PASSES * P], U32, name="codes", align_bytes=64, offset=3 * T)
+        codes = slot_tile([P, J_PASSES * M + N_TILES * J_PASSES * P], U32, "codes", LAST_SLOT, 3 * T)
         h_codes = codes[:, 0 : J_PASSES * M]
         h_plane = keep.tile([P, J_PASSES * M], U8, name="h_plane", align_bytes=64)
 
-        for c, chunk in enumerate(chunks):
-            response(0, chunk, 1.0, calm[c], bank_tile([P, PASS], "calm_sum%d" % c, c))
+        calm_order = sorted(range(len(chunks)), key=lambda c: chunks[c])
+        calm_bank = {c: place % CALM_BANKS for place, c in enumerate(calm_order)}
+        for c in calm_order:
+            response(0, chunks[c], 1.0, calm[c], bank_tile([P, PASS], "calm_sum%d" % c, calm_bank[c]))
 
-        sum_bank = [BANKS - SUM_BANKS + c % SUM_BANKS for c in range(len(chunks))]
         opened_early = [c for c in range(len(chunks)) if c != ADDED_CHUNK][: BANKS - SUM_BANKS]
-        diff_bank = {c: bank for bank, c in enumerate(opened_early)}
+        diff_bank = {c: calm_bank[c] for c in opened_early}
+        diff_bank[0] = CALM_BANKS
+        turning = [CALM_BANKS + 1, calm_bank[last - 1], calm_bank[last]]
+        sum_bank = [turning[c % SUM_BANKS] for c in range(len(chunks))]
         diff_bank[ADDED_CHUNK] = diff_bank[0]
         diff_bank[last - 1] = diff_bank[ADDED_CHUNK + 1]
         diff_bank[last] = diff_bank[ADDED_CHUNK]
@@ -223,7 +250,7 @@ def tile_list_regime_spread_hedge_kernel(
                     is_transpose=True,
                 )
 
-        for c in opened_early:
+        for c in sorted(opened_early, key=calm_order.index):
             turn_onto_diff(c, calm[c], True, False)
 
         def spread(c):
@@ -286,20 +313,19 @@ def tile_list_regime_spread_hedge_kernel(
         def open_total(pair, half, bank):
             tile = bank_tile([P, 2, M // 2], "total%d_%d" % (pair, half), bank)
             totals[pair, half] = tile
+            cols = slice(half * M // 2, (half + 1) * M // 2)
             for u in range(2):
                 n = 2 * pair + u
-                for v in range(2):
-                    cols = slice((2 * half + v) * P, (2 * half + v + 1) * P)
-                    for a in range(K_PASSES):
-                        nc.tensor.matmul_mx(
-                            out=tile[:, u, v * P : (v + 1) * P],
-                            lhsT=w4_codes[:, a, 2 * n * P : 2 * (n + 1) * P].bitcast(FP4X4),
-                            lhsT_scale=w4_plane[:, a, :].bitcast(U8)[:, n * P : (n + 1) * P],
-                            rhs=x_codes[a][:, cols].bitcast(FP8X4),
-                            rhs_scale=x_plane[a][:, cols],
-                            start=(u == 0 and v == 0 and a == 0),
-                            stop=False,
-                        )
+                for a in range(K_PASSES):
+                    nc.tensor.matmul_mx(
+                        out=tile[:, u, :],
+                        lhsT=w4_codes[:, a, 2 * n * P : 2 * (n + 1) * P].bitcast(FP4X4),
+                        lhsT_scale=w4_plane[:, a, :].bitcast(U8)[:, n * P : (n + 1) * P],
+                        rhs=x_codes[a][:, cols].bitcast(FP8X4),
+                        rhs_scale=x_plane[a][:, cols],
+                        start=(u == 0 and a == 0),
+                        stop=False,
+                    )
 
         def down(pair, first, many):
             s, mt = chunks[first]

@@ -28,8 +28,15 @@ QUADRANTS = 4
 LIST_ROWS = 16
 X_COLS = M // 2
 SLOT = 4 * T
-LAST_SLOT = 6
-GAINS_BYTES = 64
+TOUCH = 64
+AT_X_THIRD = SLOT // 2
+AT_X_LAST = SLOT + SLOT // 2 - TOUCH
+AT_CALM_SECOND = AT_X_LAST + SLOT // 2
+AT_STRESSED_FIRST = AT_CALM_SECOND + SLOT
+AT_GAINS = AT_STRESSED_FIRST + SLOT
+AT_STRESSED_SECOND = AT_GAINS + TOUCH
+AT_CALM_FIRST = AT_STRESSED_SECOND + SLOT
+AT_X_FIRST = AT_CALM_FIRST + SLOT
 ROWS_AT = (0, 64)
 PLANE_AT = (0, 8)
 BANK = 2048
@@ -61,10 +68,13 @@ def tile_list_regime_spread_hedge_kernel(
         ident = keep.tile([P, P], F32, name="ident")
         make_identity(nc, ident[:])
 
-        def slot_tile(shape, dtype, name, slot, shift=0):
-            return stream.tile(shape, dtype, name=name, align_bytes=64, offset=SLOT * slot + GAINS_BYTES * (slot > 2) + shift)
+        def slot_tile(shape, dtype, name, at):
+            return stream.tile(shape, dtype, name=name, align_bytes=64, offset=at)
 
-        scale_rows = [slot_tile([P, T // 4], I32, "scale_rows%d" % t, 2 * t + 1, -T // 2) for t in range(2)]
+        scale_rows = [
+            slot_tile([P, T // 4], I32, "scale_rows%d" % t, border - T // 2)
+            for t, border in enumerate((AT_CALM_SECOND, AT_STRESSED_SECOND))
+        ]
         for t, src in enumerate((tab_scales, tab2_scales)):
             first = ROWS_AT[t]
             nc.sync.dma_start(scale_rows[t][first : first + 32, :], src.rearrange("a q c -> (a q) c").bitcast(I32))
@@ -90,10 +100,18 @@ def tile_list_regime_spread_hedge_kernel(
             nc.sync.dma_start(tile[:], wdT[n * P : (n + 1) * P, :])
             return tile
 
-        words = {(0, 0): load_words("words0_0", tab_words[0], 4)}
-        x_raw = [slot_tile([P, PACK, M], F32, "x_raw%d" % a, 5 + a) for a in range(K_PASSES)]
-        for a in range(K_PASSES):
-            nc.sync.dma_start(x_raw[a][:], x[a * PASS : (a + 1) * PASS, :].rearrange("(p i) m -> p i m", i=PACK))
+        words = {(0, 0): load_words("words0_0", tab_words[0], AT_CALM_FIRST)}
+        x_first = slot_tile([P, PACK, M], F32, "x_first", AT_X_FIRST)
+        nc.sync.dma_start(x_first[:], x[0:PASS, :].rearrange("(p i) m -> p i m", i=PACK))
+
+        def load_x_second(half):
+            tile = slot_tile([P, PACK, X_COLS], F32, "x_second%d" % half, (AT_X_THIRD, AT_X_LAST)[half])
+            cols = slice(half * X_COLS, (half + 1) * X_COLS)
+            nc.sync.dma_start(tile[:], x[PASS:K, cols].rearrange("(p i) m -> p i m", i=PACK))
+            return tile[:]
+
+        x_raw = {(0, half): x_first[:, :, half * X_COLS : (half + 1) * X_COLS] for half in range(2)}
+        x_raw[1, 0] = load_x_second(0)
 
         picked_rows = [keep.tile([P, S], U8, name="picked_rows%d" % t, align_bytes=64) for t in range(2)]
         for t in range(2):
@@ -107,16 +125,16 @@ def tile_list_regime_spread_hedge_kernel(
                     planes[t][a][PLANE_AT[t] + u : P : 32, :], picked_rows[t][row : row + 13 : 4, :].bitcast(I32)
                 )
 
-        move_rows(0, 0, 6)
-        words[0, 1] = load_words("words0_1", tab_words[1], 0)
-        move_rows(0, 6, 2)
-        words[1, 0] = load_words("words1_0", tab2_words[0], 1)
+        move_rows(0, 0, 5)
+        words[0, 1] = load_words("words0_1", tab_words[1], AT_CALM_SECOND)
+        move_rows(0, 5, 3)
+        x_raw[1, 1] = load_x_second(1)
+        words[1, 0] = load_words("words1_0", tab2_words[0], AT_STRESSED_FIRST)
         move_rows(1, 0, 4)
-        words[1, 1] = load_words("words1_1", tab2_words[1], 2)
+        words[1, 1] = load_words("words1_1", tab2_words[1], AT_STRESSED_SECOND)
         move_rows(1, 4, 4)
-        gains = slot_tile([P, J_PASSES, 2 * PACK], F32, "gains", 3, -GAINS_BYTES)
+        gains = slot_tile([P, J_PASSES, 2 * PACK], F32, "gains", AT_GAINS)
         nc.sync.dma_start(gains[:, :, 0:PACK], g.rearrange("(s p i) -> p s i", p=P, i=PACK))
-        wd_raw = [load_wd(0, 3)]
 
         def list_half(s):
             return offsets[:, s * PASS // LIST_ROWS : (s + 1) * PASS // LIST_ROWS]
@@ -136,7 +154,7 @@ def tile_list_regime_spread_hedge_kernel(
             )
             nc.scalar.activation(
                 x_bf[:].rearrange("p (c e) i -> p c i e", e=4),
-                x_raw[a][:, :, cols].rearrange("p i (c e) -> p c i e", e=4),
+                x_raw[a, half].rearrange("p i (c e) -> p c i e", e=4),
                 ACT.Copy,
             )
             nc.vector.quantize_mx(
@@ -151,25 +169,22 @@ def tile_list_regime_spread_hedge_kernel(
         calm_first.append(early.tile([P, PASS], U32, name="calm_first1", align_bytes=64, offset=0))
         nc.vector.tensor_copy(calm_first[1][:], words[0, 0][:].indirect(list_half(1)))
         quantise_x(0, 1)
-        for half in range(2):
-            quantise_x(1, half)
+        quantise_x(1, 0)
         for s in range(J_PASSES):
             nc.vector.tensor_copy(second_words[0][s][:], words[0, 1][:].indirect(list_half(s)))
+        quantise_x(1, 1)
         nc.vector.tensor_copy(stressed_first[:], words[1, 0][:].indirect(offsets[:]))
         for s in range(J_PASSES):
             nc.vector.tensor_copy(second_words[1][s][:], words[1, 1][:].indirect(list_half(s)))
 
-        wd_raw.extend(load_wd(n, 3 + n) for n in range(1, N_TILES - 1))
-        w4_plane = slot_tile([P, K_PASSES, N // 4], I32, "w4_plane", 0, SLOT // 2)
+        wd_raw = [load_wd(n, slot) for n, slot in enumerate((AT_CALM_FIRST, AT_X_FIRST, 0))]
+        w4_plane = early.tile([P, K_PASSES, N // 4], I32, name="w4_plane", align_bytes=64, offset=6 * PACK * X_COLS)
         nc.gpsimd.memset(w4_plane[:], 0)
         for q in range(QUADRANTS):
             nc.sync.dma_start(
                 w4_plane[32 * q : 32 * q + 4, :, :],
                 w4_scales[:, 4 * q : 4 * q + 4, :].rearrange("a r c -> r a c").bitcast(I32),
             )
-        wd_raw.append(load_wd(N_TILES - 1, LAST_SLOT))
-        w4_codes = slot_tile([P, K_PASSES, 2 * N], U8, "w4_codes", 1)
-        nc.sync.dma_start(w4_codes[:].bitcast(I32), w4_words.rearrange("a p c -> p a c").bitcast(I32))
 
         def picked_words(t, a, s):
             if a == 1:
@@ -200,21 +215,23 @@ def tile_list_regime_spread_hedge_kernel(
 
         chunks = [(s, 2 * half + u) for half in range(2) for s in range(J_PASSES) for u in range(2)]
         last = len(chunks) - 1
-        calm = [keep.tile([P, PACK, P], F32, name="calm%d_%d" % chunk) for chunk in chunks]
+        held = [slot_tile([P, 2, PACK, P], F32, "calm_held%d" % k, SLOT + k * SLOT // 2) for k in range(2)]
+        calm = [held[c // 2][:, c % 2, :, :] for c in range(4)]
+        calm.extend(keep.tile([P, PACK, P], F32, name="calm%d_%d" % chunk)[:] for chunk in chunks[4:])
 
         h_early = keep.tile([P, POOL_CHUNKS * P, PACK], BF16, name="h_early", align_bytes=64)
-        h_late = slot_tile([P, (len(chunks) - POOL_CHUNKS) * P, PACK], BF16, "h_late", LAST_SLOT)
+        h_late = slot_tile([P, (len(chunks) - POOL_CHUNKS) * P, PACK], BF16, "h_late", AT_CALM_SECOND + TOUCH)
 
         def h_bf(first, many):
             if first < POOL_CHUNKS:
                 return h_early[:, first * P : (first + many) * P, :]
             return h_late[:, (first - POOL_CHUNKS) * P : (first - POOL_CHUNKS + many) * P, :]
 
-        codes = slot_tile([P, J_PASSES * M + N_TILES * J_PASSES * P], U32, "codes", LAST_SLOT, 3 * T)
+        codes = slot_tile([P, J_PASSES * M + N_TILES * J_PASSES * P], U32, "codes", AT_CALM_SECOND + TOUCH + 3 * T)
         h_codes = codes[:, 0 : J_PASSES * M]
         h_plane = keep.tile([P, J_PASSES * M], U8, name="h_plane", align_bytes=64)
 
-        calm_order = sorted(range(len(chunks)), key=lambda c: chunks[c])
+        calm_order = list(range(len(chunks)))
         calm_bank = {c: place % CALM_BANKS for place, c in enumerate(calm_order)}
         for c in calm_order:
             response(0, chunks[c], 1.0, calm[c], bank_tile([P, PASS], "calm_sum%d" % c, calm_bank[c]))
@@ -252,6 +269,10 @@ def tile_list_regime_spread_hedge_kernel(
 
         for c in sorted(opened_early, key=calm_order.index):
             turn_onto_diff(c, calm[c], True, False)
+
+        wd_raw.append(load_wd(N_TILES - 1, AT_CALM_SECOND + TOUCH))
+        w4_codes = slot_tile([P, K_PASSES, 2 * N], U8, "w4_codes", AT_STRESSED_SECOND)
+        nc.sync.dma_start(w4_codes[:].bitcast(I32), w4_words.rearrange("a p c -> p a c").bitcast(I32))
 
         def spread(c):
             s, mt = chunks[c]

@@ -113,9 +113,12 @@ def tile_list_regime_spread_hedge_kernel(
         x_raw = {(0, half): x_first[:, :, half * X_COLS : (half + 1) * X_COLS] for half in range(2)}
         x_raw[1, 0] = load_x_second(0)
 
+        def dealt(tile):
+            return tile[:].rearrange("k (s i p) -> k s p i", i=PACK, p=P)
+
         picked_rows = [keep.tile([P, S], U8, name="picked_rows%d" % t, align_bytes=64) for t in range(2)]
         for t in range(2):
-            nc.vector.tensor_copy(picked_rows[t][:], scale_rows[t][:].bitcast(U8).indirect(offsets[:]))
+            nc.vector.tensor_copy(dealt(picked_rows[t]), scale_rows[t][:].bitcast(U8).indirect(offsets[:]))
 
         def move_rows(t, first, many):
             for u in range(first, first + many):
@@ -164,18 +167,18 @@ def tile_list_regime_spread_hedge_kernel(
             )
 
         calm_first = [keep.tile([P, PASS], U32, name="calm_first0", align_bytes=64)]
-        nc.vector.tensor_copy(calm_first[0][:], words[0, 0][:].indirect(list_half(0)))
+        nc.vector.tensor_copy(dealt(calm_first[0]), words[0, 0][:].indirect(list_half(0)))
         quantise_x(0, 0)
         calm_first.append(early.tile([P, PASS], U32, name="calm_first1", align_bytes=64, offset=0))
-        nc.vector.tensor_copy(calm_first[1][:], words[0, 0][:].indirect(list_half(1)))
+        nc.vector.tensor_copy(dealt(calm_first[1]), words[0, 0][:].indirect(list_half(1)))
         quantise_x(0, 1)
         quantise_x(1, 0)
         for s in range(J_PASSES):
-            nc.vector.tensor_copy(second_words[0][s][:], words[0, 1][:].indirect(list_half(s)))
+            nc.vector.tensor_copy(dealt(second_words[0][s]), words[0, 1][:].indirect(list_half(s)))
         quantise_x(1, 1)
-        nc.vector.tensor_copy(stressed_first[:], words[1, 0][:].indirect(offsets[:]))
+        nc.vector.tensor_copy(dealt(stressed_first), words[1, 0][:].indirect(offsets[:]))
         for s in range(J_PASSES):
-            nc.vector.tensor_copy(second_words[1][s][:], words[1, 1][:].indirect(list_half(s)))
+            nc.vector.tensor_copy(dealt(second_words[1][s]), words[1, 1][:].indirect(list_half(s)))
 
         wd_raw = [load_wd(n, slot) for n, slot in enumerate((AT_CALM_FIRST, AT_X_FIRST, 0))]
         w4_plane = early.tile([P, K_PASSES, N // 4], I32, name="w4_plane", align_bytes=64, offset=6 * PACK * X_COLS)
@@ -206,12 +209,7 @@ def tile_list_regime_spread_hedge_kernel(
                     start=(a == 0),
                     stop=(a == K_PASSES - 1),
                 )
-            nc.scalar.activation(
-                dst[:].rearrange("m i (c e) -> m c i e", e=2),
-                acc[:].rearrange("m (c e i) -> m c i e", e=2, i=PACK),
-                ACT.Tanh,
-                scale=sign,
-            )
+            nc.scalar.activation(dst[:].rearrange("m i p -> m (i p)"), acc[:], ACT.Tanh, scale=sign)
 
         chunks = [(s, 2 * half + u) for half in range(2) for s in range(J_PASSES) for u in range(2)]
         last = len(chunks) - 1

@@ -284,12 +284,21 @@ def tile_list_regime_spread_hedge_kernel(
                 turn_onto_diff(c, stressed[c], False, True)
             nc.scalar.activation(size[:, s, mt * P : (mt + 1) * P, :], diffs[c][:].rearrange("p i m -> p m i"), ACT.Abs)
 
+        spread_gains = keep.tile([P, J_PASSES, P, PACK], F32, name="spread_gains")
+        nc.gpsimd.tensor_scalar(
+            spread_gains[:],
+            gains[:, :, 0:PACK].unsqueeze(2).to_broadcast([P, J_PASSES, P, PACK]),
+            1.0,
+            0.0,
+            ALU.mult,
+            ALU.add,
+        )
+
         def weigh(c):
             s, mt = chunks[c]
             engine = nc.gpsimd if c < POOL_CHUNKS else nc.vector
             cols = slice(mt * P, (mt + 1) * P)
-            gain = gains[:, s : s + 1, 0:PACK].to_broadcast([P, P, PACK])
-            engine.tensor_tensor(h_bf(c, 1), size[:, s, cols, :], gain, ALU.mult)
+            engine.tensor_tensor(h_bf(c, 1), size[:, s, cols, :], spread_gains[:, s, :, :], ALU.mult)
 
         def quantise_h(first, many):
             cols = slice(first * P, (first + many) * P)

@@ -378,7 +378,7 @@ def tile_list_regime_spread_hedge_kernel(
             rows = out[2 * pair * P : 2 * (pair + 1) * P, 0 : M // 2]
             nc.sync.dma_start(rows.rearrange("(u p) m -> p u m", p=P), result[:])
 
-        spread_order = [ADDED_CHUNK + 1, ADDED_CHUNK] + list(range(ADDED_CHUNK + 2, last))
+        spread_order = [ADDED_CHUNK + 1, ADDED_CHUNK] + list(range(ADDED_CHUNK + 2, last - 1))
         for c in range(SUM_BANKS):
             stress(c)
         spread(0)
@@ -387,18 +387,19 @@ def tile_list_regime_spread_hedge_kernel(
                 stress(d)
             for d in spread_order[c - SUM_BANKS : c - SUM_BANKS + 2]:
                 spread(d)
-        spread(last)
-
         turn_wd(0, diff_bank[3])
         turn_wd(1, sum_bank[5])
+        collect_wd(0)
+        collect_wd(1)
+        spread(last - 1)
+        spread(last)
+
         turn_wd(2, diff_bank[5])
         open_total(0, 0, diff_bank[4])
         open_total(1, 0, sum_bank[6])
-        turn_wd(3, diff_bank[7])
-        open_total(0, 1, sum_bank[7])
-        open_total(1, 1, diff_bank[6])
-        for n in range(N_TILES):
-            collect_wd(n)
+        turn_wd(3, sum_bank[7])
+        collect_wd(2)
+        collect_wd(3)
 
         for c in range(POOL_CHUNKS):
             weigh(c)
@@ -411,13 +412,15 @@ def tile_list_regime_spread_hedge_kernel(
 
         quantise_h(0, 4)
         finish_first_half(0)
+        open_total(0, 1, diff_bank[5])
+        open_total(1, 1, sum_bank[7])
         weigh(5)
-        finish_first_half(1)
         quantise_h(4, 1)
         quantise_h(5, 1)
-        for pair in range(2):
-            down(pair, 4, 2)
+        down(0, 4, 2)
         weigh(6)
+        finish_first_half(1)
+        down(1, 4, 2)
         weigh(7)
         for c in (last - 1, last):
             quantise_h(c, 1)

@@ -37,7 +37,7 @@ AT_GAINS = AT_STRESSED_FIRST + SLOT
 AT_STRESSED_SECOND = AT_GAINS + TOUCH
 AT_CALM_FIRST = AT_STRESSED_SECOND + SLOT
 AT_X_FIRST = AT_CALM_FIRST + SLOT
-ROWS_AT = (0, 64)
+ROWS_AT = (96, 96)
 PLANE_AT = (0, 8)
 BANK = 2048
 BANKS = 8
@@ -78,17 +78,15 @@ def tile_list_regime_spread_hedge_kernel(
         for t, src in enumerate((tab_scales, tab2_scales)):
             first = ROWS_AT[t]
             nc.sync.dma_start(scale_rows[t][first : first + 32, :], src.rearrange("a q c -> (a q) c").bitcast(I32))
-        nc.vector.memset(scale_rows[0][32:64, :], 0)
-        nc.vector.memset(scale_rows[0][64:P, :], 0)
-        nc.vector.memset(scale_rows[1][0:64, :], 0)
-        nc.vector.memset(scale_rows[1][96:P, :], 0)
+        for t in range(2):
+            nc.vector.memset(scale_rows[t][0 : ROWS_AT[t], :], 0)
         planes = [
             [keep.tile([P, S // 4], I32, name="plane%d_%d" % (t, a), align_bytes=64) for a in range(K_PASSES)]
             for t in range(2)
         ]
         for t in range(2):
             for a in range(K_PASSES):
-                nc.gpsimd.memset(planes[t][a][:], 0)
+                nc.vector.memset(planes[t][a][:], 0)
 
         def load_words(name, src, slot):
             tile = slot_tile([P, T], U32, name, slot)

@@ -267,8 +267,9 @@ def tile_list_regime_spread_hedge_kernel(
             turn_onto_diff(c, calm[c], True, False)
 
         wd_raw.append(load_wd(N_TILES - 1, AT_CALM_SECOND + TOUCH))
-        w4_codes = slot_tile([P, K_PASSES, 2 * N], U8, "w4_codes", AT_STRESSED_SECOND)
-        nc.sync.dma_start(w4_codes[:].bitcast(I32), w4_words.rearrange("a p c -> p a c").bitcast(I32))
+        w4_codes = [slot_tile([P, 2 * N], U8, "w4_codes%d" % a, AT_STRESSED_SECOND + 2 * N * a) for a in range(K_PASSES)]
+        for a in range(K_PASSES):
+            nc.sync.dma_start(w4_codes[a][:].bitcast(I32), w4_words[a].bitcast(I32))
 
         def spread(c):
             s, mt = chunks[c]
@@ -340,12 +341,12 @@ def tile_list_regime_spread_hedge_kernel(
             tile = bank_tile([P, 2, M // 2], "total%d_%d" % (pair, half), bank)
             totals[pair, half] = tile
             cols = slice(half * M // 2, (half + 1) * M // 2)
-            for u in range(2):
-                n = 2 * pair + u
-                for a in range(K_PASSES):
+            for a in range(K_PASSES):
+                for u in range(2):
+                    n = 2 * pair + u
                     nc.tensor.matmul_mx(
                         out=tile[:, u, :],
-                        lhsT=w4_codes[:, a, 2 * n * P : 2 * (n + 1) * P].bitcast(FP4X4),
+                        lhsT=w4_codes[a][:, 2 * n * P : 2 * (n + 1) * P].bitcast(FP4X4),
                         lhsT_scale=w4_plane[:, a, :].bitcast(U8)[:, n * P : (n + 1) * P],
                         rhs=x_codes[a][:, cols].bitcast(FP8X4),
                         rhs_scale=x_plane[a][:, cols],
@@ -394,8 +395,8 @@ def tile_list_regime_spread_hedge_kernel(
 
         turn_wd(2, diff_bank[5])
         open_total(0, 0, diff_bank[4])
-        open_total(1, 0, sum_bank[6])
         turn_wd(3, sum_bank[7])
+        open_total(1, 0, sum_bank[6])
         collect_wd(2)
         collect_wd(3)
 

@@ -195,7 +195,7 @@ def tile_list_regime_spread_hedge_kernel(
         def picked_plane(t, a, s):
             return planes[t][a][:].bitcast(U8)[PLANE_AT[t] + 4 * a : P, s * PASS : (s + 1) * PASS]
 
-        def response(t, chunk, sign, dst, acc):
+        def respond(t, chunk, acc):
             s, mt = chunk
             for a in range(K_PASSES):
                 nc.tensor.matmul_mx(
@@ -207,6 +207,9 @@ def tile_list_regime_spread_hedge_kernel(
                     start=(a == 0),
                     stop=(a == K_PASSES - 1),
                 )
+
+        def response(t, chunk, sign, dst, acc):
+            respond(t, chunk, acc)
             nc.scalar.activation(dst[:].rearrange("m i p -> m (i p)"), acc[:], ACT.Tanh, scale=sign)
 
         chunks = [(s, 2 * half + u) for half in range(2) for s in range(J_PASSES) for u in range(2)]
@@ -390,15 +393,17 @@ def tile_list_regime_spread_hedge_kernel(
         turn_wd(1, sum_bank[5])
         collect_wd(0)
         collect_wd(1)
+        respond(1, chunks[last - 1], bank_tile([P, PASS], "warm_up", sum_bank[last - 1]))
         spread(last - 1)
-        spread(last)
 
         turn_wd(2, diff_bank[5])
         open_total(0, 0, diff_bank[4])
-        turn_wd(3, sum_bank[7])
         open_total(1, 0, sum_bank[6])
+        turn_wd(3, sum_bank[7])
+        open_total(0, 1, diff_bank[6])
         collect_wd(2)
         collect_wd(3)
+        spread(last)
 
         for c in range(POOL_CHUNKS):
             weigh(c)
@@ -411,15 +416,14 @@ def tile_list_regime_spread_hedge_kernel(
 
         quantise_h(0, 4)
         finish_first_half(0)
-        open_total(0, 1, diff_bank[5])
-        open_total(1, 1, sum_bank[7])
+        open_total(1, 1, diff_bank[5])
         weigh(5)
         quantise_h(4, 1)
         quantise_h(5, 1)
         down(0, 4, 2)
-        weigh(6)
         finish_first_half(1)
         down(1, 4, 2)
+        weigh(6)
         weigh(7)
         for c in (last - 1, last):
             quantise_h(c, 1)

@@ -212,7 +212,8 @@ def tile_list_regime_spread_hedge_kernel(
             respond(t, chunk, acc)
             nc.scalar.activation(dst[:].rearrange("m i p -> m (i p)"), acc[:], ACT.Tanh, scale=sign)
 
-        chunks = [(s, 2 * half + u) for half in range(2) for s in range(J_PASSES) for u in range(2)]
+        chunks = [(s, mt) for s in range(J_PASSES) for mt in range(2)]
+        chunks.extend((s, mt) for mt in range(2, M_TILES) for s in range(J_PASSES))
         last = len(chunks) - 1
         held = [slot_tile([P, 2, PACK, P], F32, "calm_held%d" % k, SLOT + k * SLOT // 2) for k in range(2)]
         calm = [held[c // 2][:, c % 2, :, :] for c in range(4)]
@@ -338,12 +339,13 @@ def tile_list_regime_spread_hedge_kernel(
                 in_=wd_in[pair][:].rearrange("p t s n u -> p (t s n u)").bitcast(BF16),
             )
 
+        parts = [slice(0, 2 * P), slice(2 * P, 3 * P), slice(3 * P, 4 * P)]
         totals = {}
 
-        def open_total(pair, half, bank):
-            tile = bank_tile([P, 2, M // 2], "total%d_%d" % (pair, half), bank)
-            totals[pair, half] = tile
-            cols = slice(half * M // 2, (half + 1) * M // 2)
+        def open_total(pair, part, bank):
+            cols = parts[part]
+            tile = bank_tile([P, 2, cols.stop - cols.start], "total%d_%d" % (pair, part), bank)
+            totals[pair, part] = tile
             for a in range(K_PASSES):
                 for u in range(2):
                     n = 2 * pair + u
@@ -359,25 +361,25 @@ def tile_list_regime_spread_hedge_kernel(
 
         def down(pair, first, many):
             s, mt = chunks[first]
-            half, v = divmod(mt, 2)
-            closes = s == J_PASSES - 1 and v + many == 2
+            part = max(mt - 1, 0)
             cols = slice(first * P, (first + many) * P)
             for u in range(2):
                 n = 2 * pair + u
                 nc.tensor.matmul_mx(
-                    out=totals[pair, half][:, u, v * P : (v + many) * P],
+                    out=totals[pair, part][:, u, :],
                     lhsT=wd_codes[:, n, s * P : (s + 1) * P].bitcast(FP8X4),
                     lhsT_scale=wd_plane[:, n, s * P : (s + 1) * P],
                     rhs=h_codes[:, cols].bitcast(FP8X4),
                     rhs_scale=h_plane[:, cols],
                     start=False,
-                    stop=(closes and u == 1),
+                    stop=(s == J_PASSES - 1 and u == 1),
                 )
 
-        def store_first_half(pair):
-            result = ring.tile([P, 2, M // 2], F32, name="result", bufs=2)
-            nc.scalar.copy(result[:], totals[pair, 0][:])
-            rows = out[2 * pair * P : 2 * (pair + 1) * P, 0 : M // 2]
+        def store(pair, part, copy):
+            cols = parts[part]
+            result = keep.tile([P, 2, cols.stop - cols.start], F32, name="result%d_%d" % (pair, part))
+            copy(result[:], totals[pair, part][:])
+            rows = out[2 * pair * P : 2 * (pair + 1) * P, cols]
             nc.sync.dma_start(rows.rearrange("(u p) m -> p u m", p=P), result[:])
 
         spread_order = [ADDED_CHUNK + 1, ADDED_CHUNK] + list(range(ADDED_CHUNK + 2, last - 1))
@@ -393,8 +395,8 @@ def tile_list_regime_spread_hedge_kernel(
         turn_wd(1, sum_bank[5])
         collect_wd(0)
         collect_wd(1)
-        respond(1, chunks[last - 1], bank_tile([P, PASS], "warm_up", sum_bank[last - 1]))
         spread(last - 1)
+        respond(1, chunks[last - 1], bank_tile([P, PASS], "warm_up", sum_bank[last - 1]))
 
         turn_wd(2, diff_bank[5])
         open_total(0, 0, diff_bank[4])
@@ -402,6 +404,7 @@ def tile_list_regime_spread_hedge_kernel(
         turn_wd(3, sum_bank[7])
         open_total(0, 1, diff_bank[6])
         collect_wd(2)
+        open_total(1, 1, diff_bank[5])
         collect_wd(3)
         spread(last)
 
@@ -412,26 +415,26 @@ def tile_list_regime_spread_hedge_kernel(
             quantise_wd(pair)
             for s in range(J_PASSES):
                 down(pair, 2 * s, 2)
-            store_first_half(pair)
+            store(pair, 0, nc.scalar.copy)
 
         quantise_h(0, 4)
         finish_first_half(0)
-        open_total(1, 1, diff_bank[5])
+        open_total(0, 2, sum_bank[7])
+        open_total(1, 2, diff_bank[7])
         weigh(5)
-        quantise_h(4, 1)
-        quantise_h(5, 1)
-        down(0, 4, 2)
+        for c in (4, 5):
+            quantise_h(c, 1)
+            down(0, c, 1)
+        store(0, 1, nc.scalar.copy)
         finish_first_half(1)
-        down(1, 4, 2)
+        for c in (4, 5):
+            down(1, c, 1)
+        store(1, 1, nc.scalar.copy)
         weigh(6)
         weigh(7)
         for c in (last - 1, last):
             quantise_h(c, 1)
             for pair in range(2):
                 down(pair, c, 1)
-        for u in range(2):
-            for pair, copy in enumerate((nc.scalar.copy, nc.vector.tensor_copy)):
-                n = 2 * pair + u
-                tile_out = ring.tile([P, M // 2], F32, name="tile_out", bufs=N_TILES)
-                copy(tile_out[:], totals[pair, 1][:, u, :])
-                nc.sync.dma_start(out[n * P : (n + 1) * P, M // 2 : M], tile_out[:])
+        for pair, copy in enumerate((nc.scalar.copy, nc.vector.tensor_copy)):
+            store(pair, 2, copy)

@@ -396,7 +396,6 @@ def tile_list_regime_spread_hedge_kernel(
         collect_wd(0)
         collect_wd(1)
         spread(last - 1)
-        respond(1, chunks[last - 1], bank_tile([P, PASS], "warm_up", sum_bank[last - 1]))
 
         turn_wd(2, diff_bank[5])
         open_total(0, 0, diff_bank[4])

from contextlib import ExitStack

import concourse.mybir as mybir
from concourse.masks import make_identity

K, T, S, M, N = 1024, 2048, 1024, 512, 512
FLOPS = 2 * (2 * K * S * M + S * N * M + K * N * M)

F32 = mybir.dt.float32
BF16 = mybir.dt.bfloat16
I32 = mybir.dt.int32
U32 = mybir.dt.uint32
U16 = mybir.dt.uint16
U8 = mybir.dt.uint8
FP8X4 = mybir.dt.float8_e4m3fn_x4
FP4X4 = mybir.dt.float4_e2m1fn_x4
ACT = mybir.ActivationFunctionType
ALU = mybir.AluOpType

P = 128
PACK = 4
PASS = P * PACK
K_PASSES = K // PASS
J_PASSES = S // PASS
M_TILES = M // P
N_TILES = N // P
QUADRANTS = 4
LIST_ROWS = 16
X_COLS = M // 2
SLOT = 4 * T
TOUCH = 64
AT_X_THIRD = SLOT // 2
AT_X_LAST = SLOT + SLOT // 2 - TOUCH
AT_CALM_SECOND = AT_X_LAST + SLOT // 2
AT_STRESSED_FIRST = AT_CALM_SECOND + SLOT
AT_GAINS = AT_STRESSED_FIRST + SLOT
AT_STRESSED_SECOND = AT_GAINS + TOUCH
AT_CALM_FIRST = AT_STRESSED_SECOND + SLOT
AT_X_FIRST = AT_CALM_FIRST + SLOT
ROWS_AT = (96, 96)
PLANE_AT = (0, 8)
BANK = 2048
BANKS = 8
CALM_BANKS = 6
SUM_BANKS = 3
POOL_CHUNKS = 5
ADDED_CHUNK = 1
STRESSED_BUFS = 5


def tile_list_regime_spread_hedge_kernel(
    tc, x, tab_words, tab_scales, tab2_words, tab2_scales, offs, g, wdT, w4_words, w4_scales, out
):
    nc = tc.nc
    with ExitStack() as ctx:
        keep = ctx.enter_context(tc.tile_pool(name="keep", bufs=1))
        ring = ctx.enter_context(tc.tile_pool(name="ring", bufs=1))
        psum = ctx.enter_context(tc.psum_pool(name="psum", bufs=1))
        stream = ctx.enter_context(tc.tile_pool(name="stream", bufs=1))
        early = ctx.enter_context(tc.tile_pool(name="early", bufs=1))

        def bank_tile(shape, name, bank):
            return psum.tile(shape, F32, name=name, offset=BANK * bank)

        offsets = keep.tile([P, S // LIST_ROWS], U16, name="offsets")
        nc.sync.dma_start(offsets[:], offs)

        ident = keep.tile([P, P], F32, name="ident")
        make_identity(nc, ident[:])

        def slot_tile(shape, dtype, name, at):
            return stream.tile(shape, dtype, name=name, align_bytes=64, offset=at)

        scale_rows = [
            slot_tile([P, T // 4], I32, "scale_rows%d" % t, border - T // 2)
            for t, border in enumerate((AT_CALM_SECOND, AT_STRESSED_SECOND))
        ]
        for t, src in enumerate((tab_scales, tab2_scales)):
            first = ROWS_AT[t]
            nc.sync.dma_start(scale_rows[t][first : first + 32, :], src.rearrange("a q c -> (a q) c").bitcast(I32))
        for t in range(2):
            nc.vector.memset(scale_rows[t][0 : ROWS_AT[t], :], 0)
        planes = [
            [keep.tile([P, S // 4], I32, name="plane%d_%d" % (t, a), align_bytes=64) for a in range(K_PASSES)]
            for t in range(2)
        ]
        for t in range(2):
            for a in range(K_PASSES):
                nc.vector.memset(planes[t][a][:], 0)

        def load_words(name, src, slot):
            tile = slot_tile([P, T], U32, name, slot)
            nc.sync.dma_start(tile[:].bitcast(I32), src.rearrange("p c i -> p (c i)").bitcast(I32))
            return tile

        def load_wd(n, slot):
            tile = slot_tile([P, T], F32, "wd_raw%d" % n, slot)
            nc.sync.dma_start(tile[:], wdT[n * P : (n + 1) * P, :])
            return tile

        words = {(0, 0): load_words("words0_0", tab_words[0], AT_CALM_FIRST)}
        x_first = slot_tile([P, PACK, M], F32, "x_first", AT_X_FIRST)
        nc.sync.dma_start(x_first[:], x[0:PASS, :].rearrange("(p i) m -> p i m", i=PACK))

        def load_x_second(half):
            tile = slot_tile([P, PACK, X_COLS], F32, "x_second%d" % half, (AT_X_THIRD, AT_X_LAST)[half])
            cols = slice(half * X_COLS, (half + 1) * X_COLS)
            nc.sync.dma_start(tile[:], x[PASS:K, cols].rearrange("(p i) m -> p i m", i=PACK))
            return tile[:]

        x_raw = {(0, half): x_first[:, :, half * X_COLS : (half + 1) * X_COLS] for half in range(2)}
        x_raw[1, 0] = load_x_second(0)

        def dealt(tile):
            return tile[:].rearrange("k (s i p) -> k s p i", i=PACK, p=P)

        picked_rows = [keep.tile([P, S], U8, name="picked_rows%d" % t, align_bytes=64) for t in range(2)]
        for t in range(2):
            nc.vector.tensor_copy(dealt(picked_rows[t]), scale_rows[t][:].bitcast(U8).indirect(offsets[:]))

        def move_rows(t, first, many):
            for u in range(first, first + many):
                a, r = divmod(u, 4)
                row = ROWS_AT[t] + 16 * a + r
                nc.sync.dma_start(
                    planes[t][a][PLANE_AT[t] + u : P : 32, :], picked_rows[t][row : row + 13 : 4, :].bitcast(I32)
                )

        move_rows(0, 0, 5)
        words[0, 1] = load_words("words0_1", tab_words[1], AT_CALM_SECOND)
        move_rows(0, 5, 3)
        x_raw[1, 1] = load_x_second(1)
        words[1, 0] = load_words("words1_0", tab2_words[0], AT_STRESSED_FIRST)
        move_rows(1, 0, 4)
        words[1, 1] = load_words("words1_1", tab2_words[1], AT_STRESSED_SECOND)
        move_rows(1, 4, 4)
        gains = slot_tile([P, J_PASSES, 2 * PACK], F32, "gains", AT_GAINS)
        nc.sync.dma_start(gains[:, :, 0:PACK], g.rearrange("(s p i) -> p s i", p=P, i=PACK))

        def list_half(s):
            return offsets[:, s * PASS // LIST_ROWS : (s + 1) * PASS // LIST_ROWS]

        stressed_first = keep.tile([P, S], U32, name="stressed_first", align_bytes=64)
        second_words = [
            [keep.tile([P, PASS], U32, name="second_words%d_%d" % (t, s), align_bytes=64) for s in range(J_PASSES)]
            for t in range(2)
        ]
        x_codes = [keep.tile([P, M], U32, name="x_codes%d" % a, align_bytes=64) for a in range(K_PASSES)]
        x_plane = [keep.tile([P, M], U8, name="x_plane%d" % a, align_bytes=64) for a in range(K_PASSES)]

        def quantise_x(a, half):
            cols = slice(half * X_COLS, (half + 1) * X_COLS)
            x_bf = early.tile(
                [P, X_COLS, PACK], BF16, name="x_bf%d_%d" % (a, half), align_bytes=64, offset=2 * PACK * X_COLS * (2 * a + half)
            )
            nc.scalar.activation(
                x_bf[:].rearrange("p (c e) i -> p c i e", e=4),
                x_raw[a, half].rearrange("p i (c e) -> p c i e", e=4),
                ACT.Copy,
            )
            nc.vector.quantize_mx(
                out=x_codes[a][:, cols].bitcast(FP8X4),
                scales=x_plane[a][:, cols],
                in_=x_bf[:].rearrange("p m i -> p (m i)"),
            )

        calm_first = [keep.tile([P, PASS], U32, name="calm_first0", align_bytes=64)]
        nc.vector.tensor_copy(dealt(calm_first[0]), words[0, 0][:].indirect(list_half(0)))
        quantise_x(0, 0)
        calm_first.append(early.tile([P, PASS], U32, name="calm_first1", align_bytes=64, offset=0))
        nc.vector.tensor_copy(dealt(calm_first[1]), words[0, 0][:].indirect(list_half(1)))
        quantise_x(0, 1)
        quantise_x(1, 0)
        for s in range(J_PASSES):
            nc.vector.tensor_copy(dealt(second_words[0][s]), words[0, 1][:].indirect(list_half(s)))
        quantise_x(1, 1)
        nc.vector.tensor_copy(dealt(stressed_first), words[1, 0][:].indirect(offsets[:]))
        for s in range(J_PASSES):
            nc.vector.tensor_copy(dealt(second_words[1][s]), words[1, 1][:].indirect(list_half(s)))

        wd_raw = [load_wd(n, slot) for n, slot in enumerate((AT_CALM_FIRST, AT_X_FIRST, 0))]
        w4_plane = early.tile([P, K_PASSES, N // 4], I32, name="w4_plane", align_bytes=64, offset=6 * PACK * X_COLS)
        nc.gpsimd.memset(w4_plane[:], 0)
        for q in range(QUADRANTS):
            nc.sync.dma_start(
                w4_plane[32 * q : 32 * q + 4, :, :],
                w4_scales[:, 4 * q : 4 * q + 4, :].rearrange("a r c -> r a c").bitcast(I32),
            )

        def picked_words(t, a, s):
            if a == 1:
                return second_words[t][s][:]
            return calm_first[s][:] if t == 0 else stressed_first[:, s * PASS : (s + 1) * PASS]

        def picked_plane(t, a, s):
            return planes[t][a][:].bitcast(U8)[PLANE_AT[t] + 4 * a : P, s * PASS : (s + 1) * PASS]

        def respond(t, chunk, acc):
            s, mt = chunk
            for a in range(K_PASSES):
                nc.tensor.matmul_mx(
                    out=acc[:],
                    lhsT=x_codes[a][:, mt * P : (mt + 1) * P].bitcast(FP8X4),
                    lhsT_scale=x_plane[a][:, mt * P : (mt + 1) * P],
                    rhs=picked_words(t, a, s).bitcast(FP8X4),
                    rhs_scale=picked_plane(t, a, s),
                    start=(a == 0),
                    stop=(a == K_PASSES - 1),
                )

        def response(t, chunk, sign, dst, acc):
            respond(t, chunk, acc)
            nc.scalar.activation(dst[:].rearrange("m i p -> m (i p)"), acc[:], ACT.Tanh, scale=sign)

        chunks = [(s, mt) for s in range(J_PASSES) for mt in range(2)]
        chunks.extend((s, mt) for mt in range(2, M_TILES) for s in range(J_PASSES))
        last = len(chunks) - 1
        held = [slot_tile([P, 2, PACK, P], F32, "calm_held%d" % k, SLOT + k * SLOT // 2) for k in range(2)]
        calm = [held[c // 2][:, c % 2, :, :] for c in range(4)]
        calm.extend(keep.tile([P, PACK, P], F32, name="calm%d_%d" % chunk)[:] for chunk in chunks[4:])

        h_early = keep.tile([P, POOL_CHUNKS * P, PACK], BF16, name="h_early", align_bytes=64)
        h_late = slot_tile([P, (len(chunks) - POOL_CHUNKS) * P, PACK], BF16, "h_late", AT_CALM_SECOND + TOUCH)

        def h_bf(first, many):
            if first < POOL_CHUNKS:
                return h_early[:, first * P : (first + many) * P, :]
            return h_late[:, (first - POOL_CHUNKS) * P : (first - POOL_CHUNKS + many) * P, :]

        codes = slot_tile([P, J_PASSES * M + N_TILES * J_PASSES * P], U32, "codes", AT_CALM_SECOND + TOUCH + 3 * T)
        h_codes = codes[:, 0 : J_PASSES * M]
        h_plane = keep.tile([P, J_PASSES * M], U8, name="h_plane", align_bytes=64)

        calm_order = list(range(len(chunks)))
        calm_bank = {c: place % CALM_BANKS for place, c in enumerate(calm_order)}
        for c in calm_order:
            response(0, chunks[c], 1.0, calm[c], bank_tile([P, PASS], "calm_sum%d" % c, calm_bank[c]))

        opened_early = [c for c in range(len(chunks)) if c != ADDED_CHUNK][: BANKS - SUM_BANKS]
        diff_bank = {c: calm_bank[c] for c in opened_early}
        diff_bank[0] = CALM_BANKS
        turning = [CALM_BANKS + 1, calm_bank[last - 1], calm_bank[last]]
        sum_bank = [turning[c % SUM_BANKS] for c in range(len(chunks))]
        diff_bank[ADDED_CHUNK] = diff_bank[0]
        diff_bank[last - 1] = diff_bank[ADDED_CHUNK + 1]
        diff_bank[last] = diff_bank[ADDED_CHUNK]

        stressed = {}
        size = keep.tile([P, J_PASSES, M, PACK], F32, name="size")

        def stress(c):
            stressed[c] = ring.tile([P, PACK, P], F32, name="stressed", bufs=STRESSED_BUFS)
            response(1, chunks[c], -1.0, stressed[c], bank_tile([P, PASS], "stressed_sum%d" % c, sum_bank[c]))

        diffs = {}

        def turn_onto_diff(c, values, opens, closes):
            if opens:
                diffs[c] = bank_tile([P, PACK, P], "diff%d" % c, diff_bank[c])
            for i in range(PACK):
                nc.tensor.matmul(
                    diffs[c][:, i, :],
                    values[:, i, :],
                    ident[:],
                    start=(opens and i == 0),
                    stop=(closes and i == PACK - 1),
                    is_transpose=True,
                )

        for c in sorted(opened_early, key=calm_order.index):
            turn_onto_diff(c, calm[c], True, False)

        wd_raw.append(load_wd(N_TILES - 1, AT_CALM_SECOND + TOUCH))
        w4_codes = [slot_tile([P, 2 * N], U8, "w4_codes%d" % a, AT_STRESSED_SECOND + 2 * N * a) for a in range(K_PASSES)]
        for a in range(K_PASSES):
            nc.sync.dma_start(w4_codes[a][:].bitcast(I32), w4_words[a].bitcast(I32))

        def spread(c):
            s, mt = chunks[c]
            if c == ADDED_CHUNK:
                both = ring.tile([P, PACK, P], F32, name="both")
                nc.gpsimd.tensor_tensor(both[:], calm[c][:], stressed[c][:], ALU.add)
                turn_onto_diff(c, both, True, True)
            else:
                if c not in opened_early:
                    turn_onto_diff(c, calm[c], True, False)
                turn_onto_diff(c, stressed[c], False, True)
            nc.scalar.activation(size[:, s, mt * P : (mt + 1) * P, :], diffs[c][:].rearrange("p i m -> p m i"), ACT.Abs)

        spread_gains = keep.tile([P, J_PASSES, P, PACK], F32, name="spread_gains")
        nc.gpsimd.tensor_scalar(
            spread_gains[:],
            gains[:, :, 0:PACK].unsqueeze(2).to_broadcast([P, J_PASSES, P, PACK]),
            1.0,
            0.0,
            ALU.mult,
            ALU.add,
        )

        def weigh(c):
            s, mt = chunks[c]
            engine = nc.gpsimd if c < POOL_CHUNKS else nc.vector
            cols = slice(mt * P, (mt + 1) * P)
            engine.tensor_tensor(h_bf(c, 1), size[:, s, cols, :], spread_gains[:, s, :, :], ALU.mult)

        def quantise_h(first, many):
            cols = slice(first * P, (first + many) * P)
            nc.vector.quantize_mx(
                out=h_codes[:, cols].bitcast(FP8X4),
                scales=h_plane[:, cols],
                in_=h_bf(first, many).rearrange("p m i -> p (m i)"),
            )

        wd_codes = codes[:, J_PASSES * M :].rearrange("p (n c) -> p n c", n=N_TILES)
        wd_plane = keep.tile([P, N_TILES, J_PASSES * P], U8, name="wd_plane", align_bytes=64)
        wd_in = [keep.tile([P, 2, J_PASSES, P, 2], F32, name="wd_in%d" % pair, align_bytes=64) for pair in range(2)]

        wd_bf = [keep.tile([P, 2, S // PACK, 2], BF16, name="wd_bf%d" % n, align_bytes=64) for n in range(N_TILES)]
        for n in range(N_TILES):
            nc.vector.tensor_copy(wd_bf[n][:].rearrange("n u c e -> n c u e"), wd_raw[n][:].indirect(offsets[:]))

        turned = {}

        def turn_wd(n, bank):
            pairs = wd_bf[n][:].rearrange("n u c e -> n u (c e)").bitcast(F32)
            turned[n] = bank_tile([P, J_PASSES, 2, P], "turned%d" % n, bank)
            for s in range(J_PASSES):
                for u in range(2):
                    nc.tensor.transpose(turned[n][:, s, u, :], pairs[:, u, s * P : (s + 1) * P], ident[:])

        def collect_wd(n):
            nc.scalar.copy(wd_in[n // 2][:, n % 2, :, :, :], turned[n][:].rearrange("p s u n -> p s n u"))

        def quantise_wd(pair):
            tiles = slice(2 * pair, 2 * pair + 2)
            nc.vector.quantize_mx(
                out=wd_codes[:, tiles, :].rearrange("p n c -> p (n c)").bitcast(FP8X4),
                scales=wd_plane[:, tiles, :].rearrange("p n c -> p (n c)"),
                in_=wd_in[pair][:].rearrange("p t s n u -> p (t s n u)").bitcast(BF16),
            )

        parts = [slice(0, 2 * P), slice(2 * P, 3 * P), slice(3 * P, 4 * P)]
        totals = {}

        def open_total(pair, part, bank):
            cols = parts[part]
            tile = bank_tile([P, 2, cols.stop - cols.start], "total%d_%d" % (pair, part), bank)
            totals[pair, part] = tile
            for a in range(K_PASSES):
                for u in range(2):
                    n = 2 * pair + u
                    nc.tensor.matmul_mx(
                        out=tile[:, u, :],
                        lhsT=w4_codes[a][:, 2 * n * P : 2 * (n + 1) * P].bitcast(FP4X4),
                        lhsT_scale=w4_plane[:, a, :].bitcast(U8)[:, n * P : (n + 1) * P],
                        rhs=x_codes[a][:, cols].bitcast(FP8X4),
                        rhs_scale=x_plane[a][:, cols],
                        start=(u == 0 and a == 0),
                        stop=False,
                    )

        def down(pair, first, many):
            s, mt = chunks[first]
            part = max(mt - 1, 0)
            cols = slice(first * P, (first + many) * P)
            for u in range(2):
                n = 2 * pair + u
                nc.tensor.matmul_mx(
                    out=totals[pair, part][:, u, :],
                    lhsT=wd_codes[:, n, s * P : (s + 1) * P].bitcast(FP8X4),
                    lhsT_scale=wd_plane[:, n, s * P : (s + 1) * P],
                    rhs=h_codes[:, cols].bitcast(FP8X4),
                    rhs_scale=h_plane[:, cols],
                    start=False,
                    stop=(s == J_PASSES - 1 and u == 1),
                )

        def store(pair, part, copy):
            cols = parts[part]
            result = keep.tile([P, 2, cols.stop - cols.start], F32, name="result%d_%d" % (pair, part))
            copy(result[:], totals[pair, part][:])
            rows = out[2 * pair * P : 2 * (pair + 1) * P, cols]
            nc.sync.dma_start(rows.rearrange("(u p) m -> p u m", p=P), result[:])

        spread_order = [ADDED_CHUNK + 1, ADDED_CHUNK] + list(range(ADDED_CHUNK + 2, last - 1))
        for c in range(SUM_BANKS):
            stress(c)
        spread(0)
        for c in range(SUM_BANKS, len(chunks), 2):
            for d in range(c, min(c + 2, len(chunks))):
                stress(d)
            for d in spread_order[c - SUM_BANKS : c - SUM_BANKS + 2]:
                spread(d)
        turn_wd(0, diff_bank[3])
        turn_wd(1, sum_bank[5])
        collect_wd(0)
        collect_wd(1)
        spread(last - 1)

        turn_wd(2, diff_bank[5])
        open_total(0, 0, diff_bank[4])
        open_total(1, 0, sum_bank[6])
        turn_wd(3, sum_bank[7])
        open_total(0, 1, diff_bank[6])
        collect_wd(2)
        open_total(1, 1, diff_bank[5])
        collect_wd(3)
        spread(last)

        for c in range(POOL_CHUNKS):
            weigh(c)

        def finish_first_half(pair):
            quantise_wd(pair)
            for s in range(J_PASSES):
                down(pair, 2 * s, 2)
            store(pair, 0, nc.scalar.copy)

        quantise_h(0, 4)
        finish_first_half(0)
        open_total(0, 2, sum_bank[7])
        open_total(1, 2, diff_bank[7])
        weigh(5)
        for c in (4, 5):
            quantise_h(c, 1)
            down(0, c, 1)
        store(0, 1, nc.scalar.copy)
        finish_first_half(1)
        for c in (4, 5):
            down(1, c, 1)
        store(1, 1, nc.scalar.copy)
        weigh(6)
        weigh(7)
        for c in (last - 1, last):
            quantise_h(c, 1)
            for pair in range(2):
                down(pair, c, 1)
        for pair, copy in enumerate((nc.scalar.copy, nc.vector.tensor_copy)):
            store(pair, 2, copy)
